import numpy as np, ml_dtypes
CORES = [48,51,52,55]
N = 4
import mx_ref
BF = ml_dtypes.bfloat16
def gentries(a):
    return np.ascontiguousarray(a.reshape(8, 16, -1).transpose(0, 2, 1)).reshape(8, -1)
def gtable(e):
    e = np.asarray(e); return np.ascontiguousarray(e.reshape(8, -1, 16).transpose(0, 2, 1)).reshape(128, -1).astype(np.int32)
def gcols(t, e):
    v = np.concatenate([t.reshape(8, 16, -1, 4), np.zeros((8, 16, 1, 4), BF)], axis=2)
    return np.ascontiguousarray(np.stack([v[g][:, e[g]] for g in range(8)])).reshape(128, -1)
def cut(t, i, w=512):
    return t[:, w * i:w * i + w]
def pick(q, e):
    c = np.concatenate([q[0].reshape(128, -1, 4), np.zeros((128, 1, 4), np.uint8)], axis=1); s = np.concatenate([q[1], np.ones((16, 1), np.uint8)], axis=1)
    return (np.ascontiguousarray(c[:, e].reshape(128, -1)), np.ascontiguousarray(s[:, e]))
def join(*qs):
    return (np.concatenate([q[0] for q in qs], axis=1), np.concatenate([q[1] for q in qs], axis=1))
def put(q, e, v):
    c, s = q[0].reshape(128, -1, 4).copy(), q[1].copy(); c[:, e] = v[0].reshape(128, -1, 4); s[:, e] = v[1]
    return (c.reshape(128, -1), s)
def pk(c, s):
    return (np.ascontiguousarray(c), mx_ref.live(s))
def emit(q):
    return q[0], q[1]
def packed(v, rng):
    q = [mx_ref.quantize(np.ascontiguousarray(v[r])) for r in range(N)]
    return np.stack([a for a, b in q]), np.stack([mx_ref.plane(b, rng) for a, b in q])
def values_of_codes():
    e, c = np.zeros((128, 128, 4), np.float32), np.zeros((128, 2, 4), np.uint8)
    e[np.arange(128), np.arange(128), 0] = 1
    c[:127, :, 0] = np.arange(256).reshape(2, 128).T[:127]
    return mx_ref.matmul(mx_ref.quantize(e.reshape(128, 512).astype(BF)), (c.reshape(128, 8), np.full((16, 2), 127, np.uint8))).T.reshape(-1).astype(np.float64)
CODE_VALUE, SCALE_VALUE = values_of_codes(), 2.0 ** (np.arange(256) - 127.0)
def decode(q):
    return (CODE_VALUE[q[0]].reshape(16, 8, -1, 4) * SCALE_VALUE[q[1]][:, None, :, None] + 0.0).reshape(128, -1).astype(np.float32)
def f(rng, *shape):
    return mx_ref.flush((rng.standard_normal(shape, dtype=np.float32) * np.exp2(rng.integers(-2, 3, shape[:-1] + (1,)))).astype(BF))
def wide(rng, *shape, cols=0):
    v = rng.standard_normal(shape, dtype=np.float32) * np.exp2(rng.integers(-12, 13, shape)).astype(np.float32)
    if cols: v *= np.repeat(np.exp2(rng.integers(-cols, cols + 1, shape[:-2] + (1, shape[-1] // 4))) * (rng.random(shape[:-2] + (1, shape[-1] // 4)) > 0.0625), 4, axis=-1).astype(np.float32)
    return mx_ref.flush(v.astype(BF))
C, E, B, NB, P, R = 384, 96, 96, 3, 288, 3
def big(v):
    v = v.astype(np.float32)
    v[np.abs(v) < np.float32(2.0 ** -16)] = 0
    return v.astype(BF)
def dominators(a, b, lost):
    dom = np.zeros((8, C, C), bool)
    dom[:, np.arange(C), np.arange(C)] = True
    d = np.full((8, P), -1)
    for k in range(NB):
        i = B * k + np.arange(B)
        one = np.take_along_axis(dom, a[:, i, None], axis=1)
        two = np.take_along_axis(dom, b[:, i, None], axis=1)
        both = one & (two | lost[:, i, None])
        d[:, i] = np.max(np.where(both, np.arange(C), -1), axis=2)
        dom[:, E + i] = dom[:, E + i] | both
    return d, np.sum(dom, axis=1)
def numbers_of(rng):
    return {"x": big(f(rng, N, 128, 4 * C)), "u": np.array(f(rng, N, 128, 512)), "v": np.array(f(rng, N, 128, 512))}
def lists_of(rng):
    n = E + B * (np.arange(P) // B)
    w = 2 ** rng.integers(0, 6, (N, 8, 1))
    e = np.argsort(rng.random((N, 8, E)), axis=2)
    l = []
    for k in range(2):
        p = rng.integers(0, n, (N, 8, P))
        l.append(np.where(p < E, np.take_along_axis(e, p % w, axis=2), p))
    return l
def stored(a, b):
    return {"pa": np.stack([gtable(e) for e in a]), "pb": np.stack([gtable(e) for e in b])}
def packedw(w, rng):
    c, p = packed(w, rng)
    return {"wc": c, "ws": p}
def weights(rng, q=-1):
    w = np.array(f(rng, N, 128, 2048)).reshape(N, 128, 4, 128, 4)
    if q >= 0:
        w[:, 16 * q:16 * q + 8] = 0
        w[:, :, :, 16 * q:16 * q + 8] = 0
    return packedw(w.reshape(N, 128, 2048), rng)
def setup_inputs(rng):
    return {**numbers_of(rng), **stored(*lists_of(rng)), **weights(rng)}
def setup_inputs_cuts(rng):
    d = numbers_of(rng)
    q = int(rng.integers(8))
    o, z = rng.permutation(N), rng.permutation(N) % 4
    size = np.array([2.0 ** -30, 2.0 ** -12, 1.0, 2.0 ** 29])[z]
    one = np.where(z % 2 == 0, 2.0 ** -30, 1.0).astype(np.float32).astype(BF)
    less = np.where(z == 0, -2.0 ** -30, 0.0).astype(np.float32).astype(BF)
    k = rng.integers(-1, 2, (N, 8, C, 4))
    k[:, :, :, 3] = 0
    for r in range(N):
        if o[r] == 0:
            k[r, :, :, 0] = np.abs(k[r, :, :, 0])
            k[r, :, :, 1] = -1
        if o[r] == 1:
            k[r, :, :, 0] = -1
            k[r, :, :, 1] = 0
        if o[r] == 2: k[r, :, :, 2] = np.arange(8)[:, None] % 2 * 2 - 1
    mark = np.where((z == 0)[:, None, None, None], 1.5 + 0.125 * k, k)
    x = d["x"].reshape(N, 8, 16, C, 4)
    x[:, q, :8] = (mark * size[:, None, None, None]).astype(np.float32).astype(BF)
    u = d["u"].reshape(N, 128, 128, 4)
    for t in range(R):
        u[:, :, t::16] = 0
        for g in range(8):
            u[:, 16 * q + g, 16 * g + t, t] = one
            u[:, 16 * q + g, 16 * g + t, 3] = less
    return {"x": x.reshape(N, 128, 4 * C), "u": u.reshape(N, 128, 512), "v": d["v"], **stored(*lists_of(rng)), **weights(rng, q)}
def column(j, i):
    return np.where(j < 0, i % E, E + B * j + i)
def setup_inputs_trees(rng):
    d = numbers_of(rng)
    a, b = lists_of(rng)
    o = rng.permutation(N)
    i, j = np.arange(P) % B, np.arange(P) // B
    for r in range(N):
        for g in range(8):
            k = (g + o[r]) % 8
            e = E // 2 + rng.permutation(E // 2)
            if k == 0:
                n = np.full(P, e[0])
                if o[r] % 2: n[rng.permutation(P)[255:]] = e[1]
                a[r, g], b[r, g] = n, n
            if k == 1:
                n = column(j - 1, np.concatenate([rng.permutation(B) for m in range(NB)]))
                a[r, g], b[r, g] = n, n
            if k == 2: a[r, g], b[r, g] = column(j - 1, i), column(rng.integers(-1, j, P), i)
            if k == 3: a[r, g], b[r, g] = column(j - 1, i), column(j - 1, i ^ 1)
            if k == 4:
                a[r, g] = np.where(j == 0, e[0], column(j - 1, rng.integers(0, B, P)))
                b[r, g] = np.where(j == 0, e[0], column(j - 1, rng.integers(0, B, P)))
            if k == 5: a[r, g], b[r, g] = column(j - 1, B - 1 + 0 * i), column(j - 1, 0 * i)
            if k == 6:
                n = np.where(j == 0, e[0], column(j - 1, i))
                a[r, g], b[r, g] = n, np.where(j == NB - 1, column(j - 1, i ^ 1), n)
            if k == 7 and o[r] % 2 == 0:
                n = np.where(rng.permutation(P) < P // 2 - 1, min(e[0], e[1]), max(e[0], e[1]))
                a[r, g], b[r, g] = n, n
    return {**d, **stored(a, b), **weights(rng)}
def setup_inputs_huge(rng):
    d = numbers_of(rng)
    a, b = lists_of(rng)
    e = int(rng.integers(N))
    x = 2.0 ** 28 * (1.7 + 0.15 * rng.random((N, 128, C, 4)))
    c = np.stack([rng.permutation(C) % 2 * 2.0 - 1.0 for r in range(N)])
    c[e] = 0
    c[(e + 1) % N] = -1
    c[(e + 2) % N] = -1
    x *= c[:, None, :, None]
    s = np.stack([rng.permutation(8 * R) % 2 * 2.0 - 1.0 for r in range(N)]).reshape(N, 1, 8, R, 1)
    k, m = [int(g) for g in rng.permutation(8)[:2]]
    i, j = [int(n) for n in rng.permutation(E - 1)[:2]]
    for r in ((e + 1) % N, (e + 2) % N):
        a[r, k] = i
        b[r, k] = j
        x[r, 16 * k:16 * k + 16, i] = -2.0 ** 30
        x[r, 16 * k:16 * k + 16, j] = -2.0 ** 30
        s[r, 0, k] = -1
    r = (e + 2) % N
    a[r, m] = np.where(np.arange(P) < B, i, E)
    b[r, m] = E - 1
    x[r, 16 * m:16 * m + 16, E - 1] = 2.0 ** 30
    s[r, 0, m] = 1
    h = (2.0 ** 30 * (1 - 0.1 * rng.random((N, 128, 8, R, 4))) * s).astype(np.float32).astype(BF)
    u = d["u"].reshape(N, 128, 128, 4)
    for t in range(R): u[:, :, t::16] = h[:, :, :, t]
    w = np.zeros((N, 128, 4, 128, 4), np.float32)
    p = np.arange(128)
    for n in range(4): w[:, p, n, p, n] = 1 - 2 * (p % 2)
    return {"x": x.astype(np.float32).reshape(N, 128, 4 * C).astype(BF), "u": u.reshape(N, 128, 512), "v": d["v"], **stored(a, b), **packedw(w.reshape(N, 128, 2048).astype(BF), rng)}
def setup_inputs_spread(rng):
    d = setup_inputs(rng)
    d["x"] = big(wide(rng, N, 128, 4 * C, cols=6))
    return d
def check_inputs(d):
    b = []
    for k in ("x", "u", "v"):
        a = np.abs(d[k].astype(np.float32))
        if not (np.isfinite(a).all() and ((a == 0) | (a >= 2.0 ** -30) & (a <= 2.0 ** 30)).all()): b.append("a value of " + k)
    n = E + B * (np.arange(P) // B)
    for k in ("pa", "pb"):
        for r in range(N):
            e = gentries(d[k][r])
            if ((e < 0) | (e >= n)).any(): b.append("an entry of " + k)
    if ((d["wc"] == 0x7F) | (d["wc"] == 0xFF)).any(): b.append("a code of wc that is no number")
    return b
def reference(x, u, v, pa, pb, wc, ws):
    qu = [mx_ref.quantize(u[r]) for r in range(N)]
    lay = [pk(wc[r], ws[r]) for r in range(N)]
    a = [gentries(pa[r]).astype(np.int64) for r in range(N)]
    b = [gentries(pb[r]).astype(np.int64) for r in range(N)]
    now = [x[r] for r in range(N)]
    od = np.zeros((N, 8, P), np.float32)
    for t in range(R):
        nodes, feed = [], []
        for r in range(N):
            s = mx_ref.matmul(qu[r], mx_ref.quantize(now[r]))[t::16]
            lost = s[:, E:] + np.float32(0.0) < 0
            d, n = dominators(a[r], b[r], lost)
            h = np.argsort(-n, axis=1, kind="stable")[:, :E]
            feed.append(mx_ref.quantize(gcols(now[r], h)))
            one = gcols(now[r], a[r]).astype(np.float32)
            two = gcols(now[r], np.where(lost, a[r], b[r])).astype(np.float32)
            m = (np.maximum(one, two) + gcols(now[r], d).astype(np.float32)).astype(BF)
            q = mx_ref.quantize(m)
            z = [np.maximum(mx_ref.matmul(pick(lay[r], np.arange(128 * i, 128 * i + 128)), q), np.float32(0.0)) * np.float32(0.015625) for i in range(4)]
            nodes.append((now[r][:, 4 * E:].astype(np.float32) + np.stack(z, axis=2).reshape(128, -1)).astype(BF))
            od[r] = d
        came = decode(join(*feed))
        for r in range(N):
            entry = np.maximum(now[r][:, :4 * E].astype(np.float32), cut(came, (r - 1) % N, 4 * E)).astype(BF)
            now[r] = np.ascontiguousarray(np.concatenate([entry, nodes[r]], axis=1))
    y = np.zeros((N, 128, C), np.float32)
    oc, osc = np.zeros((N, 128, 4 * C), np.uint8), np.zeros((N, 16, C), np.uint8)
    for r in range(N):
        q = mx_ref.quantize(now[r])
        y[r] = mx_ref.matmul(mx_ref.quantize(v[r]), q)
        oc[r], osc[r] = emit(q)
    return {"y": y, "od": od, "oc": oc, "osc": osc}

@@ -1,0 +1,589 @@
+import numpy as np
+from concourse.mybir import dt, AluOpType as A, AxisListType as AX, ActivationFunctionType as AF
+
+C, E, B, P, R = 384, 96, 96, 288, 3
+X0 = 16
+BIG = 1e29
+KN = 2048.0
+ON_VECTOR = (0, 0, 2)
+BY_DMA = ((0, 0), (0, 1), (1, 0), (1, 1))
+TRIES, SEED, TEMP = 14000, 1, 60.0
+F32, BF, I32, U16, QC, U8 = "float32", "bfloat16", "int32", "uint16", "float8_e4m3fn_x4", "uint8"
+
+
+def _sb(n, d):
+    return ("sbuf", [128, n], d)
+
+
+SCRATCH = {
+    "ub": _sb(512, BF), "vb": _sb(512, BF), "uq": _sb(128, QC), "us": _sb(128, U8), "vq": _sb(128, QC), "vs": _sb(128, U8),
+    "wq": _sb(512, QC), "wp": _sb(512, U8), "oq": _sb(384, QC), "op": _sb(384, U8),
+    "ab": _sb(36, I32), "ab16": _sb(36, U16), "t0": _sb(108, F32), "ll": _sb(72, F32), "la": _sb(18, U16), "lb": _sb(18, U16),
+    "tab": _sb(296, F32), "tabhi": _sb(288, F32), "tabd": _sb(1552, F32), "pix": _sb(4, I32), "pc": _sb(4, I32), "pf": _sb(8, F32),
+    "j4": _sb(144, F32), "j16": _sb(96, F32), "j2": _sb(32, F32), "mq": _sb(96, F32), "ms4": _sb(4, F32), "mr": _sb(144, F32),
+    "r4": _sb(576, BF), "m16": _sb(96, F32), "r16": _sb(96, F32), "m32": _sb(32, F32), "sb": _sb(6, F32),
+    "wt": _sb(1152, F32), "eq": _sb(576, F32), "eqb": _sb(576, F32), "tq": _sb(864, F32), "sq": _sb(864, F32),
+    "a4": _sb(72, F32), "a2": _sb(24, F32), "dab": _sb(72, F32), "aoff": _sb(72, U16), "stt": _sb(144, F32), "stm": _sb(144, F32),
+    "ct": _sb(224, BF), "w4": _sb(288, F32),
+    "cqb": _sb(1536, BF), "cq": _sb(384, QC), "cs": _sb(384, U8), "eb": _sb(2048, BF), "eqq": _sb(512, QC), "es": _sb(512, U8),
+    "fw": _sb(864, BF), "yb": _sb(288, F32), "t2": _sb(288, F32), "fq": _sb(144, QC), "fs": _sb(144, U8),
+    "pr": _sb(216, F32), "gd": _sb(72, F32), "doff": _sb(144, U16),
+    "pm": _sb(144, F32), "pms": _sb(144, F32), "cl": _sb(36, U16), "junk": _sb(1152 + 7 * 288 + 576, BF), "acc": _sb(10, F32), "acci": _sb(10, I32),
+    "un": _sb(30, I32), "n16": _sb(18, U16), "nr": _sb(288, BF), "ga": _sb(4, F32), "g32": _sb(32, F32), "g32t": _sb(32, F32), "z32": _sb(32, F32),
+    "zz": _sb(32, F32), "gt": _sb(288, BF), "ge": _sb(288, BF), "cap": _sb(288, BF), "cum": _sb(288, BF), "wl": _sb(6, F32), "wl16": _sb(6, U16),
+    "w4c": _sb(96, F32), "kk": _sb(96, F32), "km": _sb(96, F32), "ks": _sb(96, F32), "rk": _sb(6, F32), "rk16": _sb(6, U16),
+    "hr": _sb(96, F32), "hm": _sb(96, F32), "hs": _sb(96, F32), "dx": _sb(4 * P, BF),
+    "xa": _sb(1152, BF), "mx": _sb(1152, BF), "mt": _sb(1152, BF), "mq8": _sb(320, QC), "ms8": _sb(320, U8), "rr": _sb(1152, F32),
+    "dw": _sb(1152, F32), "dr": _sb(288, F32), "yo": _sb(384, F32),
+    "ps": ("psum", [128, 4096], F32),
+}
+for _t in range(R + 1):
+    SCRATCH["x%d" % _t] = _sb(X0 + 4 * C, BF)
+for _t in range(R):
+    SCRATCH["xq%d" % _t] = _sb(P + 128, QC)
+    SCRATCH["xs%d" % _t] = _sb(P + 128, U8)
+    SCRATCH["lq%d" % _t] = _sb(P, QC)
+    SCRATCH["ls%d" % _t] = _sb(P, U8)
+    SCRATCH["h%d" % _t] = _sb(24, U16)
+    SCRATCH["lh%d" % _t] = _sb(24, U16)
+SEMAPHORES = ["sv", "sa", "st", "sg", "left"] + ["d%d" % k for k in range(48)] + ["aq%d" % t for t in range(R)] + ["ah%d" % t for t in range(R)]
+
+PER = ("yb t2 fq fs pr gd doff pm pms cl junk acc acci un n16 nr ga g32 g32t z32 zz gt ge cap cum wl wl16 w4c kk km ks rk rk16 hr hm hs "
+       "dx xa mx mt mq8 ms8 rr").split()
+WIDE = {k: v[1][1] for k, v in SCRATCH.items()}
+for _k in PER:
+    SCRATCH[_k] = _sb(R * (-(-WIDE[_k] // 32) * 32), SCRATCH[_k][2])
+NOW = [0]
+
+CYC, HOP, AHEAD = 1.04, 80.0, 100.0
+BANK_Z, BANK_S, BANK_Q, BANK_D = 0, 4, 5, 6
+
+
+def V(name, lo=0, hi=None, st=1):
+    o = NOW[0] * (SCRATCH[name][1][1] // R) if name in PER else 0
+    return (name, o + lo, o + (WIDE[name] if hi is None else hi), st)
+
+
+def PS(bank, lo, hi):
+    return ("ps", 512 * bank + lo, 512 * bank + hi, 1)
+
+
+def size(v):
+    return len(range(v[1], v[2], v[3]))
+
+
+def narrow(*vs):
+    return all(SCRATCH[v[0]][2] in (BF, U16) for v in vs)
+
+
+def meet(a, b):
+    if a[0] != b[0]:
+        return False
+    if a[0] == "ps":
+        return a[1] // 512 == b[1] // 512
+    if a[1] >= b[2] or b[1] >= a[2]:
+        return False
+    return not (a[3] == b[3] and a[3] > 1 and (a[1] - b[1]) % a[3] != 0)
+
+
+def build(g, core, T, topo):
+    ops = []
+    NOW[0] = 0
+    rank = T.rank_of(core)
+    nxt = T.cores[(rank + 1) % len(T.cores)]
+
+    def ap(v):
+        if isinstance(v, (int, float)):
+            return v
+        if len(v) == 2:
+            return ap(v[0]).indirect(ap(v[1]))
+        return T[v[0]][:, v[1]:v[2]] if v[3] == 1 else T[v[0]][:, v[1]:v[2]:v[3]]
+
+    def views(xs):
+        out = []
+        for v in xs:
+            if v is None or isinstance(v, (int, float)):
+                continue
+            out.extend(v if len(v) == 2 else [v])
+        return out
+
+    def add(q, cost, rd, wr, fn, kind="c", lat=0.0, arr=None):
+        ops.append({"ways": [(q, cost, fn)], "rd": views(rd), "wr": views(wr), "kind": kind, "lat": lat, "arr": arr})
+
+    def either():
+        o = ops.pop()
+        ops[-1]["ways"].extend(o["ways"])
+
+    def vcost(out, first, per):
+        n = size(out)
+        return 50 + 1.56 * CYC * n if len(first) == 2 else 20 + CYC * max(64, n * per)
+
+    def ts(out, in0, s1, s2, op0, op1=None):
+        per = 1 if len(in0) == 2 or not narrow(out, in0) else 0.5
+        if op1 is None:
+            fn = lambda: g.vector.tensor_scalar(ap(out), ap(in0), ap(s1), None, op0)
+        else:
+            fn = lambda: g.vector.tensor_scalar(ap(out), ap(in0), ap(s1), ap(s2), op0, op1)
+        add("v", vcost(out, in0, per), [in0, s1, s2], [out], fn)
+
+    def tt(out, in0, in1, op, arr=None):
+        per = 1 if "ps" in (in0[0], in1[0]) else 2
+        add("v", vcost(out, in0, per), [in0, in1], [out], lambda: g.vector.tensor_tensor(ap(out), ap(in0), ap(in1), op), arr=arr)
+
+    def cp(out, in_):
+        add("v", vcost(out, in_, 1), [in_], [out], lambda: g.vector.tensor_copy(ap(out), ap(in_)))
+
+    def scatter(win, off, in_):
+        add("v", 50 + 3.8 * CYC * size(in_), [in_, off], [win], lambda: g.vector.tensor_copy(ap((win, off)), ap(in_)))
+
+    def scan(out, d0, d1, init=0.0, op0=A.mult, op1=A.add):
+        add("v", vcost(out, d0, 0.5 if narrow(out, d0, d1) else 1), [d0, d1, init], [out],
+            lambda: g.vector.tensor_tensor_scan(ap(out), ap(d0), ap(d1), ap(init), op0, op1))
+
+    def red(out, in_, op=A.add, neg=False):
+        add("v", vcost(in_, in_, 1), [in_], [out], lambda: g.vector.tensor_reduce(ap(out), ap(in_), AX.X, op, negate=neg))
+
+    def turn(out, in_):
+        add("v", vcost(in_, in_, 1), [in_], [out], lambda: g.vector.transpose(ap(out), ap(in_)))
+
+    def fill(out, c):
+        add("v", vcost(out, out, 0.5 if narrow(out) else 1), [], [out], lambda: g.vector.memset(ap(out), c))
+
+    def quant(q, s, in_):
+        add("v", 30 + 0.27 * size(in_), [in_], [q, s], lambda: g.vector.quantize_mx(ap(q), ap(s), ap(in_)))
+
+    def act(out, in_, f, scale=None, bias=None, acc=None):
+        def fn():
+            kw = {}
+            if scale is not None:
+                kw["scale"] = ap(scale)
+            if bias is not None:
+                kw["bias"] = ap(bias)
+            if acc is not None:
+                kw["accum_out"] = ap(acc)
+            return g.scalar.activation(ap(out), ap(in_), f, **kw)
+        n = size(out)
+        add("a", 65 + (25 if acc else 0) + CYC * n * (1.56 if len(in_) == 2 else 1), [in_, scale, bias], [out, acc], fn)
+
+    def move(out, in_, scale=None):
+        act(out, in_, AF.Copy, scale=scale)
+        if scale is None:
+            cp(out, in_)
+        else:
+            ts(out, in_, scale, None, A.mult)
+        either()
+
+    def line(out, in_, scale, bias):
+        act(out, in_, AF.Identity, scale=scale, bias=bias)
+        ts(out, in_, scale, bias, A.mult, A.add)
+        either()
+
+    def relu(out, in_, scale=None, bias=None):
+        act(out, in_, AF.Relu, scale=scale, bias=bias)
+        if bias is None:
+            ts(out, in_, 0.0, scale, A.max, A.mult)
+        else:
+            ts(out, in_, bias, 0.0, A.add, A.max)
+        either()
+
+    def mm(out, lq, ls, rq, rs, arr=None):
+        add("t", 60 + 0.9 * (size(out) + 16), [lq, ls, rq, rs], [out],
+            lambda: g.tensor.matmul_mx(ap(out), ap(lq), ap(ls), ap(rq), ap(rs), True, True), arr=arr)
+
+    def iota(out, pat, base, cm):
+        if SCRATCH[out[0]][2] == I32:
+            fn = lambda: g.iota(ap(out), pat, base, cm)
+        else:
+            fn = lambda: g.iota(ap(out), pat, base, cm, allow_small_or_imprecise_dtypes=True)
+        add("g", 140 + 2 * CYC * size(out), [], [out], fn)
+
+    def sel(out, in_, pat, op, base, cm):
+        add("g", 180 + 2 * CYC * size(out), [in_], [out], lambda: g.affine_select(ap(out), ap(in_), pat, op, 0.0, base, cm))
+
+    def dma(q, out, in_, rd, wr, lat):
+        eng = g.sync if q == "s" else g.scalar
+        add(q, 60, rd, wr, lambda: eng.dma_start(out, in_), kind="d", lat=lat)
+
+    def send(pairs, sem, rd, wr, lat):
+        def fn():
+            rid, pid = topo.addr(nxt)[0:2]
+            for dst, src in pairs:
+                g.remote_dma(dst, src, T.sem[sem], T.sem.left, pid, rid, topo.mask(core, nxt))
+        add("g", 300 * len(pairs), rd, wr, fn, kind="r", lat=lat, arr=None)
+        ops[-1]["calls"] = len(pairs)
+
+    def col(name, k):
+        return V(name, k, k + 1)
+
+    dma("s", T.ab[:, 0:18], T.pa[:], [], [V("ab", 0, 18)], 1900)
+    dma("a", T.ab[:, 18:36], T.pb[:], [], [V("ab", 18, 36)], 1900)
+    dma("s", T.x0[:, X0 + 4 * E:], T.x[:, 4 * E:], [], [V("x0", X0 + 4 * E)], 3200)
+    dma("a", T.ub[:], T.u[:], [], [V("ub")], 2600)
+    dma("s", T.x0[:, X0:X0 + 4 * E], T.x[:, 0:4 * E], [], [V("x0", X0, X0 + 4 * E)], 3600)
+    dma("s", T.wq[:].bitcast(dt.uint8), T.wc[:], [V("ab")], [V("wq")], 2500)
+    dma("s", T.wp[:], T.ws[:], [V("ab")], [V("wp")], 2700)
+    dma("s", T.vb[:], T.v[:], [V("ab")], [V("vb")], 3200)
+
+    iota(col("pix", 0), [[1, 1]], 0, 1)
+    iota(V("tab"), [[1, 296]], 1, 0)
+    iota(V("j4"), [[0, 36], [1, 4]], 0, 0)
+    iota(V("j16"), [[0, 6], [1, 16]], 0, 0)
+    iota(V("j2"), [[1, 2], [0, 16]], 0, 0)
+    fill(V("wt", 960, 1056), 0.0)
+    fill(V("tabhi", 0, 192), 0.0)
+    fill(V("fw", 480, 864), 1.0)
+    fill(V("r4"), 1.0)
+    fill(V("r4", 0, 576, 4), 0.0)
+    for t in range(R):
+        fill(V("x%d" % t, 0, X0), 0.0)
+    move(V("wt", 864, 960), V("tab", 0, 96))
+    move(V("wt", 1056, 1152), V("tab", 96, 192))
+    move(V("tabhi", 192, 288), V("tab", 192, 288))
+    for t in range(R):
+        for e in range(4):
+            sel(V("cqb", 512 * t + e, 512 * t + 512, 4), V("fw", 576, 704), [[-128, 8], [1, 4], [0, 4]], A.is_equal, -8 * t - e, 8)
+    quant(V("cq", 0, 128), V("cs", 0, 128), V("cqb", 0, 512))
+    quant(V("cq", 128, 384), V("cs", 128, 384), V("cqb", 512, 1536))
+    for b in range(4):
+        for lo in (0, 256):
+            sel(V("eb", 512 * b + lo, 512 * b + lo + 256), V("fw", 576, 832), [[1, 256]], A.is_equal, lo - b, -4)
+    quant(V("eqq"), V("es"), V("eb"))
+    iota(V("tabd"), [[1, 388], [0, 4]], -4, 0)
+    ts(col("pc", 0), col("pix", 0), 2, 3, A.logical_shift_right, A.bitwise_and)
+    ts(col("pc", 1), col("pix", 0), 3, None, A.bitwise_and)
+    ts(col("pc", 2), col("pix", 0), 4, 1, A.logical_shift_right, A.bitwise_and)
+    ts(col("pc", 3), col("pix", 0), 15, None, A.bitwise_and)
+    cp(V("pf", 0, 4), V("pc"))
+    S_, R_, H_, I0, R12, TH, I2, RM4 = [col("pf", k) for k in range(8)]
+    line(R12, R_, 1.0, 12.0)
+    line(RM4, R_, 1.0, -4.0)
+    line(TH, I0, -KN, -0.5 * KN)
+    line(I2, I0, 2.0, -223.0)
+    ts(V("ms4"), V("j4", 0, 4), S_, 4.0, A.is_equal, A.mult)
+    ts(V("mq"), V("j4", 0, 96), S_, None, A.is_equal)
+    ts(V("mr"), V("j4"), R_, 0.25, A.is_equal, A.mult)
+    ts(V("m16"), V("j16"), I0, None, A.is_equal)
+    act(V("r16"), V("j16"), AF.Sign)
+    ts(V("r16"), V("j16"), 0.0, None, A.not_equal)
+    either()
+    ts(V("j2"), V("j2"), H_, None, A.is_equal)
+    line(V("m32"), V("j2"), 1440.0, -1152.0)
+    line(V("sb"), V("tab", 0, 6), 32.0, I2)
+    fill(V("ct"), 0.0)
+    for k in range(6):
+        lo = 112 * (k // 3) + 1 + 16 * k
+        move(V("ct", lo, lo + 16), V("m16", 0, 16), float(256 ** (k % 3)))
+    move(V("w4"), V("tab", 0, 288), 4.0)
+    quant(V("uq"), V("us"), V("ub"))
+    quant(V("vq"), V("vs"), V("vb"))
+
+    cp(V("ab16"), V("ab"))
+    ts(V("t0", 0, 36), V("ab"), 96.0, 384.0, A.is_lt, A.mult)
+    ts(V("t0", 36, 72), V("ab"), 192.0, -192.0, A.is_ge, A.mult)
+    ts(V("t0", 72, 108), V("ab"), 192.0, 480.0, A.is_lt, A.mult)
+    tt(V("t0", 0, 36), V("t0", 0, 36), V("t0", 36, 72), A.add)
+    tt(V("ll", 0, 36), V("t0", 0, 36), V("ab"), A.add)
+    tt(V("ll", 36, 72), V("t0", 72, 108), V("ab"), A.add)
+    for name, o in (("la", 0), ("lb", 18)):
+        ts(V(name, 0, 6), V("ll", o + 6, o + 12), -96.0, None, A.add)
+        cp(V(name, 6, 12), V("ll", o + 48, o + 54))
+        cp(V(name, 12, 18), V("ll", o + 12, o + 18))
+    move(V("wt", 576, 672), (V("tab"), V("ab16", 0, 6)))
+    move(V("wt", 672, 768), (V("wt", 960, 1152), V("ab16", 6, 12)))
+    move(V("wt", 768, 864), (V("tabhi"), V("ab16", 12, 18)))
+    move(V("wt", 0, 288), (V("tab"), V("ab16", 18, 36)))
+    move(V("wt", 480, 576), (V("wt", 576, 1152), V("la", 0, 6)))
+    move(V("wt", 288, 480), (V("wt", 480, 1152), V("la", 6, 18)))
+    tt(V("eq", 0, 288), (V("tab"), V("ab16", 0, 18)), V("wt", 0, 288), A.is_equal)
+    tt(V("eq", 288, 384), (V("wt", 576, 1152), V("lb", 0, 6)), V("wt", 480, 576), A.is_equal)
+    tt(V("eq", 384, 576), (V("wt", 480, 1152), V("lb", 6, 18)), V("wt", 288, 480), A.is_equal)
+    move(V("eqb", 0, 288), V("eq", 0, 288), BIG)
+    move(V("eqb", 288, 384), V("eq", 288, 384), BIG)
+    move(V("eqb", 384, 576), V("eq", 384, 576), BIG)
+    for lo, hi in ((288, 864), (0, 288)):
+        for s in range(4):
+            move(V("tq", lo + s, hi, 4), V("wt", lo + s, hi, 4), col("ms4", s))
+        scan(V("sq", lo, hi), V("r4", 0, hi - lo), V("tq", lo, hi))
+
+    def SQ(lo, hi):
+        return V("sq", 4 * lo + 3, 4 * hi, 4)
+    move(V("a4", 0, 24), SQ(144, 168))
+    tt(V("a4", 24, 48), SQ(168, 192), SQ(120, 144), A.max)
+    tt(V("a2"), SQ(72, 96), SQ(96, 120), A.max)
+    tt(V("a4", 48, 72), V("a2"), SQ(192, 216), A.max)
+    ts(V("aoff"), V("a4"), R12, None, A.add)
+    tt(V("dab"), V("a4"), SQ(0, 72), A.subtract)
+    for lo, hi, lev in ((0, 24, 1), (24, 96, 0), (96, 120, 1), (120, 144, 2)):
+        relu(V("stt", lo, hi), SQ(72 + lo, 72 + hi), bias=-4.0 * B * lev)
+    tt(V("stm"), V("stt"), V("mr"), A.mult)
+
+    for t in range(R):
+        NOW[0] = t
+        x, xn = "x%d" % t, "x%d" % (t + 1)
+        xq, xs, lq, ls, hh, lh = ["%s%d" % (s, t) for s in ("xq", "xs", "lq", "ls", "h", "lh")]
+        win = V(x)
+        quant(V(xq, E, P), V(xs, E, P), V(x, X0 + 4 * E, X0 + 4 * P))
+        mm(PS(BANK_S, 0, 192), V("uq"), V("us"), V(xq, E, P), V(xs, E, P))
+        quant(V(xq, P, P + 128), V(xs, P, P + 128), V(x, X0 + 4 * 256))
+        mm(PS(BANK_Q, 0, 128), V("uq"), V("us"), V(xq, P, P + 128), V(xs, P, P + 128))
+        quant(V(xq, 0, 128), V(xs, 0, 128), V(x, X0, X0 + 512))
+        send([(T[lq][:].bitcast(dt.uint8), T[xq][:, 0:P].bitcast(dt.uint8)), (T[ls][:], T[xs][:, 0:P])], "aq%d" % t,
+             [V(xq, 0, P), V(xs, 0, P)], [V(lq), V(ls)], 3500)
+        tt(V("fw", 288, 480), PS(BANK_S, 0, 192), V("eqb", 0, 192), A.is_lt)
+        tt(V("yb", 0, 96), (V("fw", 288), V("lb", 0, 6)), V("eqb", 288, 384), A.mult)
+        tt(V("t2", 0, 96), PS(BANK_S, 96, 192), V("yb", 0, 96), A.is_lt)
+        tt(V("fw", 192, 288), (V("fw", 288), V("la", 0, 6)), V("t2", 0, 96), A.mult)
+        tt(V("fw", 480, 576), PS(BANK_Q, 32, 128), V("eqb", 192, 288), A.is_lt)
+        tt(V("yb", 96, 288), (V("fw", 192), V("lb", 6, 18)), V("eqb", 384, 576), A.mult)
+        tt(V("t2", 96, 192), PS(BANK_Q, 32, 128), V("yb", 96, 192), A.is_lt)
+        tt(V("t2", 192, 288), PS(BANK_Q, 32, 128), V("yb", 192, 288), A.is_lt)
+        tt(V("fw", 0, 192), (V("fw", 192), V("la", 6, 18)), V("t2", 96, 288), A.mult)
+        quant(V("fq"), V("fs"), V("fw", 0, 576))
+        mm(PS(BANK_S, 0, 144), V("cq", 128 * t, 128 * t + 128), V("cs", 128 * t, 128 * t + 128), V("fq"), V("fs"))
+        tt(V("pm"), PS(BANK_S, 0, 144), V("stm"), A.mult)
+        tt(V("pr", 0, 144), PS(BANK_S, 0, 144), SQ(72, 216), A.mult)
+        tt(V("gd"), PS(BANK_S, 72, 144), V("dab"), A.mult)
+        tt(V("pr", 0, 24), V("pr", 0, 24), V("pr", 24, 48), A.max)
+        tt(V("pr", 96, 120), V("pr", 96, 120), V("pr", 48, 72), A.max)
+        tt(V("pr", 144, 216), V("gd"), SQ(0, 72), A.add)
+        tt(V("pr", 120, 144), V("pr", 120, 144), V("pr", 0, 24), A.max)
+        ts(V("doff"), V("pr", 72, 216), R12, None, A.add)
+        scan(V("pms"), V("r4", 0, 144), V("pm"))
+        cp(V("cl"), V("pms", 3, 144, 4))
+        j = 0
+        for k, (lo, hi) in enumerate(((6, 18), (0, 6), (30, 36), (18, 24), (24, 30))):
+            for w in range(2):
+                n = 16 * (hi - lo)
+                act(V("junk", j, j + n), (V("ct", 112 * w, 112 * w + 112), V("cl", lo, hi)), AF.Identity, acc=col("acc", 2 * k + w))
+                j += n
+        cp(V("acci"), V("acc"))
+        ts(V("un", 0, 30, 3), V("acci"), 255, None, A.bitwise_and)
+        ts(V("un", 1, 30, 3), V("acci"), 8, 255, A.logical_shift_right, A.bitwise_and)
+        ts(V("un", 2, 30, 3), V("acci"), 16, None, A.logical_shift_right)
+        tt(V("un", 0, 12), V("un", 0, 12), V("un", 18, 30), A.add)
+        cp(V("n16"), V("un", 0, 18))
+        line(V("nr"), (V("tab"), V("n16")), KN, -KN)
+        act(V("junk", j, j + 288), V("nr"), AF.Sign, bias=TH, acc=col("ga", 0))
+        j += 288
+        relu(V("g32"), V("m32"), bias=col("ga", 0))
+        turn(V("g32t"), V("g32"))
+        ts(V("z32"), V("g32t"), 192.0, KN, A.is_ge, A.mult)
+        red(col("ga", 1), V("z32"))
+        tt(V("zz"), V("g32t"), V("z32"), A.subtract)
+        red(col("ga", 2), V("zz"), A.max, True)
+        ts(V("gt"), V("nr"), col("ga", 1), 2.0, A.is_gt, A.mult)
+        ts(V("ge"), V("nr"), col("ga", 1), 2.0, A.is_ge, A.mult)
+        scan(V("cap"), V("gt"), V("gt"), col("ga", 2), A.add, A.min)
+        scan(V("cum"), V("ge"), V("cap"), -192.0, A.add, A.min)
+        na = 6 - ON_VECTOR[t]
+        for c in range(6):
+            jk = V("junk", j, j + 288)
+            j += 288
+            if c < na:
+                act(jk, V("cum"), AF.Sign, scale=-1.0, bias=col("sb", c), acc=col("wl", c))
+            else:
+                ts(jk, V("cum"), col("sb", c), None, A.is_lt)
+                red(col("wl", c), jk)
+        ts(V("wl16", 0, na), V("wl", 0, na), 0.5, 144.0, A.mult, A.add)
+        if na < 6:
+            cp(V("wl16", na, 6), V("wl", na, 6))
+        move(V("w4c"), (V("w4"), V("wl16")))
+        tt(V("kk"), (V("nr"), V("wl16")), V("w4c"), A.subtract)
+        tt(V("km"), V("kk"), V("m16"), A.mult)
+        scan(V("ks"), V("r16"), V("km"))
+        for c in range(6):
+            act(V("junk", j, j + 96), V("kk"), AF.Sign, scale=-1.0, bias=col("ks", 16 * c + 15), acc=col("rk", c))
+            j += 96
+        ts(V("rk16"), V("rk"), -0.5, 47.5, A.mult, A.add)
+        scatter(V("hr"), V("rk16"), V("w4c"))
+        tt(V("hm"), V("hr"), V("mq"), A.mult)
+        scan(V("hs"), V("r4", 0, 96), V("hm"))
+        ts(V(hh), V("hs", 3, 96, 4), RM4, None, A.add)
+        send([(T[lh][:], T[hh][:])], "ah%d" % t, [V(hh)], [V(lh)], 2200)
+        for k in range(3):
+            lo, hi = 384 * k, 384 * k + 384
+            move(V("xa", lo, hi), (win, V("aoff", 24 * k, 24 * k + 24)))
+            tt(V("mx", lo, hi), (win, V("doff", 72 + 24 * k, 96 + 24 * k)), V("xa", lo, hi), A.max)
+            tt(V("mt", lo, hi), (win, V("doff", 24 * k, 24 * k + 24)), V("mx", lo, hi), A.add)
+        for h, (c0, n, skip) in enumerate(((0, 192, 0), (160, 128, 32))):
+            lo, hi = 4 * (c0 + skip), 4 * (c0 + n)
+            mq, ms = V("mq8", 192 * h, 192 * h + n), V("ms8", 192 * h, 192 * h + n)
+            quant(mq, ms, V("mt", 4 * c0, hi))
+            for b in range(4):
+                mm(PS(BANK_Z + b, 0, n), V("wq", 128 * b, 128 * b + 128), V("wp", 128 * b, 128 * b + 128), mq, ms)
+                relu(V("rr", lo + b, hi, 4), PS(BANK_Z + b, skip, n), scale=0.015625)
+            for l2 in range(lo, hi, 384):
+                old, new = V(x, X0 + 4 * E + l2, X0 + 4 * E + l2 + 384), V(xn, X0 + 4 * E + l2, X0 + 4 * E + l2 + 384)
+                if (t, l2 // 384) in BY_DMA:
+                    dma("s", ap(new), ap(old), [old], [new], 2200)
+                    add("g", 700, [V("rr", l2, l2 + 384), new], [new],
+                        lambda new=new, r=V("rr", l2, l2 + 384): g.dma_start(ap(new), ap(r), accum_op=A.add), kind="d", lat=2800)
+                else:
+                    tt(new, V("rr", l2, l2 + 384), old, A.add)
+        if t == R - 1:
+            move(V("dw"), (V("tabd"), V("doff", 0, 72)))
+            move(V("dr"), V("dw", 0, 1152, 4))
+            dma("s", T.od[:], T.dr[0:128:16, :], [V("dr")], [], 2000)
+            quant(V("oq", 128, 384), V("op", 128, 384), V(xn, X0 + 512))
+            dma("s", T.oc[:, 512:], T.oq[:, 128:384].bitcast(dt.uint8), [V("oq", 128, 384)], [], 2400)
+            mm(PS(BANK_S, 0, 256), V("vq"), V("vs"), V("oq", 128, 384), V("op", 128, 384))
+            move(V("yo", 128, 384), PS(BANK_S, 0, 256))
+            dma("s", T.y[:, 128:], T.yo[:, 128:], [V("yo", 128, 384)], [], 2400)
+        for b in range(4):
+            bank = BANK_D + b % 2
+            mm(PS(bank, 0, P), V("eqq", 128 * b, 128 * b + 128), V("es", 128 * b, 128 * b + 128), V(lq), V(ls), arr=("aq%d" % t, 2))
+            move(V("dx", b, 4 * P, 4), PS(bank, 0, P))
+        tt(V(xn, X0, X0 + 4 * E), (V("dx"), V(lh)), V(x, X0, X0 + 4 * E), A.max, arr=("ah%d" % t, 1))
+    xn = "x%d" % R
+    quant(V("oq", 0, 128), V("op", 0, 128), V(xn, X0, X0 + 512))
+    mm(PS(BANK_Q, 0, 128), V("vq"), V("vs"), V("oq", 0, 128), V("op", 0, 128))
+    dma("s", T.oc[:, 0:512], T.oq[:, 0:128].bitcast(dt.uint8), [V("oq", 0, 128)], [], 2000)
+    for k in range(4):
+        dma("sa"[k % 2], T.osc[4 * k:4 * k + 4, :], T.op[32 * k:32 * k + 4, :], [V("op")], [], 1900)
+    move(V("yo", 0, 128), PS(BANK_Q, 0, 128))
+    dma("s", T.y[:, 0:128], T.yo[:, 0:128], [V("yo", 0, 128)], [], 2000)
+    return ops
+
+
+def link(ops):
+    seen = {}
+    for k, o in enumerate(ops):
+        deps = set()
+        for v in o["rd"]:
+            for j, w, wr in seen.get(v[0], []):
+                if meet(v, w) and (wr or (v[0] == "ps" and len(o["ways"]) + len(ops[j]["ways"]) > 2)):
+                    deps.add(j)
+        for v in o["wr"]:
+            for j, w, wr in seen.get(v[0], []):
+                if meet(v, w):
+                    deps.add(j)
+        deps.discard(k)
+        o["deps"] = sorted(deps)
+        o["after"] = []
+        for j in deps:
+            ops[j]["after"].append(k)
+        for v in o["rd"]:
+            seen.setdefault(v[0], []).append((k, v, False))
+        for v in o["wr"]:
+            seen.setdefault(v[0], []).append((k, v, True))
+
+
+def deal(ops, prio, way, back=False):
+    n = len(ops)
+    pre, post = ("after", "deps") if back else ("deps", "after")
+    miss = [len(o[pre]) for o in ops]
+    can = [ops[k]["lat"] if back else 0.0 for k in range(n)]
+    ready = {q: [] for q in "vatgs"}
+    for k in range(n):
+        if miss[k] == 0:
+            ready[ops[k]["ways"][way[k]][0]].append(k)
+    free = {q: 0.0 for q in ready}
+    out, at, end = [], [0.0] * n, 0.0
+    for _ in range(n):
+        at0, q = min((max(free[q], min([can[k] for k in ks])), q) for q, ks in ready.items() if ks)
+        k = max([k for k in ready[q] if can[k] <= at0 + AHEAD], key=lambda k: prio[k])
+        ready[q].remove(k)
+        at[k] = max(free[q], can[k])
+        free[q] = at[k] + ops[k]["ways"][way[k]][1]
+        fin = free[q] + HOP + (0.0 if back else ops[k]["lat"])
+        end = max(end, fin)
+        out.append(k)
+        for j in ops[k][post]:
+            f = fin + ops[j]["lat"] if back else fin
+            if f > can[j]:
+                can[j] = f
+            miss[j] -= 1
+            if miss[j] == 0:
+                ready[ops[j]["ways"][way[j]][0]].append(j)
+    return end, out, at, way
+
+
+KEPT = {}
+
+
+def order(ops):
+    link(ops)
+    if "best" not in KEPT:
+        n = len(ops)
+        rng = np.random.default_rng(SEED)
+        prio = [0.0] * n
+        for k in range(n - 1, -1, -1):
+            prio[k] += ops[k]["ways"][0][1] + HOP + ops[k]["lat"]
+            for j in ops[k]["deps"]:
+                prio[j] = max(prio[j], prio[k])
+        way = [0] * n
+        free = [k for k in range(n) if len(ops[k]["ways"]) > 1]
+        best = last = deal(ops, prio, way)
+        now = best[0]
+        for it in range(TRIES):
+            p, w, r = list(prio), list(way), rng.random()
+            if r < 0.25:
+                k = free[int(rng.integers(len(free)))]
+                w[k] = 1 - w[k]
+            if r > 0.8:
+                b = deal(ops, [last[2][k] + float(e) for k, e in enumerate(rng.normal(0.0, 400.0, n))], w, True)
+                p = [b[2][k] + ops[k]["ways"][w[k]][1] for k in range(n)]
+            elif r > 0.15:
+                a, d = int(rng.integers(n)), float(rng.normal(0.0, 2500.0))
+                for k in range(a, min(n, a + int(rng.integers(1, 25)))):
+                    p[k] += d
+            got = deal(ops, p, w)
+            if got[0] <= now + TEMP * (1.0 - it / TRIES) * float(rng.exponential()):
+                now, prio, way, last = got[0], p, w, got
+            if got[0] < best[0]:
+                best = got
+        KEPT["best"] = best
+    end, seq, at, way = KEPT["best"]
+    for k, o in enumerate(ops):
+        o["at"] = at[k]
+        o["q"], o["cost"], o["fn"] = o["ways"][way[k]]
+    return seq
+
+
+def rank_program(g, core, T, topo):
+    if T.rank_of(core) is None:
+        return
+    ops = build(g, core, T, topo)
+    seq = order(ops)
+    prev = T.cores[(T.rank_of(core) - 1) % len(T.cores)]
+    nxt = T.cores[(T.rank_of(core) + 1) % len(T.cores)]
+    eng = {"v": g.vector, "a": g.scalar, "t": g.tensor, "g": g, "s": g.sync}
+    total = {"left": 0}
+    know = {q: {} for q in eng}
+    for k in seq:
+        o = ops[k]
+        q, mine = o["q"], know[o["q"]]
+        need = {}
+        for j in o["deps"]:
+            if ops[j]["kind"] == "r":
+                continue
+            s, val = ops[j]["tok"]
+            if val > need.get(s, (0, 0))[0]:
+                need[s] = (val, j)
+        for s, (val, j) in sorted(need.items(), key=lambda e: -ops[e[1][1]]["at"]):
+            if mine.get(s, 0) < val:
+                eng[q].wait_ge(T.sem[s], val)
+                for s2, v2 in ops[j]["clock"].items():
+                    mine[s2] = max(mine.get(s2, 0), v2)
+        if o["arr"] is not None:
+            s, val = o["arr"][0], o["arr"][1] * len(topo.engines(prev, core))
+            total[s] = val
+            if mine.get(s, 0) < val:
+                eng[q].wait_ge(T.sem[s], val)
+                mine[s] = val
+        ins = o["fn"]()
+        if o["kind"] == "r":
+            total["left"] += o["calls"] * len(topo.engines(core, nxt))
+            continue
+        if o["kind"] == "d":
+            s, inc = "d%d" % len([1 for e in total if e[0] == "d"]), 16
+        else:
+            s, inc = "s" + q, 1
+        total[s] = total.get(s, 0) + inc
+        ins.then_inc(T.sem[s], inc)
+        o["tok"] = (s, total[s])
+        o["clock"] = dict(mine)
+        o["clock"][s] = total[s]
+    for s, val in total.items():
+        if know["g"].get(s, 0) < val:
+            g.wait_ge(T.sem[s], val)

@@ -4,10 +4,9 @@ from concourse.mybir import dt, AluOpType as A, AxisListType as AX, ActivationFu
 C, E, B, P, R = 384, 96, 96, 288, 3
 X0 = 16
 BIG = 1e29
-KN = 2048.0
-ON_VECTOR = (0, 0, 2)
-BY_DMA = ((0, 0), (0, 1), (1, 0), (1, 1))
-TRIES, SEED, TEMP = 14000, 1, 60.0
+KN = 512.0
+BY_DMA = ((0, 0), (0, 1), (1, 0), (2, 0), (2, 1))
+TRIES, SEED, TEMP = 20000, 3, 100.0
 F32, BF, I32, U16, QC, U8 = "float32", "bfloat16", "int32", "uint16", "float8_e4m3fn_x4", "uint8"
 
 
@@ -28,9 +27,10 @@ SCRATCH = {
     "cqb": _sb(1536, BF), "cq": _sb(384, QC), "cs": _sb(384, U8), "eb": _sb(2048, BF), "eqq": _sb(512, QC), "es": _sb(512, U8),
     "fw": _sb(864, BF), "yb": _sb(288, F32), "t2": _sb(288, F32), "fq": _sb(144, QC), "fs": _sb(144, U8),
     "pr": _sb(216, F32), "gd": _sb(72, F32), "doff": _sb(144, U16),
-    "pm": _sb(144, F32), "pms": _sb(144, F32), "cl": _sb(36, U16), "junk": _sb(1152 + 7 * 288 + 576, BF), "acc": _sb(10, F32), "acci": _sb(10, I32),
-    "un": _sb(30, I32), "n16": _sb(18, U16), "nr": _sb(288, BF), "ga": _sb(4, F32), "g32": _sb(32, F32), "g32t": _sb(32, F32), "z32": _sb(32, F32),
-    "zz": _sb(32, F32), "gt": _sb(288, BF), "ge": _sb(288, BF), "cap": _sb(288, BF), "cum": _sb(288, BF), "wl": _sb(6, F32), "wl16": _sb(6, U16),
+    "pm": _sb(144, F32), "pms": _sb(144, F32), "cl": _sb(36, U16), "junk": _sb(1152 + 288, BF), "jw": _sb(6 * 290, BF), "jr": _sb(6 * 98, BF),
+    "acc": _sb(10, F32), "acci": _sb(10, I32),
+    "un": _sb(30, I32), "n16": _sb(18, U16), "nr": _sb(288, BF), "ga": _sb(4, F32), "g32": _sb(64, F32), "g32t": _sb(64, F32),
+    "gt": _sb(288, BF), "ge": _sb(288, BF), "cap": _sb(288, BF), "cum": _sb(288, BF), "wl": _sb(6, F32), "wl16": _sb(6, U16),
     "w4c": _sb(96, F32), "kk": _sb(96, F32), "km": _sb(96, F32), "ks": _sb(96, F32), "rk": _sb(6, F32), "rk16": _sb(6, U16),
     "hr": _sb(96, F32), "hm": _sb(96, F32), "hs": _sb(96, F32), "dx": _sb(4 * P, BF),
     "xa": _sb(1152, BF), "mx": _sb(1152, BF), "mt": _sb(1152, BF), "mq8": _sb(320, QC), "ms8": _sb(320, U8), "rr": _sb(1152, F32),
@@ -48,14 +48,14 @@ for _t in range(R):
     SCRATCH["lh%d" % _t] = _sb(24, U16)
 SEMAPHORES = ["sv", "sa", "st", "sg", "left"] + ["d%d" % k for k in range(48)] + ["aq%d" % t for t in range(R)] + ["ah%d" % t for t in range(R)]
 
-PER = ("yb t2 fq fs pr gd doff pm pms cl junk acc acci un n16 nr ga g32 g32t z32 zz gt ge cap cum wl wl16 w4c kk km ks rk rk16 hr hm hs "
+PER = ("yb t2 fq fs pr gd doff pm pms cl junk acc acci un n16 nr ga g32 g32t gt ge cap cum wl wl16 w4c kk km ks rk rk16 hr hm hs "
        "dx xa mx mt mq8 ms8 rr").split()
 WIDE = {k: v[1][1] for k, v in SCRATCH.items()}
 for _k in PER:
     SCRATCH[_k] = _sb(R * (-(-WIDE[_k] // 32) * 32), SCRATCH[_k][2])
 NOW = [0]
 
-CYC, HOP, AHEAD = 1.04, 80.0, 100.0
+CYC, HOP, AHEAD = 0.92, 150.0, 150.0
 BANK_Z, BANK_S, BANK_Q, BANK_D = 0, 4, 5, 6
 
 
@@ -165,6 +165,11 @@ def build(g, core, T, topo):
         n = size(out)
         add("a", 65 + (25 if acc else 0) + CYC * n * (1.56 if len(in_) == 2 else 1), [in_, scale, bias], [out, acc], fn)
 
+    def summed(last):
+        b, a = ops.pop(), ops.pop()
+        ops[-1]["ways"].append(("v", a["ways"][0][1] + HOP + b["ways"][0][1], (a["ways"][0][2], b["ways"][0][2])))
+        ops[-1]["rd"].extend(views([last]))
+
     def move(out, in_, scale=None):
         act(out, in_, AF.Copy, scale=scale)
         if scale is None:
@@ -209,7 +214,7 @@ def build(g, core, T, topo):
             rid, pid = topo.addr(nxt)[0:2]
             for dst, src in pairs:
                 g.remote_dma(dst, src, T.sem[sem], T.sem.left, pid, rid, topo.mask(core, nxt))
-        add("g", 300 * len(pairs), rd, wr, fn, kind="r", lat=lat, arr=None)
+        add("g", 300 * len(pairs) + (2500 if sem == "aq0" else 0), rd, wr, fn, kind="r", lat=lat, arr=None)
         ops[-1]["calls"] = len(pairs)
 
     def col(name, k):
@@ -222,7 +227,6 @@ def build(g, core, T, topo):
     dma("s", T.x0[:, X0:X0 + 4 * E], T.x[:, 0:4 * E], [], [V("x0", X0, X0 + 4 * E)], 3600)
     dma("s", T.wq[:].bitcast(dt.uint8), T.wc[:], [V("ab")], [V("wq")], 2500)
     dma("s", T.wp[:], T.ws[:], [V("ab")], [V("wp")], 2700)
-    dma("s", T.vb[:], T.v[:], [V("ab")], [V("vb")], 3200)
 
     iota(col("pix", 0), [[1, 1]], 0, 1)
     iota(V("tab"), [[1, 296]], 1, 0)
@@ -257,7 +261,7 @@ def build(g, core, T, topo):
     S_, R_, H_, I0, R12, TH, I2, RM4 = [col("pf", k) for k in range(8)]
     line(R12, R_, 1.0, 12.0)
     line(RM4, R_, 1.0, -4.0)
-    line(TH, I0, -KN, -0.5 * KN)
+    line(TH, I0, -1.0, -0.5)
     line(I2, I0, 2.0, -223.0)
     ts(V("ms4"), V("j4", 0, 4), S_, 4.0, A.is_equal, A.mult)
     ts(V("mq"), V("j4", 0, 96), S_, None, A.is_equal)
@@ -270,11 +274,14 @@ def build(g, core, T, topo):
     line(V("m32"), V("j2"), 1440.0, -1152.0)
     line(V("sb"), V("tab", 0, 6), 32.0, I2)
     fill(V("ct"), 0.0)
+    fill(V("jw", 288, 6 * 290, 290), -288.0)
+    fill(V("jr", 96, 6 * 98, 98), -95.0)
     for k in range(6):
         lo = 112 * (k // 3) + 1 + 16 * k
         move(V("ct", lo, lo + 16), V("m16", 0, 16), float(256 ** (k % 3)))
-    move(V("w4"), V("tab", 0, 288), 4.0)
+    move(V("w4"), V("tab", 0, 288), 1.0 / KN)
     quant(V("uq"), V("us"), V("ub"))
+    add("g", 2000, [V("cqb", 0, 512)], [V("vb")], lambda: g.dma_start(T.vb[:], T.v[:]), kind="d", lat=2500)
     quant(V("vq"), V("vs"), V("vb"))
 
     cp(V("ab16"), V("ab"))
@@ -355,6 +362,9 @@ def build(g, core, T, topo):
             for w in range(2):
                 n = 16 * (hi - lo)
                 act(V("junk", j, j + n), (V("ct", 112 * w, 112 * w + 112), V("cl", lo, hi)), AF.Identity, acc=col("acc", 2 * k + w))
+                cp(V("junk", j, j + n), (V("ct", 112 * w, 112 * w + 112), V("cl", lo, hi)))
+                red(col("acc", 2 * k + w), V("junk", j, j + n))
+                summed(None)
                 j += n
         cp(V("acci"), V("acc"))
         ts(V("un", 0, 30, 3), V("acci"), 255, None, A.bitwise_and)
@@ -362,43 +372,41 @@ def build(g, core, T, topo):
         ts(V("un", 2, 30, 3), V("acci"), 16, None, A.logical_shift_right)
         tt(V("un", 0, 12), V("un", 0, 12), V("un", 18, 30), A.add)
         cp(V("n16"), V("un", 0, 18))
-        line(V("nr"), (V("tab"), V("n16")), KN, -KN)
+        line(V("nr"), (V("tab"), V("n16")), 1.0, -1.0)
         act(V("junk", j, j + 288), V("nr"), AF.Sign, bias=TH, acc=col("ga", 0))
-        j += 288
-        relu(V("g32"), V("m32"), bias=col("ga", 0))
-        turn(V("g32t"), V("g32"))
-        ts(V("z32"), V("g32t"), 192.0, KN, A.is_ge, A.mult)
-        red(col("ga", 1), V("z32"))
-        tt(V("zz"), V("g32t"), V("z32"), A.subtract)
-        red(col("ga", 2), V("zz"), A.max, True)
+        line(col("ga", 3), col("ga", 0), -1000.0, -97000.0)
+        ts(V("g32", 0, 32), V("m32"), col("ga", 0), 192.0, A.add, A.is_ge)
+        ts(V("g32", 32, 64), V("m32"), col("ga", 0), col("ga", 3), A.add, A.min)
+        turn(V("g32t", 0, 32), V("g32", 0, 32))
+        turn(V("g32t", 32, 64), V("g32", 32, 64))
+        red(col("ga", 1), V("g32t", 0, 32))
+        red(col("ga", 2), V("g32t", 32, 64), A.max, True)
         ts(V("gt"), V("nr"), col("ga", 1), 2.0, A.is_gt, A.mult)
         ts(V("ge"), V("nr"), col("ga", 1), 2.0, A.is_ge, A.mult)
         scan(V("cap"), V("gt"), V("gt"), col("ga", 2), A.add, A.min)
         scan(V("cum"), V("ge"), V("cap"), -192.0, A.add, A.min)
-        na = 6 - ON_VECTOR[t]
         for c in range(6):
-            jk = V("junk", j, j + 288)
-            j += 288
-            if c < na:
-                act(jk, V("cum"), AF.Sign, scale=-1.0, bias=col("sb", c), acc=col("wl", c))
-            else:
-                ts(jk, V("cum"), col("sb", c), None, A.is_lt)
-                red(col("wl", c), jk)
-        ts(V("wl16", 0, na), V("wl", 0, na), 0.5, 144.0, A.mult, A.add)
-        if na < 6:
-            cp(V("wl16", na, 6), V("wl", na, 6))
+            jk = V("jw", 290 * c, 290 * c + 288)
+            act(jk, V("cum"), AF.Sign, scale=-1.0, bias=col("sb", c), acc=col("wl", c))
+            ts(jk, V("cum"), col("sb", c), 2.0, A.is_lt, A.mult)
+            red(col("wl", c), V("jw", 290 * c, 290 * c + 289))
+            summed(col("jw", 290 * c + 288))
+        ts(V("wl16"), V("wl"), 0.5, 144.0, A.mult, A.add)
         move(V("w4c"), (V("w4"), V("wl16")))
         tt(V("kk"), (V("nr"), V("wl16")), V("w4c"), A.subtract)
         tt(V("km"), V("kk"), V("m16"), A.mult)
         scan(V("ks"), V("r16"), V("km"))
         for c in range(6):
-            act(V("junk", j, j + 96), V("kk"), AF.Sign, scale=-1.0, bias=col("ks", 16 * c + 15), acc=col("rk", c))
-            j += 96
+            jk = V("jr", 98 * c, 98 * c + 96)
+            act(jk, V("kk"), AF.Sign, scale=-1.0, bias=col("ks", 16 * c + 15), acc=col("rk", c))
+            ts(jk, V("kk"), col("ks", 16 * c + 15), 2.0, A.is_lt, A.mult)
+            red(col("rk", c), V("jr", 98 * c, 98 * c + 97))
+            summed(col("jr", 98 * c + 96))
         ts(V("rk16"), V("rk"), -0.5, 47.5, A.mult, A.add)
         scatter(V("hr"), V("rk16"), V("w4c"))
         tt(V("hm"), V("hr"), V("mq"), A.mult)
         scan(V("hs"), V("r4", 0, 96), V("hm"))
-        ts(V(hh), V("hs", 3, 96, 4), RM4, None, A.add)
+        ts(V(hh), V("hs", 3, 96, 4), 4.0 * KN, RM4, A.mult, A.add)
         send([(T[lh][:], T[hh][:])], "ah%d" % t, [V(hh)], [V(lh)], 2200)
         for k in range(3):
             lo, hi = 384 * k, 384 * k + 384
@@ -416,7 +424,7 @@ def build(g, core, T, topo):
                 old, new = V(x, X0 + 4 * E + l2, X0 + 4 * E + l2 + 384), V(xn, X0 + 4 * E + l2, X0 + 4 * E + l2 + 384)
                 if (t, l2 // 384) in BY_DMA:
                     dma("s", ap(new), ap(old), [old], [new], 2200)
-                    add("g", 700, [V("rr", l2, l2 + 384), new], [new],
+                    add("g", 700, [V("rr", l2, l2 + 384), new, V("vb")], [new],
                         lambda new=new, r=V("rr", l2, l2 + 384): g.dma_start(ap(new), ap(r), accum_op=A.add), kind="d", lat=2800)
                 else:
                     tt(new, V("rr", l2, l2 + 384), old, A.add)
@@ -513,13 +521,16 @@ def order(ops):
                 prio[j] = max(prio[j], prio[k])
         way = [0] * n
         free = [k for k in range(n) if len(ops[k]["ways"]) > 1]
+        for k in free[::3]:
+            way[k] = 1 if isinstance(ops[k]["ways"][1][2], tuple) and k > 0.7 * n else 0
         best = last = deal(ops, prio, way)
         now = best[0]
         for it in range(TRIES):
             p, w, r = list(prio), list(way), rng.random()
             if r < 0.25:
-                k = free[int(rng.integers(len(free)))]
-                w[k] = 1 - w[k]
+                a, e = int(rng.integers(len(free))), int(rng.integers(2))
+                for k in free[a:a + int(rng.integers(1, 4))]:
+                    w[k] = e
             if r > 0.8:
                 b = deal(ops, [last[2][k] + float(e) for k, e in enumerate(rng.normal(0.0, 400.0, n))], w, True)
                 p = [b[2][k] + ops[k]["ways"][w[k]][1] for k in range(n)]
@@ -571,7 +582,14 @@ def rank_program(g, core, T, topo):
             if mine.get(s, 0) < val:
                 eng[q].wait_ge(T.sem[s], val)
                 mine[s] = val
-        ins = o["fn"]()
+        if isinstance(o["fn"], tuple):
+            total["sv"] = total.get("sv", 0) + 1
+            o["fn"][0]().then_inc(T.sem.sv, 1)
+            g.vector.wait_ge(T.sem.sv, total["sv"])
+            mine["sv"] = total["sv"]
+            ins = o["fn"][1]()
+        else:
+            ins = o["fn"]()
         if o["kind"] == "r":
             total["left"] += o["calls"] * len(topo.engines(core, nxt))
             continue

@@ -4,10 +4,14 @@ from concourse.mybir import dt, AluOpType as A, AxisListType as AX, ActivationFu
 C, E, B, P, R = 384, 96, 96, 288, 3
 X0 = 16
 BIG = 1e29
-KN = 512.0
+LIFT = 2.0 ** 51
 BY_DMA = ((0, 0), (0, 1), (1, 0), (2, 0), (2, 1))
-TRIES, SEED, TEMP = 20000, 3, 100.0
+M_DMA = ()
+AT_HOME = (1,)
+LIST_V, PLACE_V = (0, 0, 1), (0, 0, 1)
+TRIES, SEED, TEMP = 14000, 3, 100.0
 F32, BF, I32, U16, QC, U8 = "float32", "bfloat16", "int32", "uint16", "float8_e4m3fn_x4", "uint8"
+W0, T0, B0, A0, A1, L0, Z1, W1, T1, T2, FW = 16, 112, 208, 304, 400, 496, 784, 896, 992, 1088, 1184
 
 
 def _sb(n, d):
@@ -16,25 +20,26 @@ def _sb(n, d):
 
 SCRATCH = {
     "ub": _sb(512, BF), "vb": _sb(512, BF), "uq": _sb(128, QC), "us": _sb(128, U8), "vq": _sb(128, QC), "vs": _sb(128, U8),
+    "ut": _sb(384, QC), "ust": _sb(384, U8), "ui": _sb(24, I32), "ul": _sb(24, U16),
     "wq": _sb(512, QC), "wp": _sb(512, U8), "oq": _sb(384, QC), "op": _sb(384, U8),
-    "ab": _sb(36, I32), "ab16": _sb(36, U16), "t0": _sb(108, F32), "ll": _sb(72, F32), "la": _sb(18, U16), "lb": _sb(18, U16),
-    "tab": _sb(296, F32), "tabhi": _sb(288, F32), "tabd": _sb(1552, F32), "pix": _sb(4, I32), "pc": _sb(4, I32), "pf": _sb(8, F32),
-    "j4": _sb(144, F32), "j16": _sb(96, F32), "j2": _sb(32, F32), "mq": _sb(96, F32), "ms4": _sb(4, F32), "mr": _sb(144, F32),
-    "r4": _sb(576, BF), "m16": _sb(96, F32), "r16": _sb(96, F32), "m32": _sb(32, F32), "sb": _sb(6, F32),
-    "wt": _sb(1152, F32), "eq": _sb(576, F32), "eqb": _sb(576, F32), "tq": _sb(864, F32), "sq": _sb(864, F32),
-    "a4": _sb(72, F32), "a2": _sb(24, F32), "dab": _sb(72, F32), "aoff": _sb(72, U16), "stt": _sb(144, F32), "stm": _sb(144, F32),
-    "ct": _sb(224, BF), "w4": _sb(288, F32),
-    "cqb": _sb(1536, BF), "cq": _sb(384, QC), "cs": _sb(384, U8), "eb": _sb(2048, BF), "eqq": _sb(512, QC), "es": _sb(512, U8),
-    "fw": _sb(864, BF), "yb": _sb(288, F32), "t2": _sb(288, F32), "fq": _sb(144, QC), "fs": _sb(144, U8),
+    "ab": _sb(36, I32), "ab16": _sb(36, U16), "lt2": _sb(6, U16), "lb": _sb(18, U16), "db": _sb(18, F32), "lbf": _sb(18, F32),
+    "e16": _sb(18, F32), "el": _sb(18, U16), "zb": _sb(8, F32), "one": _sb(288, BF),
+    "tab": _sb(296, F32), "pix": _sb(5, I32), "pc": _sb(6, I32), "pf": _sb(20, F32),
+    "j4": _sb(4, F32), "j16": _sb(96, F32), "j2": _sb(32, F32), "p4": _sb(12, F32), "sel4": _sb(288, BF), "sel16": _sb(288, BF),
+    "m16": _sb(16, F32), "m32": _sb(32, F32), "sb": _sb(6, F32), "jq": _sb(96, F32),
+    "wt": _sb(1056, F32), "wt1": _sb(288, F32), "eq": _sb(288, BF), "eqs": _sb(288, BF), "eqb": _sb(288, F32), "sq": _sb(864, F32),
+    "dab": _sb(72, F32), "b16": _sb(144, F32), "aoff": _sb(72, U16), "bm": _sb(256, BF),
+    "cqb": _sb(512, BF), "cq": _sb(128, QC), "cs": _sb(128, U8), "eb": _sb(2048, BF), "eqq": _sb(512, QC), "es": _sb(512, U8),
+    "fw": _sb(FW, BF), "t2": _sb(288, BF), "fq": _sb(144, QC), "fs": _sb(144, U8),
     "pr": _sb(216, F32), "gd": _sb(72, F32), "doff": _sb(144, U16),
-    "pm": _sb(144, F32), "pms": _sb(144, F32), "cl": _sb(36, U16), "junk": _sb(1152 + 288, BF), "jw": _sb(6 * 290, BF), "jr": _sb(6 * 98, BF),
+    "junk": _sb(1152 + 288, BF), "jw": _sb(6 * 288, BF), "jx": _sb(6 * 288, BF), "jr": _sb(6 * 96, BF), "js": _sb(6 * 96, BF),
     "acc": _sb(10, F32), "acci": _sb(10, I32),
-    "un": _sb(30, I32), "n16": _sb(18, U16), "nr": _sb(288, BF), "ga": _sb(4, F32), "g32": _sb(64, F32), "g32t": _sb(64, F32),
-    "gt": _sb(288, BF), "ge": _sb(288, BF), "cap": _sb(288, BF), "cum": _sb(288, BF), "wl": _sb(6, F32), "wl16": _sb(6, U16),
-    "w4c": _sb(96, F32), "kk": _sb(96, F32), "km": _sb(96, F32), "ks": _sb(96, F32), "rk": _sb(6, F32), "rk16": _sb(6, U16),
-    "hr": _sb(96, F32), "hm": _sb(96, F32), "hs": _sb(96, F32), "dx": _sb(4 * P, BF),
+    "un": _sb(30, I32), "n16": _sb(18, U16), "nr": _sb(288, BF), "ga": _sb(4, F32), "g32": _sb(32, F32), "g32t": _sb(32, F32),
+    "gt": _sb(288, BF), "ge": _sb(288, BF), "cap": _sb(290, BF), "cum": _sb(288, BF), "wl": _sb(6, F32), "wl16": _sb(6, U16),
+    "wr": _sb(96, F32), "kk": _sb(96, F32), "ks": _sb(96, F32), "rk": _sb(6, F32), "rk16": _sb(6, U16),
+    "hr": _sb(96, F32), "hs": _sb(96, F32), "dx": _sb(4 * P, BF), "fb": _sb(512, BF),
     "xa": _sb(1152, BF), "mx": _sb(1152, BF), "mt": _sb(1152, BF), "mq8": _sb(320, QC), "ms8": _sb(320, U8), "rr": _sb(1152, F32),
-    "dw": _sb(1152, F32), "dr": _sb(288, F32), "yo": _sb(384, F32),
+    "dv": _sb(96, F32), "dw": _sb(96, F32), "dr": _sb(24, F32), "yo": _sb(384, F32),
     "ps": ("psum", [128, 4096], F32),
 }
 for _t in range(R + 1):
@@ -45,17 +50,22 @@ for _t in range(R):
     SCRATCH["lq%d" % _t] = _sb(P, QC)
     SCRATCH["ls%d" % _t] = _sb(P, U8)
     SCRATCH["h%d" % _t] = _sb(24, U16)
-    SCRATCH["lh%d" % _t] = _sb(24, U16)
-SEMAPHORES = ["sv", "sa", "st", "sg", "left"] + ["d%d" % k for k in range(48)] + ["aq%d" % t for t in range(R)] + ["ah%d" % t for t in range(R)]
+    if _t in AT_HOME:
+        SCRATCH["gq%d" % _t] = _sb(128, QC)
+        SCRATCH["gs%d" % _t] = _sb(128, U8)
+    else:
+        SCRATCH["lh%d" % _t] = _sb(24, U16)
+SEMAPHORES = ["sv", "sa", "st", "sg", "left", "od"] + ["d%d" % k for k in range(48)] + ["aq%d" % t for t in range(R)] + [
+    "ah%d" % t for t in range(R) if t not in AT_HOME]
 
-PER = ("yb t2 fq fs pr gd doff pm pms cl junk acc acci un n16 nr ga g32 g32t gt ge cap cum wl wl16 w4c kk km ks rk rk16 hr hm hs "
+PER = ("t2 fq fs pr gd doff junk jw jx jr js acc acci un n16 nr ga g32 g32t gt ge cap cum wl wl16 wr kk ks rk rk16 hr hs "
        "dx xa mx mt mq8 ms8 rr").split()
 WIDE = {k: v[1][1] for k, v in SCRATCH.items()}
 for _k in PER:
     SCRATCH[_k] = _sb(R * (-(-WIDE[_k] // 32) * 32), SCRATCH[_k][2])
 NOW = [0]
 
-CYC, HOP, AHEAD = 0.92, 150.0, 150.0
+CYC, HOP, LEAN = 0.92, 150.0, 300.0
 BANK_Z, BANK_S, BANK_Q, BANK_D = 0, 4, 5, 6
 
 
@@ -69,7 +79,7 @@ def PS(bank, lo, hi):
 
 
 def size(v):
-    return len(range(v[1], v[2], v[3]))
+    return len(range(v[1], v[2], abs(v[3])))
 
 
 def narrow(*vs):
@@ -97,6 +107,8 @@ def build(g, core, T, topo):
             return v
         if len(v) == 2:
             return ap(v[0]).indirect(ap(v[1]))
+        if v[3] == -1:
+            return T[v[0]][:, v[2] - 1:(v[1] - 1 if v[1] else None):-1]
         return T[v[0]][:, v[1]:v[2]] if v[3] == 1 else T[v[0]][:, v[1]:v[2]:v[3]]
 
     def views(xs):
@@ -133,6 +145,13 @@ def build(g, core, T, topo):
     def cp(out, in_):
         add("v", vcost(out, in_, 1), [in_], [out], lambda: g.vector.tensor_copy(ap(out), ap(in_)))
 
+    def pick(q, s, wq, ws, off):
+        add("v", vcost(q, (wq, off), 1), [wq, off], [q],
+            lambda: g.vector.tensor_copy(ap(q).bitcast(dt.uint32), ap(wq).bitcast(dt.uint32).indirect(ap(off))))
+        act(s, (ws, off), AF.Copy)
+        cp(s, (ws, off))
+        either()
+
     def scatter(win, off, in_):
         add("v", 50 + 3.8 * CYC * size(in_), [in_, off], [win], lambda: g.vector.tensor_copy(ap((win, off)), ap(in_)))
 
@@ -140,8 +159,8 @@ def build(g, core, T, topo):
         add("v", vcost(out, d0, 0.5 if narrow(out, d0, d1) else 1), [d0, d1, init], [out],
             lambda: g.vector.tensor_tensor_scan(ap(out), ap(d0), ap(d1), ap(init), op0, op1))
 
-    def red(out, in_, op=A.add, neg=False):
-        add("v", vcost(in_, in_, 1), [in_], [out], lambda: g.vector.tensor_reduce(ap(out), ap(in_), AX.X, op, negate=neg))
+    def red(out, in_, op=A.add, sizes=False):
+        add("v", vcost(in_, in_, 1), [in_], [out], lambda: g.vector.tensor_reduce(ap(out), ap(in_), AX.X, op, apply_absolute_value=sizes))
 
     def turn(out, in_):
         add("v", vcost(in_, in_, 1), [in_], [out], lambda: g.vector.transpose(ap(out), ap(in_)))
@@ -165,11 +184,6 @@ def build(g, core, T, topo):
         n = size(out)
         add("a", 65 + (25 if acc else 0) + CYC * n * (1.56 if len(in_) == 2 else 1), [in_, scale, bias], [out, acc], fn)
 
-    def summed(last):
-        b, a = ops.pop(), ops.pop()
-        ops[-1]["ways"].append(("v", a["ways"][0][1] + HOP + b["ways"][0][1], (a["ways"][0][2], b["ways"][0][2])))
-        ops[-1]["rd"].extend(views([last]))
-
     def move(out, in_, scale=None):
         act(out, in_, AF.Copy, scale=scale)
         if scale is None:
@@ -183,12 +197,9 @@ def build(g, core, T, topo):
         ts(out, in_, scale, bias, A.mult, A.add)
         either()
 
-    def relu(out, in_, scale=None, bias=None):
-        act(out, in_, AF.Relu, scale=scale, bias=bias)
-        if bias is None:
-            ts(out, in_, 0.0, scale, A.max, A.mult)
-        else:
-            ts(out, in_, bias, 0.0, A.add, A.max)
+    def relu(out, in_, scale):
+        act(out, in_, AF.Relu, scale=scale)
+        ts(out, in_, 0.0, scale, A.max, A.mult)
         either()
 
     def mm(out, lq, ls, rq, rs, arr=None):
@@ -220,206 +231,234 @@ def build(g, core, T, topo):
     def col(name, k):
         return V(name, k, k + 1)
 
+    def fw(lo, n=B):
+        return V("fw", lo, lo + n)
+
     dma("s", T.ab[:, 0:18], T.pa[:], [], [V("ab", 0, 18)], 1900)
     dma("a", T.ab[:, 18:36], T.pb[:], [], [V("ab", 18, 36)], 1900)
+    dma("a", T.ub[:], T.u[:], [], [V("ub")], 2400)
     dma("s", T.x0[:, X0 + 4 * E:], T.x[:, 4 * E:], [], [V("x0", X0 + 4 * E)], 3200)
-    dma("a", T.ub[:], T.u[:], [], [V("ub")], 2600)
     dma("s", T.x0[:, X0:X0 + 4 * E], T.x[:, 0:4 * E], [], [V("x0", X0, X0 + 4 * E)], 3600)
     dma("s", T.wq[:].bitcast(dt.uint8), T.wc[:], [V("ab")], [V("wq")], 2500)
     dma("s", T.wp[:], T.ws[:], [V("ab")], [V("wp")], 2700)
 
-    iota(col("pix", 0), [[1, 1]], 0, 1)
-    iota(V("tab"), [[1, 296]], 1, 0)
-    iota(V("j4"), [[0, 36], [1, 4]], 0, 0)
+    iota(V("pix"), [[1, 5]], 0, 1)
     iota(V("j16"), [[0, 6], [1, 16]], 0, 0)
+    iota(V("tab"), [[1, 296]], 1, 0)
+    iota(V("ui"), [[1, R], [16, 8]], 0, 0)
+    iota(V("j4"), [[1, 4]], 0, 0)
     iota(V("j2"), [[1, 2], [0, 16]], 0, 0)
-    fill(V("wt", 960, 1056), 0.0)
-    fill(V("tabhi", 0, 192), 0.0)
-    fill(V("fw", 480, 864), 1.0)
-    fill(V("r4"), 1.0)
-    fill(V("r4", 0, 576, 4), 0.0)
+    fill(V("one"), 1.0)
+    fill(fw(0, W0), 0.0)
+    fill(fw(Z1, W1 - Z1), 0.0)
+    fill(V("wt1", 0, 96), 0.0)
+    fill(V("zb", 0, 1), 0.0)
+    fill(V("zb", 1, 8), BIG)
     for t in range(R):
         fill(V("x%d" % t, 0, X0), 0.0)
-    move(V("wt", 864, 960), V("tab", 0, 96))
-    move(V("wt", 1056, 1152), V("tab", 96, 192))
-    move(V("tabhi", 192, 288), V("tab", 192, 288))
-    for t in range(R):
-        for e in range(4):
-            sel(V("cqb", 512 * t + e, 512 * t + 512, 4), V("fw", 576, 704), [[-128, 8], [1, 4], [0, 4]], A.is_equal, -8 * t - e, 8)
-    quant(V("cq", 0, 128), V("cs", 0, 128), V("cqb", 0, 512))
-    quant(V("cq", 128, 384), V("cs", 128, 384), V("cqb", 512, 1536))
+    fill(V("cap", 289, SCRATCH["cap"][1][1], SCRATCH["cap"][1][1] // R), 0.0)
+    if AT_HOME:
+        fill(V("fb", 4 * E), 0.0)
+    sel(V("bm", 0, 128), V("one", 0, 128), [[-16, 8], [0, 16]], A.is_ge, 0, 1)
+    sel(V("bm", 128, 256), V("bm", 0, 128), [[16, 8], [0, 16]], A.is_ge, 15, -1)
+    for e in range(4):
+        sel(V("cqb", e, 512, 4), V("bm", 128, 256), [[0, 8], [1, 4], [0, 4]], A.is_equal, -e, 0)
+    quant(V("cq"), V("cs"), V("cqb"))
     for b in range(4):
         for lo in (0, 256):
-            sel(V("eb", 512 * b + lo, 512 * b + lo + 256), V("fw", 576, 832), [[1, 256]], A.is_equal, lo - b, -4)
+            sel(V("eb", 512 * b + lo, 512 * b + lo + 256), V("one", 0, 256), [[1, 256]], A.is_equal, lo - b, -4)
     quant(V("eqq"), V("es"), V("eb"))
-    iota(V("tabd"), [[1, 388], [0, 4]], -4, 0)
-    ts(col("pc", 0), col("pix", 0), 2, 3, A.logical_shift_right, A.bitwise_and)
-    ts(col("pc", 1), col("pix", 0), 3, None, A.bitwise_and)
-    ts(col("pc", 2), col("pix", 0), 4, 1, A.logical_shift_right, A.bitwise_and)
-    ts(col("pc", 3), col("pix", 0), 15, None, A.bitwise_and)
-    cp(V("pf", 0, 4), V("pc"))
-    S_, R_, H_, I0, R12, TH, I2, RM4 = [col("pf", k) for k in range(8)]
+    ts(V("pc", 0, 2), V("pix", 0, 5, 4), 2, 3, A.logical_shift_right, A.bitwise_and)
+    ts(V("pc", 2, 4), V("pix", 0, 2), 15, None, A.bitwise_and)
+    ts(col("pc", 4), col("pix", 0), 3, None, A.bitwise_and)
+    ts(col("pc", 5), col("pix", 0), 4, 1, A.logical_shift_right, A.bitwise_and)
+    cp(V("pf", 0, 6), V("pc"))
+    S_, S1, I0, I1, R_, H_, R12, RM4, TH, I2, F4, F4H, F4D, F4E, F16, K0, K16, NK16 = [col("pf", k) for k in range(18)]
     line(R12, R_, 1.0, 12.0)
     line(RM4, R_, 1.0, -4.0)
-    line(TH, I0, -1.0, -0.5)
+    line(TH, I0, -1.0, -1.5)
     line(I2, I0, 2.0, -223.0)
-    ts(V("ms4"), V("j4", 0, 4), S_, 4.0, A.is_equal, A.mult)
-    ts(V("mq"), V("j4", 0, 96), S_, None, A.is_equal)
-    ts(V("mr"), V("j4"), R_, 0.25, A.is_equal, A.mult)
-    ts(V("m16"), V("j16"), I0, None, A.is_equal)
-    act(V("r16"), V("j16"), AF.Sign)
-    ts(V("r16"), V("j16"), 0.0, None, A.not_equal)
-    either()
+    ts(F4, S_, 3.0, 1.0 / LIFT, A.is_equal, A.max)
+    move(F4H, F4, 4.0)
+    move(F4D, F4, 1.0 / 16)
+    move(F4E, F4, 1.0 / 64)
+    ts(F16, I0, 15.0, 1.0 / LIFT, A.is_equal, A.max)
+    ts(K0, I0, 15.0, LIFT, A.not_equal, A.mult)
+    ts(K16, K0, 1.0, None, A.max)
+    move(NK16, K16, -1.0)
+    ts(V("m16"), V("j16", 0, 16), I0, None, A.is_equal)
+    ts(V("p4", 0, 4), V("j4"), S_, None, A.not_equal)
+    ts(V("p4", 4, 8), V("j4"), S1, LIFT, A.is_equal, A.mult)
+    tt(V("p4", 8, 12), V("p4", 0, 4), V("p4", 4, 8), A.max)
+    for s in range(4):
+        move(V("sel4", s, 288, 4), V("one", 0, 72), col("p4", 8 + s))
+    ts(V("sel16", 96, 192), V("j16"), I0, None, A.not_equal)
+    ts(V("sel16", 192, 288), V("j16"), I1, LIFT, A.is_equal, A.mult)
+    tt(V("sel16", 0, 96), V("sel16", 96, 192), V("sel16", 192, 288), A.max)
+    SEL16 = V("sel16", 0, 96)
     ts(V("j2"), V("j2"), H_, None, A.is_equal)
     line(V("m32"), V("j2"), 1440.0, -1152.0)
     line(V("sb"), V("tab", 0, 6), 32.0, I2)
-    fill(V("ct"), 0.0)
-    fill(V("jw", 288, 6 * 290, 290), -288.0)
-    fill(V("jr", 96, 6 * 98, 98), -95.0)
+    line(V("jq"), V("tab", 0, 96), 1.0 / 128, -2.0)
     for k in range(6):
-        lo = 112 * (k // 3) + 1 + 16 * k
-        move(V("ct", lo, lo + 16), V("m16", 0, 16), float(256 ** (k % 3)))
-    move(V("w4"), V("tab", 0, 288), 1.0 / KN)
+        w = (0.5 if k < 3 else -0.5) * 256.0 ** (k % 3)
+        move(fw(W0 + 16 * k, 16), V("m16"), w)
+        move(V("wt", 16 * k, 16 * k + 16), V("tab", 16 * k, 16 * k + 16), 64.0 / w)
+        move(V("wt1", B + 16 * k, B + 16 * k + 16), V("tab", B + 16 * k, B + 16 * k + 16), 64.0 / w)
+    move(fw(W1), fw(W0))
+    cp(V("ul"), V("ui"))
     quant(V("uq"), V("us"), V("ub"))
+    pick(V("ut", 0, 128), V("ust", 0, 128), V("uq"), V("us"), V("ul", 0, 8))
+    pick(V("ut", 128, 384), V("ust", 128, 384), V("uq"), V("us"), V("ul", 8, 24))
     add("g", 2000, [V("cqb", 0, 512)], [V("vb")], lambda: g.dma_start(T.vb[:], T.v[:]), kind="d", lat=2500)
     quant(V("vq"), V("vs"), V("vb"))
 
     cp(V("ab16"), V("ab"))
-    ts(V("t0", 0, 36), V("ab"), 96.0, 384.0, A.is_lt, A.mult)
-    ts(V("t0", 36, 72), V("ab"), 192.0, -192.0, A.is_ge, A.mult)
-    ts(V("t0", 72, 108), V("ab"), 192.0, 480.0, A.is_lt, A.mult)
-    tt(V("t0", 0, 36), V("t0", 0, 36), V("t0", 36, 72), A.add)
-    tt(V("ll", 0, 36), V("t0", 0, 36), V("ab"), A.add)
-    tt(V("ll", 36, 72), V("t0", 72, 108), V("ab"), A.add)
-    for name, o in (("la", 0), ("lb", 18)):
-        ts(V(name, 0, 6), V("ll", o + 6, o + 12), -96.0, None, A.add)
-        cp(V(name, 6, 12), V("ll", o + 48, o + 54))
-        cp(V(name, 12, 18), V("ll", o + 12, o + 18))
-    move(V("wt", 576, 672), (V("tab"), V("ab16", 0, 6)))
-    move(V("wt", 672, 768), (V("wt", 960, 1152), V("ab16", 6, 12)))
-    move(V("wt", 768, 864), (V("tabhi"), V("ab16", 12, 18)))
-    move(V("wt", 0, 288), (V("tab"), V("ab16", 18, 36)))
-    move(V("wt", 480, 576), (V("wt", 576, 1152), V("la", 0, 6)))
-    move(V("wt", 288, 480), (V("wt", 480, 1152), V("la", 6, 18)))
-    tt(V("eq", 0, 288), (V("tab"), V("ab16", 0, 18)), V("wt", 0, 288), A.is_equal)
-    tt(V("eq", 288, 384), (V("wt", 576, 1152), V("lb", 0, 6)), V("wt", 480, 576), A.is_equal)
-    tt(V("eq", 384, 576), (V("wt", 480, 1152), V("lb", 6, 18)), V("wt", 288, 480), A.is_equal)
-    move(V("eqb", 0, 288), V("eq", 0, 288), BIG)
-    move(V("eqb", 288, 384), V("eq", 288, 384), BIG)
-    move(V("eqb", 384, 576), V("eq", 384, 576), BIG)
-    for lo, hi in ((288, 864), (0, 288)):
-        for s in range(4):
-            move(V("tq", lo + s, hi, 4), V("wt", lo + s, hi, 4), col("ms4", s))
-        scan(V("sq", lo, hi), V("r4", 0, hi - lo), V("tq", lo, hi))
+    pa = [V("ab16", 6 * k, 6 * k + 6) for k in range(3)]
+    pb = [V("ab16", 18 + 6 * k, 24 + 6 * k) for k in range(3)]
+    tt(V("e16"), V("ab", 0, 18), V("ab", 18, 36), A.is_equal)
+    cp(V("el"), V("e16"))
+    move(V("eqb", 0, 192), (V("zb"), V("el", 0, 12)))
+    move(V("eqb", 192, 288), (V("zb"), V("el", 12, 18)))
+    ts(V("lt2"), V("ab", 12, 18), -96.0, None, A.add)
+    ts(V("db", 0, 12), V("ab", 24, 36), float(W0), F16, A.add, A.mult)
+    ts(V("db", 12, 18), V("ab", 30, 36), float(W0), F16, A.add, A.mult)
+    move(V("wt", 96, 192), (V("wt", 0, 96), pa[0]))
+    move(V("wt", 192, 288), (V("wt", 0, 192), pa[1]))
+    move(V("wt", 288, 384), (V("wt", 0, 288), pa[2]))
+    move(V("wt1", 192, 288), (V("wt1", 0, 192), pa[1]))
+    move(V("wt", 384, 480), (V("wt1"), pa[2]))
+    move(V("wt", 480, 768), (V("tab"), V("ab16", 0, 18)), 4.0)
+    move(V("wt", 768, 1056), (V("tab"), V("ab16", 18, 36)), 4.0)
+    for k, (win, lst) in enumerate(((V("wt", 0, 192), pb[1]), (V("wt", 0, 288), pb[2]), (V("wt1"), pb[2]))):
+        tt(V("eq", B * k, B * k + B), (win, lst), V("wt", 192 + B * k, 288 + B * k), A.is_equal)
+        scan(V("eqs", B * k, B * k + B), SEL16, V("eq", B * k, B * k + B), op1=A.max)
+        tt(V("lbf", 6 * k, 6 * k + 6), V("eqs", B * k + 15, B * k + B, 16), V("db", 6 * k, 6 * k + 6), A.mult)
+        cp(V("lb", 6 * k, 6 * k + 6), V("lbf", 6 * k, 6 * k + 6))
+    for k in range(3):
+        scan(V("sq", P * k, P * k + P), V("sel4"), V("wt", 192 + P * k, 480 + P * k))
 
     def SQ(lo, hi):
         return V("sq", 4 * lo + 3, 4 * hi, 4)
-    move(V("a4", 0, 24), SQ(144, 168))
-    tt(V("a4", 24, 48), SQ(168, 192), SQ(120, 144), A.max)
-    tt(V("a2"), SQ(72, 96), SQ(96, 120), A.max)
-    tt(V("a4", 48, 72), V("a2"), SQ(192, 216), A.max)
-    ts(V("aoff"), V("a4"), R12, None, A.add)
-    tt(V("dab"), V("a4"), SQ(0, 72), A.subtract)
-    for lo, hi, lev in ((0, 24, 1), (24, 96, 0), (96, 120, 1), (120, 144, 2)):
-        relu(V("stt", lo, hi), SQ(72 + lo, 72 + hi), bias=-4.0 * B * lev)
-    tt(V("stm"), V("stt"), V("mr"), A.mult)
+    ts(V("aoff"), SQ(72, 144), F4, R12, A.mult, A.add)
+    tt(V("dab"), SQ(72, 144), SQ(144, 216), A.subtract)
+    move(V("b16", 0, 72), SQ(144, 216), 16.0)
 
     for t in range(R):
         NOW[0] = t
         x, xn = "x%d" % t, "x%d" % (t + 1)
         xq, xs, lq, ls, hh, lh = ["%s%d" % (s, t) for s in ("xq", "xs", "lq", "ls", "h", "lh")]
         win = V(x)
+        home = t in AT_HOME
+        ut, ust = V("ut", 128 * t, 128 * t + 128), V("ust", 128 * t, 128 * t + 128)
         quant(V(xq, E, P), V(xs, E, P), V(x, X0 + 4 * E, X0 + 4 * P))
-        mm(PS(BANK_S, 0, 192), V("uq"), V("us"), V(xq, E, P), V(xs, E, P))
+        mm(PS(BANK_S, 0, 192), ut, ust, V(xq, E, P), V(xs, E, P))
         quant(V(xq, P, P + 128), V(xs, P, P + 128), V(x, X0 + 4 * 256))
-        mm(PS(BANK_Q, 0, 128), V("uq"), V("us"), V(xq, P, P + 128), V(xs, P, P + 128))
-        quant(V(xq, 0, 128), V(xs, 0, 128), V(x, X0, X0 + 512))
-        send([(T[lq][:].bitcast(dt.uint8), T[xq][:, 0:P].bitcast(dt.uint8)), (T[ls][:], T[xs][:, 0:P])], "aq%d" % t,
-             [V(xq, 0, P), V(xs, 0, P)], [V(lq), V(ls)], 3500)
-        tt(V("fw", 288, 480), PS(BANK_S, 0, 192), V("eqb", 0, 192), A.is_lt)
-        tt(V("yb", 0, 96), (V("fw", 288), V("lb", 0, 6)), V("eqb", 288, 384), A.mult)
-        tt(V("t2", 0, 96), PS(BANK_S, 96, 192), V("yb", 0, 96), A.is_lt)
-        tt(V("fw", 192, 288), (V("fw", 288), V("la", 0, 6)), V("t2", 0, 96), A.mult)
-        tt(V("fw", 480, 576), PS(BANK_Q, 32, 128), V("eqb", 192, 288), A.is_lt)
-        tt(V("yb", 96, 288), (V("fw", 192), V("lb", 6, 18)), V("eqb", 384, 576), A.mult)
-        tt(V("t2", 96, 192), PS(BANK_Q, 32, 128), V("yb", 96, 192), A.is_lt)
-        tt(V("t2", 192, 288), PS(BANK_Q, 32, 128), V("yb", 192, 288), A.is_lt)
-        tt(V("fw", 0, 192), (V("fw", 192), V("la", 6, 18)), V("t2", 96, 288), A.mult)
-        quant(V("fq"), V("fs"), V("fw", 0, 576))
-        mm(PS(BANK_S, 0, 144), V("cq", 128 * t, 128 * t + 128), V("cs", 128 * t, 128 * t + 128), V("fq"), V("fs"))
-        tt(V("pm"), PS(BANK_S, 0, 144), V("stm"), A.mult)
-        tt(V("pr", 0, 144), PS(BANK_S, 0, 144), SQ(72, 216), A.mult)
-        tt(V("gd"), PS(BANK_S, 72, 144), V("dab"), A.mult)
-        tt(V("pr", 0, 24), V("pr", 0, 24), V("pr", 24, 48), A.max)
-        tt(V("pr", 96, 120), V("pr", 96, 120), V("pr", 48, 72), A.max)
-        tt(V("pr", 144, 216), V("gd"), SQ(0, 72), A.add)
-        tt(V("pr", 120, 144), V("pr", 120, 144), V("pr", 0, 24), A.max)
-        ts(V("doff"), V("pr", 72, 216), R12, None, A.add)
-        scan(V("pms"), V("r4", 0, 144), V("pm"))
-        cp(V("cl"), V("pms", 3, 144, 4))
+        mm(PS(BANK_Q, 0, 128), ut, ust, V(xq, P, P + 128), V(xs, P, P + 128))
+        if not home:
+            quant(V(xq, 0, 128), V(xs, 0, 128), V(x, X0, X0 + 512))
+            send([(T[lq][:].bitcast(dt.uint8), T[xq][:, 0:P].bitcast(dt.uint8)), (T[ls][:], T[xs][:, 0:P])], "aq%d" % t,
+                 [V(xq, 0, P), V(xs, 0, P)], [V(lq), V(ls)], 3500)
+        tt(fw(L0, 192), PS(BANK_S, 0, 192), V("eqb", 0, 192), A.is_lt)
+        tt(fw(T0), (fw(W0), pa[0]), fw(L0), A.mult)
+        tt(V("t2", 0, 96), (fw(0, B0), V("lb", 0, 6)), fw(L0 + B), A.not_equal)
+        tt(fw(B0), (fw(W0, 192), pa[1]), V("t2", 0, 96), A.mult)
+        tt(fw(T1), (fw(W1 - B, 192), pa[1]), fw(L0 + B), A.mult)
+        tt(fw(L0 + 192), PS(BANK_Q, 32, 128), V("eqb", 192, 288), A.is_lt)
+        tt(V("t2", 96, 192), (fw(0, A0), V("lb", 6, 12)), fw(L0 + 192), A.not_equal)
+        tt(V("t2", 192, 288), (fw(Z1, T2 - Z1), V("lb", 12, 18)), fw(L0 + 192), A.not_equal)
+        tt(fw(A0), (fw(W0, P), pa[2]), V("t2", 96, 192), A.mult)
+        tt(fw(A1), (fw(W1 - B, P), pa[2]), V("t2", 192, 288), A.mult)
+        tt(fw(T2), (fw(W1 - B, 192), V("lt2")), fw(L0 + 192), A.mult)
         j = 0
-        for k, (lo, hi) in enumerate(((6, 18), (0, 6), (30, 36), (18, 24), (24, 30))):
+        for k, run in enumerate((fw(A0), fw(A1), fw(T2), fw(T0, 192), fw(T1))):
             for w in range(2):
-                n = 16 * (hi - lo)
-                act(V("junk", j, j + n), (V("ct", 112 * w, 112 * w + 112), V("cl", lo, hi)), AF.Identity, acc=col("acc", 2 * k + w))
-                cp(V("junk", j, j + n), (V("ct", 112 * w, 112 * w + 112), V("cl", lo, hi)))
-                red(col("acc", 2 * k + w), V("junk", j, j + n))
-                summed(None)
+                n = size(run)
+                act(V("junk", j, j + n), run, AF.Abs if w else AF.Identity, acc=col("acc", 5 * w + k))
+                red(col("acc", 5 * w + k), run, sizes=bool(w))
+                either()
                 j += n
-        cp(V("acci"), V("acc"))
+        tt(V("acci", 0, 10, 2), V("acc", 5, 10), V("acc", 0, 5), A.add)
+        tt(V("acci", 1, 10, 2), V("acc", 5, 10), V("acc", 0, 5), A.subtract)
         ts(V("un", 0, 30, 3), V("acci"), 255, None, A.bitwise_and)
         ts(V("un", 1, 30, 3), V("acci"), 8, 255, A.logical_shift_right, A.bitwise_and)
         ts(V("un", 2, 30, 3), V("acci"), 16, None, A.logical_shift_right)
         tt(V("un", 0, 12), V("un", 0, 12), V("un", 18, 30), A.add)
         cp(V("n16"), V("un", 0, 18))
+        quant(V("fq"), V("fs"), fw(B0, 576))
+        mm(PS(BANK_S, 0, 144), V("cq"), V("cs"), V("fq"), V("fs"))
+        tt(V("pr", 0, 144), PS(BANK_S, 0, 144), SQ(0, 144), A.mult)
+        tt(V("gd"), PS(BANK_S, 72, 144), V("dab"), A.mult)
+        tt(V("pr", 24, 48), V("pr", 24, 48), V("pr", 48, 72), A.max)
+        tt(V("pr", 144, 216), V("gd"), V("b16", 0, 72), A.add)
+        tt(V("pr", 96, 144), V("pr", 96, 144), V("pr", 0, 48), A.max)
+        ts(V("doff"), V("pr", 72, 216), F4D, R12, A.mult, A.add)
+        act(V("junk", j, j + P), (V("tab"), V("n16")), AF.Sign, bias=TH, acc=col("ga", 0))
         line(V("nr"), (V("tab"), V("n16")), 1.0, -1.0)
-        act(V("junk", j, j + 288), V("nr"), AF.Sign, bias=TH, acc=col("ga", 0))
-        line(col("ga", 3), col("ga", 0), -1000.0, -97000.0)
-        ts(V("g32", 0, 32), V("m32"), col("ga", 0), 192.0, A.add, A.is_ge)
-        ts(V("g32", 32, 64), V("m32"), col("ga", 0), col("ga", 3), A.add, A.min)
-        turn(V("g32t", 0, 32), V("g32", 0, 32))
-        turn(V("g32t", 32, 64), V("g32", 32, 64))
-        red(col("ga", 1), V("g32t", 0, 32))
-        red(col("ga", 2), V("g32t", 32, 64), A.max, True)
-        ts(V("gt"), V("nr"), col("ga", 1), 2.0, A.is_gt, A.mult)
+        ts(V("g32"), V("m32"), col("ga", 0), 192.0, A.add, A.is_ge)
+        turn(V("g32t"), V("g32"))
+        red(col("ga", 1), V("g32t"))
+        ts(V("gt"), V("nr"), col("ga", 1), -2.0, A.is_gt, A.mult)
         ts(V("ge"), V("nr"), col("ga", 1), 2.0, A.is_ge, A.mult)
-        scan(V("cap"), V("gt"), V("gt"), col("ga", 2), A.add, A.min)
-        scan(V("cum"), V("ge"), V("cap"), -192.0, A.add, A.min)
+        scan(V("cap", 1, 289, -1), V("gt", 0, P, -1), V("gt", 0, P, -1), 0.0, A.add, A.min)
+        scan(V("cum"), V("ge"), V("cap", 2, 290), -192.0, A.add, A.min)
+        na = 6 - LIST_V[t]
         for c in range(6):
-            jk = V("jw", 290 * c, 290 * c + 288)
-            act(jk, V("cum"), AF.Sign, scale=-1.0, bias=col("sb", c), acc=col("wl", c))
-            ts(jk, V("cum"), col("sb", c), 2.0, A.is_lt, A.mult)
-            red(col("wl", c), V("jw", 290 * c, 290 * c + 289))
-            summed(col("jw", 290 * c + 288))
-        ts(V("wl16"), V("wl"), 0.5, 144.0, A.mult, A.add)
-        move(V("w4c"), (V("w4"), V("wl16")))
-        tt(V("kk"), (V("nr"), V("wl16")), V("w4c"), A.subtract)
-        tt(V("km"), V("kk"), V("m16"), A.mult)
-        scan(V("ks"), V("r16"), V("km"))
+            jk = V("jw", P * c, P * c + P)
+            if c < na:
+                act(jk, V("cum"), AF.Sign, scale=-1.0, bias=col("sb", c), acc=col("wl", c))
+            else:
+                ts(jk, V("cum"), col("sb", c), -0.5, A.is_lt, A.add)
+        for c in range(na, 6):
+            scan(V("jx", P * c, P * c + P), V("one"), V("jw", P * c, P * c + P))
+        if na < 6:
+            ts(V("wl16", na, 6), V("jx", P * na + P - 1, 6 * P, P), 144.0, None, A.add)
+        if na:
+            ts(V("wl16", 0, na), V("wl", 0, na), 0.5, 144.0, A.mult, A.add)
+        tt(V("kk"), (V("nr"), V("wl16")), V("jq"), A.subtract)
+        move(V("wr"), (V("tab"), V("wl16")))
+        scan(V("ks"), SEL16, V("kk"), op1=A.max)
+        na = 6 - PLACE_V[t]
         for c in range(6):
-            jk = V("jr", 98 * c, 98 * c + 96)
-            act(jk, V("kk"), AF.Sign, scale=-1.0, bias=col("ks", 16 * c + 15), acc=col("rk", c))
-            ts(jk, V("kk"), col("ks", 16 * c + 15), 2.0, A.is_lt, A.mult)
-            red(col("rk", c), V("jr", 98 * c, 98 * c + 97))
-            summed(col("jr", 98 * c + 96))
-        ts(V("rk16"), V("rk"), -0.5, 47.5, A.mult, A.add)
-        scatter(V("hr"), V("rk16"), V("w4c"))
-        tt(V("hm"), V("hr"), V("mq"), A.mult)
-        scan(V("hs"), V("r4", 0, 96), V("hm"))
-        ts(V(hh), V("hs", 3, 96, 4), 4.0 * KN, RM4, A.mult, A.add)
-        send([(T[lh][:], T[hh][:])], "ah%d" % t, [V(hh)], [V(lh)], 2200)
+            jk = V("jr", B * c, B * c + B)
+            if c < na:
+                act(jk, V("kk"), AF.Sign, scale=NK16, bias=col("ks", 16 * c + 15), acc=col("rk", c))
+            else:
+                ts(jk, V("kk"), K16, col("ks", 16 * c + 15), A.mult, A.is_gt)
+        for c in range(na, 6):
+            scan(V("js", B * c, B * c + B), V("one", 0, B), V("jr", B * c, B * c + B))
+        if na < 6:
+            cp(V("rk16", na, 6), V("js", B * na + B - 1, 6 * B, B))
+        if na:
+            ts(V("rk16", 0, na), V("rk", 0, na), -0.5, 47.5, A.mult, A.add)
+        scatter(V("hr"), V("rk16"), V("wr"))
+        scan(V("hs"), V("sel4", 0, 96), V("hr"), op1=A.max)
+        ts(V(hh), V("hs", 3, 96, 4), F4H, R12 if home else RM4, A.mult, A.add)
+        if home:
+            gq, gs = "gq%d" % t, "gs%d" % t
+            move(V("fb", 0, 4 * E), (win, V(hh)))
+            quant(V(gq), V(gs), V("fb"))
+            send([(T[lq][:, 0:128].bitcast(dt.uint8), T[gq][:].bitcast(dt.uint8)), (T[ls][:, 0:128], T[gs][:])], "aq%d" % t,
+                 [V(gq), V(gs)], [V(lq), V(ls)], 2500)
+        else:
+            send([(T[lh][:], T[hh][:])], "ah%d" % t, [V(hh)], [V(lh)], 2200)
         for k in range(3):
             lo, hi = 384 * k, 384 * k + 384
             move(V("xa", lo, hi), (win, V("aoff", 24 * k, 24 * k + 24)))
             tt(V("mx", lo, hi), (win, V("doff", 72 + 24 * k, 96 + 24 * k)), V("xa", lo, hi), A.max)
-            tt(V("mt", lo, hi), (win, V("doff", 24 * k, 24 * k + 24)), V("mx", lo, hi), A.add)
+            if (t, k) in M_DMA:
+                move(V("mt", lo, hi), (win, V("doff", 24 * k, 24 * k + 24)))
+                add("g", 700, [V("mx", lo, hi), V("mt", lo, hi), V("vb")], [V("mt", lo, hi)],
+                    lambda o=V("mt", lo, hi), r=V("mx", lo, hi): g.dma_start(ap(o), ap(r), accum_op=A.add), kind="d", lat=2800)
+            else:
+                tt(V("mt", lo, hi), (win, V("doff", 24 * k, 24 * k + 24)), V("mx", lo, hi), A.add)
         for h, (c0, n, skip) in enumerate(((0, 192, 0), (160, 128, 32))):
             lo, hi = 4 * (c0 + skip), 4 * (c0 + n)
             mq, ms = V("mq8", 192 * h, 192 * h + n), V("ms8", 192 * h, 192 * h + n)
             quant(mq, ms, V("mt", 4 * c0, hi))
             for b in range(4):
                 mm(PS(BANK_Z + b, 0, n), V("wq", 128 * b, 128 * b + 128), V("wp", 128 * b, 128 * b + 128), mq, ms)
-                relu(V("rr", lo + b, hi, 4), PS(BANK_Z + b, skip, n), scale=0.015625)
+                relu(V("rr", lo + b, hi, 4), PS(BANK_Z + b, skip, n), 0.015625)
             for l2 in range(lo, hi, 384):
                 old, new = V(x, X0 + 4 * E + l2, X0 + 4 * E + l2 + 384), V(xn, X0 + 4 * E + l2, X0 + 4 * E + l2 + 384)
                 if (t, l2 // 384) in BY_DMA:
@@ -429,19 +468,28 @@ def build(g, core, T, topo):
                 else:
                     tt(new, V("rr", l2, l2 + 384), old, A.add)
         if t == R - 1:
-            move(V("dw"), (V("tabd"), V("doff", 0, 72)))
-            move(V("dr"), V("dw", 0, 1152, 4))
-            dma("s", T.od[:], T.dr[0:128:16, :], [V("dr")], [], 2000)
+            line(V("dv"), V("pr", 72, 168), F4E, -1.0)
+            turn(V("dw"), V("dv"))
+            move(V("dr"), V("dw", 0, 96, 4))
+            for gr in range(8):
+                for k, n in enumerate((32, 32, 8)):
+                    c0 = 8 * k + 4 * (gr % 2)
+                    dma("s", T.od[gr, 128 * k:128 * k + 4 * n], T.dr[32 * (gr // 2):32 * (gr // 2) + n, c0:c0 + 4], [V("dr")], [], 2000)
+                    ops[-1]["sem"] = "od"
             quant(V("oq", 128, 384), V("op", 128, 384), V(xn, X0 + 512))
             dma("s", T.oc[:, 512:], T.oq[:, 128:384].bitcast(dt.uint8), [V("oq", 128, 384)], [], 2400)
             mm(PS(BANK_S, 0, 256), V("vq"), V("vs"), V("oq", 128, 384), V("op", 128, 384))
             move(V("yo", 128, 384), PS(BANK_S, 0, 256))
             dma("s", T.y[:, 128:], T.yo[:, 128:], [V("yo", 128, 384)], [], 2400)
         for b in range(4):
-            bank = BANK_D + b % 2
-            mm(PS(bank, 0, P), V("eqq", 128 * b, 128 * b + 128), V("es", 128 * b, 128 * b + 128), V(lq), V(ls), arr=("aq%d" % t, 2))
-            move(V("dx", b, 4 * P, 4), PS(bank, 0, P))
-        tt(V(xn, X0, X0 + 4 * E), (V("dx"), V(lh)), V(x, X0, X0 + 4 * E), A.max, arr=("ah%d" % t, 1))
+            bank, n = BANK_D + b % 2, 128 if home else P
+            mm(PS(bank, 0, n), V("eqq", 128 * b, 128 * b + 128), V("es", 128 * b, 128 * b + 128), V(lq, 0, n), V(ls, 0, n), arr=("aq%d" % t, 2))
+            if home:
+                tt(V(xn, X0 + b, X0 + 4 * E, 4), PS(bank, 0, E), V(x, X0 + b, X0 + 4 * E, 4), A.max)
+            else:
+                move(V("dx", b, 4 * P, 4), PS(bank, 0, P))
+        if not home:
+            tt(V(xn, X0, X0 + 4 * E), (V("dx"), V(lh)), V(x, X0, X0 + 4 * E), A.max, arr=("ah%d" % t, 1))
     xn = "x%d" % R
     quant(V("oq", 0, 128), V("op", 0, 128), V(xn, X0, X0 + 512))
     mm(PS(BANK_Q, 0, 128), V("vq"), V("vs"), V("oq", 0, 128), V("op", 0, 128))
@@ -476,34 +524,33 @@ def link(ops):
             seen.setdefault(v[0], []).append((k, v, True))
 
 
-def deal(ops, prio, way, back=False):
+def deal(ops, key, way, back, lean):
+    pre = "after" if back else "deps"
     n = len(ops)
-    pre, post = ("after", "deps") if back else ("deps", "after")
-    miss = [len(o[pre]) for o in ops]
-    can = [ops[k]["lat"] if back else 0.0 for k in range(n)]
-    ready = {q: [] for q in "vatgs"}
-    for k in range(n):
-        if miss[k] == 0:
-            ready[ops[k]["ways"][way[k]][0]].append(k)
-    free = {q: 0.0 for q in ready}
-    out, at, end = [], [0.0] * n, 0.0
-    for _ in range(n):
-        at0, q = min((max(free[q], min([can[k] for k in ks])), q) for q, ks in ready.items() if ks)
-        k = max([k for k in ready[q] if can[k] <= at0 + AHEAD], key=lambda k: prio[k])
-        ready[q].remove(k)
-        at[k] = max(free[q], can[k])
-        free[q] = at[k] + ops[k]["ways"][way[k]][1]
-        fin = free[q] + HOP + (0.0 if back else ops[k]["lat"])
-        end = max(end, fin)
-        out.append(k)
-        for j in ops[k][post]:
-            f = fin + ops[j]["lat"] if back else fin
-            if f > can[j]:
-                can[j] = f
-            miss[j] -= 1
-            if miss[j] == 0:
-                ready[ops[j]["ways"][way[j]][0]].append(j)
-    return end, out, at, way
+    at, fin, w = [0.0] * n, [0.0] * n, list(way)
+    st, en = {q: [] for q in "vatgs"}, {q: [] for q in "vatgs"}
+    for k in sorted(range(n), key=lambda k: (key[k], k)):
+        o = ops[k]
+        can = max([fin[j] for j in o[pre]] + [0.0]) + (o["lat"] if back else 0.0)
+        best = None
+        for i in ((w[k],) if back else range(len(o["ways"]))):
+            q, c = o["ways"][i][0:2]
+            s, e = st[q], en[q]
+            m, t = len(s), can
+            while m and e[m - 1] > can:
+                m -= 1
+            while m < len(s) and s[m] < t + c:
+                t = e[m]
+                m += 1
+            end = t + c + (lean[k] if q == "v" else 0.0)
+            if best is None or end < best[0]:
+                best = (end, i, q, t, c, m)
+        end, w[k], q, t, c, m = best
+        st[q].insert(m, t)
+        en[q].insert(m, t + c)
+        at[k] = t
+        fin[k] = t + c + HOP + (0.0 if back else o["lat"])
+    return max(fin), at, w
 
 
 KEPT = {}
@@ -511,44 +558,41 @@ KEPT = {}
 
 def order(ops):
     link(ops)
+    n = len(ops)
     if "best" not in KEPT:
-        n = len(ops)
         rng = np.random.default_rng(SEED)
-        prio = [0.0] * n
+        key = [0.0] * n
         for k in range(n - 1, -1, -1):
-            prio[k] += ops[k]["ways"][0][1] + HOP + ops[k]["lat"]
+            key[k] -= min([w[1] for w in ops[k]["ways"]]) + HOP + ops[k]["lat"]
             for j in ops[k]["deps"]:
-                prio[j] = max(prio[j], prio[k])
-        way = [0] * n
-        free = [k for k in range(n) if len(ops[k]["ways"]) > 1]
-        for k in free[::3]:
-            way[k] = 1 if isinstance(ops[k]["ways"][1][2], tuple) and k > 0.7 * n else 0
-        best = last = deal(ops, prio, way)
-        now = best[0]
+                key[j] = min(key[j], key[k])
+        lean = [LEAN] * n
+        best = now = deal(ops, key, [0] * n, False, lean)
         for it in range(TRIES):
-            p, w, r = list(prio), list(way), rng.random()
-            if r < 0.25:
-                a, e = int(rng.integers(len(free))), int(rng.integers(2))
-                for k in free[a:a + int(rng.integers(1, 4))]:
-                    w[k] = e
-            if r > 0.8:
-                b = deal(ops, [last[2][k] + float(e) for k, e in enumerate(rng.normal(0.0, 400.0, n))], w, True)
-                p = [b[2][k] + ops[k]["ways"][w[k]][1] for k in range(n)]
-            elif r > 0.15:
-                a, d = int(rng.integers(n)), float(rng.normal(0.0, 2500.0))
-                for k in range(a, min(n, a + int(rng.integers(1, 25)))):
-                    p[k] += d
-            got = deal(ops, p, w)
-            if got[0] <= now + TEMP * (1.0 - it / TRIES) * float(rng.exponential()):
-                now, prio, way, last = got[0], p, w, got
+            r, a, le = rng.random(), int(rng.integers(n)), list(lean)
+            shake = rng.normal(0.0, (30.0, 150.0, 500.0)[it % 3], n)
+            if r < 0.3:
+                d = float(rng.normal(0.0, 600.0))
+                for k in range(a, min(n, a + int(rng.integers(1, 30)))):
+                    le[k] += d
+            if r > 0.6:
+                shake[a:a + int(rng.integers(1, 25))] += float(rng.normal(0.0, 2000.0))
+            key = [float(shake[k]) - now[1][k] - ops[k]["ways"][now[2][k]][1] - ops[k]["lat"] for k in range(n)]
+            for k in range(n - 1, -1, -1):
+                for j in ops[k]["deps"]:
+                    key[j] = max(key[j], key[k] + 0.01)
+            b = deal(ops, key, now[2], True, le)
+            got = deal(ops, [-b[1][k] - ops[k]["ways"][b[2][k]][1] for k in range(n)], b[2], False, le)
+            if got[0] <= now[0] + TEMP * (1.0 - it / TRIES) * float(rng.exponential()):
+                now, lean = got, le
             if got[0] < best[0]:
                 best = got
         KEPT["best"] = best
-    end, seq, at, way = KEPT["best"]
+    end, at, way = KEPT["best"]
     for k, o in enumerate(ops):
         o["at"] = at[k]
         o["q"], o["cost"], o["fn"] = o["ways"][way[k]]
-    return seq
+    return sorted(range(n), key=lambda k: (at[k], k))
 
 
 def rank_program(g, core, T, topo):
@@ -582,19 +626,12 @@ def rank_program(g, core, T, topo):
             if mine.get(s, 0) < val:
                 eng[q].wait_ge(T.sem[s], val)
                 mine[s] = val
-        if isinstance(o["fn"], tuple):
-            total["sv"] = total.get("sv", 0) + 1
-            o["fn"][0]().then_inc(T.sem.sv, 1)
-            g.vector.wait_ge(T.sem.sv, total["sv"])
-            mine["sv"] = total["sv"]
-            ins = o["fn"][1]()
-        else:
-            ins = o["fn"]()
+        ins = o["fn"]()
         if o["kind"] == "r":
             total["left"] += o["calls"] * len(topo.engines(core, nxt))
             continue
         if o["kind"] == "d":
-            s, inc = "d%d" % len([1 for e in total if e[0] == "d"]), 16
+            s, inc = o.get("sem", "d%d" % len([1 for e in total if e[0] == "d"])), 16
         else:
             s, inc = "s" + q, 1
         total[s] = total.get(s, 0) + inc

@@ -1,15 +1,26 @@
+import math
 import numpy as np
 from concourse.mybir import dt, AluOpType as A, AxisListType as AX, ActivationFunctionType as AF
 
 C, E, B, P, R = 384, 96, 96, 288, 3
-X0 = 16
+X0 = 32
 BIG = 1e29
 LIFT = 2.0 ** 51
 BY_DMA = ((0, 0), (0, 1), (1, 0), (2, 0), (2, 1))
+BY_ROW = ((0, 2), (1, 2), (2, 2))
+HALVES = ()
 M_DMA = ()
-AT_HOME = (1,)
-LIST_V, PLACE_V = (0, 0, 1), (0, 0, 1)
-TRIES, SEED, TEMP = 14000, 3, 100.0
+AT_HOME = ()
+COUNTS = ()
+LIST_V = (0, 0, 0)
+PLACE_V = (0, 0, 0)
+EQ_RUNS = ((0, 1), (1, 3))
+GT_A = ()
+WHOLE_X = (0,)
+WHOLE_M = ()
+TRIES, SEED, TEMP = 300, 3, 100.0
+SWAPS = 180000
+WARM = 70.0
 F32, BF, I32, U16, QC, U8 = "float32", "bfloat16", "int32", "uint16", "float8_e4m3fn_x4", "uint8"
 W0, T0, B0, A0, A1, L0, Z1, W1, T1, T2, FW = 16, 112, 208, 304, 400, 496, 784, 896, 992, 1088, 1184
 
@@ -25,14 +36,14 @@ SCRATCH = {
     "ab": _sb(36, I32), "ab16": _sb(36, U16), "lt2": _sb(6, U16), "lb": _sb(18, U16), "db": _sb(18, F32), "lbf": _sb(18, F32),
     "e16": _sb(18, F32), "el": _sb(18, U16), "zb": _sb(8, F32), "one": _sb(288, BF),
     "tab": _sb(296, F32), "pix": _sb(5, I32), "pc": _sb(6, I32), "pf": _sb(20, F32),
-    "j4": _sb(4, F32), "j16": _sb(96, F32), "j2": _sb(32, F32), "p4": _sb(12, F32), "sel4": _sb(288, BF), "sel16": _sb(288, BF),
+    "j16": _sb(16, F32), "p16": _sb(48, F32), "il": _sb(18, U16), "j2": _sb(32, F32), "p4": _sb(12, F32), "sel4": _sb(288, BF), "sel16": _sb(288, BF),
     "m16": _sb(16, F32), "m32": _sb(32, F32), "sb": _sb(6, F32), "jq": _sb(96, F32),
     "wt": _sb(1056, F32), "wt1": _sb(288, F32), "eq": _sb(288, BF), "eqs": _sb(288, BF), "eqb": _sb(288, F32), "sq": _sb(864, F32),
-    "dab": _sb(72, F32), "b16": _sb(144, F32), "aoff": _sb(72, U16), "bm": _sb(256, BF),
+    "bs": _sb(72, F32), "aoff": _sb(72, U16), "bm": _sb(256, BF),
     "cqb": _sb(512, BF), "cq": _sb(128, QC), "cs": _sb(128, U8), "eb": _sb(2048, BF), "eqq": _sb(512, QC), "es": _sb(512, U8),
     "fw": _sb(FW, BF), "t2": _sb(288, BF), "fq": _sb(144, QC), "fs": _sb(144, U8),
-    "pr": _sb(216, F32), "gd": _sb(72, F32), "doff": _sb(144, U16),
-    "junk": _sb(1152 + 288, BF), "jw": _sb(6 * 288, BF), "jx": _sb(6 * 288, BF), "jr": _sb(6 * 96, BF), "js": _sb(6 * 96, BF),
+    "pr": _sb(216, F32), "doff": _sb(144, U16),
+    "junk": _sb(1152 + 320, BF), "jw": _sb(6 * 288, BF), "jx": _sb(6 * 288, BF), "jr": _sb(6 * 96, BF), "js": _sb(6 * 96, BF),
     "acc": _sb(10, F32), "acci": _sb(10, I32),
     "un": _sb(30, I32), "n16": _sb(18, U16), "nr": _sb(288, BF), "ga": _sb(4, F32), "g32": _sb(32, F32), "g32t": _sb(32, F32),
     "gt": _sb(288, BF), "ge": _sb(288, BF), "cap": _sb(290, BF), "cum": _sb(288, BF), "wl": _sb(6, F32), "wl16": _sb(6, U16),
@@ -54,11 +65,13 @@ for _t in range(R):
         SCRATCH["gq%d" % _t] = _sb(128, QC)
         SCRATCH["gs%d" % _t] = _sb(128, U8)
     else:
-        SCRATCH["lh%d" % _t] = _sb(24, U16)
+        SCRATCH["lh%d" % _t] = _sb(18 if _t in COUNTS else 24, U16)
+    if _t in COUNTS:
+        SCRATCH["n%d" % _t] = _sb(18, U16)
 SEMAPHORES = ["sv", "sa", "st", "sg", "left", "od"] + ["d%d" % k for k in range(48)] + ["aq%d" % t for t in range(R)] + [
     "ah%d" % t for t in range(R) if t not in AT_HOME]
 
-PER = ("t2 fq fs pr gd doff junk jw jx jr js acc acci un n16 nr ga g32 g32t gt ge cap cum wl wl16 wr kk ks rk rk16 hr hs "
+PER = ("t2 fq fs pr doff junk jw jx jr js acc acci un n16 nr ga g32 g32t gt ge cap cum wl wl16 wr kk ks rk rk16 hr hs "
        "dx xa mx mt mq8 ms8 rr").split()
 WIDE = {k: v[1][1] for k, v in SCRATCH.items()}
 for _k in PER:
@@ -192,6 +205,11 @@ def build(g, core, T, topo):
             ts(out, in_, scale, None, A.mult)
         either()
 
+    def blank(out, c=0.0):
+        act(out, V("one", 0, size(out)), AF.Copy, scale=c)
+        fill(out, c)
+        either()
+
     def line(out, in_, scale, bias):
         act(out, in_, AF.Identity, scale=scale, bias=bias)
         ts(out, in_, scale, bias, A.mult, A.add)
@@ -237,28 +255,30 @@ def build(g, core, T, topo):
     dma("s", T.ab[:, 0:18], T.pa[:], [], [V("ab", 0, 18)], 1900)
     dma("a", T.ab[:, 18:36], T.pb[:], [], [V("ab", 18, 36)], 1900)
     dma("a", T.ub[:], T.u[:], [], [V("ub")], 2400)
-    dma("s", T.x0[:, X0 + 4 * E:], T.x[:, 4 * E:], [], [V("x0", X0 + 4 * E)], 3200)
+    dma("s", T.x0[:, X0 + 4 * E:X0 + 4 * P], T.x[:, 4 * E:4 * P], [], [V("x0", X0 + 4 * E, X0 + 4 * P)], 2900)
+    dma("s", T.x0[:, X0 + 4 * P:], T.x[:, 4 * P:], [], [V("x0", X0 + 4 * P)], 3200)
     dma("s", T.x0[:, X0:X0 + 4 * E], T.x[:, 0:4 * E], [], [V("x0", X0, X0 + 4 * E)], 3600)
     dma("s", T.wq[:].bitcast(dt.uint8), T.wc[:], [V("ab")], [V("wq")], 2500)
     dma("s", T.wp[:], T.ws[:], [V("ab")], [V("wp")], 2700)
 
     iota(V("pix"), [[1, 5]], 0, 1)
-    iota(V("j16"), [[0, 6], [1, 16]], 0, 0)
+    iota(V("j16"), [[1, 16]], 0, 0)
     iota(V("tab"), [[1, 296]], 1, 0)
     iota(V("ui"), [[1, R], [16, 8]], 0, 0)
-    iota(V("j4"), [[1, 4]], 0, 0)
     iota(V("j2"), [[1, 2], [0, 16]], 0, 0)
     fill(V("one"), 1.0)
-    fill(fw(0, W0), 0.0)
-    fill(fw(Z1, W1 - Z1), 0.0)
-    fill(V("wt1", 0, 96), 0.0)
-    fill(V("zb", 0, 1), 0.0)
-    fill(V("zb", 1, 8), BIG)
-    for t in range(R):
-        fill(V("x%d" % t, 0, X0), 0.0)
-    fill(V("cap", 289, SCRATCH["cap"][1][1], SCRATCH["cap"][1][1] // R), 0.0)
+    blank(fw(0, W0))
+    blank(fw(Z1, W1 - Z1))
+    blank(V("wt1", 0, 96))
+    blank(V("zb", 0, 1))
+    blank(V("zb", 1, 8), BIG)
+    blank(V("x0", 0, 16), -BIG)
+    blank(V("x0", 16, X0))
+    for t in range(1, R):
+        move(V("x%d" % t, 0, X0), V("x0", 0, X0))
+    blank(V("cap", 289, SCRATCH["cap"][1][1], SCRATCH["cap"][1][1] // R))
     if AT_HOME:
-        fill(V("fb", 4 * E), 0.0)
+        blank(V("fb", 4 * E))
     sel(V("bm", 0, 128), V("one", 0, 128), [[-16, 8], [0, 16]], A.is_ge, 0, 1)
     sel(V("bm", 128, 256), V("bm", 0, 128), [[16, 8], [0, 16]], A.is_ge, 15, -1)
     for e in range(4):
@@ -287,19 +307,22 @@ def build(g, core, T, topo):
     ts(K16, K0, 1.0, None, A.max)
     move(NK16, K16, -1.0)
     ts(V("m16"), V("j16", 0, 16), I0, None, A.is_equal)
-    ts(V("p4", 0, 4), V("j4"), S_, None, A.not_equal)
-    ts(V("p4", 4, 8), V("j4"), S1, LIFT, A.is_equal, A.mult)
+    ts(V("p4", 0, 4), V("j16", 0, 4), S_, None, A.not_equal)
+    ts(V("p4", 4, 8), V("j16", 0, 4), S1, LIFT, A.is_equal, A.mult)
     tt(V("p4", 8, 12), V("p4", 0, 4), V("p4", 4, 8), A.max)
     for s in range(4):
         move(V("sel4", s, 288, 4), V("one", 0, 72), col("p4", 8 + s))
-    ts(V("sel16", 96, 192), V("j16"), I0, None, A.not_equal)
-    ts(V("sel16", 192, 288), V("j16"), I1, LIFT, A.is_equal, A.mult)
-    tt(V("sel16", 0, 96), V("sel16", 96, 192), V("sel16", 192, 288), A.max)
+    ts(V("p16", 16, 32), V("j16"), I0, None, A.not_equal)
+    ts(V("p16", 32, 48), V("j16"), I1, LIFT, A.is_equal, A.mult)
+    tt(V("p16", 0, 16), V("p16", 16, 32), V("p16", 32, 48), A.max)
+    ts(V("il"), V("one", 0, 18), I0, None, A.mult)
+    n = max([hi - lo for lo, hi in EQ_RUNS])
+    move(V("sel16", 0, B * n), (V("p16", 0, 16), V("il", 0, 6 * n)))
     SEL16 = V("sel16", 0, 96)
     ts(V("j2"), V("j2"), H_, None, A.is_equal)
-    line(V("m32"), V("j2"), 1440.0, -1152.0)
+    line(V("m32"), V("j2"), 1440.0, -1343.0)
     line(V("sb"), V("tab", 0, 6), 32.0, I2)
-    line(V("jq"), V("tab", 0, 96), 1.0 / 128, -2.0)
+    line(V("jq"), V("tab", 0, 96), 1.0 / 128, -34.0)
     for k in range(6):
         w = (0.5 if k < 3 else -0.5) * 256.0 ** (k % 3)
         move(fw(W0 + 16 * k, 16), V("m16"), w)
@@ -329,32 +352,38 @@ def build(g, core, T, topo):
     move(V("wt1", 192, 288), (V("wt1", 0, 192), pa[1]))
     move(V("wt", 384, 480), (V("wt1"), pa[2]))
     move(V("wt", 480, 768), (V("tab"), V("ab16", 0, 18)), 4.0)
-    move(V("wt", 768, 1056), (V("tab"), V("ab16", 18, 36)), 4.0)
+    move(V("wt", 768, 1056), (V("tab"), V("ab16", 18, 36)), 4.0 / 128)
     for k, (win, lst) in enumerate(((V("wt", 0, 192), pb[1]), (V("wt", 0, 288), pb[2]), (V("wt1"), pb[2]))):
         tt(V("eq", B * k, B * k + B), (win, lst), V("wt", 192 + B * k, 288 + B * k), A.is_equal)
-        scan(V("eqs", B * k, B * k + B), SEL16, V("eq", B * k, B * k + B), op1=A.max)
-        tt(V("lbf", 6 * k, 6 * k + 6), V("eqs", B * k + 15, B * k + B, 16), V("db", 6 * k, 6 * k + 6), A.mult)
-        cp(V("lb", 6 * k, 6 * k + 6), V("lbf", 6 * k, 6 * k + 6))
+    for lo, hi in EQ_RUNS:
+        scan(V("eqs", B * lo, B * hi), V("sel16", 0, B * (hi - lo)), V("eq", B * lo, B * hi), op1=A.max)
+        tt(V("lbf", 6 * lo, 6 * hi), V("eqs", B * lo + 15, B * hi, 16), V("db", 6 * lo, 6 * hi), A.mult)
+        cp(V("lb", 6 * lo, 6 * hi), V("lbf", 6 * lo, 6 * hi))
     for k in range(3):
         scan(V("sq", P * k, P * k + P), V("sel4"), V("wt", 192 + P * k, 480 + P * k))
 
     def SQ(lo, hi):
         return V("sq", 4 * lo + 3, 4 * hi, 4)
     ts(V("aoff"), SQ(72, 144), F4, R12, A.mult, A.add)
-    tt(V("dab"), SQ(72, 144), SQ(144, 216), A.subtract)
-    move(V("b16", 0, 72), SQ(144, 216), 16.0)
+    line(V("bs"), SQ(144, 216), F4, 0.125)
 
     for t in range(R):
         NOW[0] = t
         x, xn = "x%d" % t, "x%d" % (t + 1)
         xq, xs, lq, ls, hh, lh = ["%s%d" % (s, t) for s in ("xq", "xs", "lq", "ls", "h", "lh")]
-        win = V(x)
+        win = V(x, 16)
         home = t in AT_HOME
         ut, ust = V("ut", 128 * t, 128 * t + 128), V("ust", 128 * t, 128 * t + 128)
-        quant(V(xq, E, P), V(xs, E, P), V(x, X0 + 4 * E, X0 + 4 * P))
-        mm(PS(BANK_S, 0, 192), ut, ust, V(xq, E, P), V(xs, E, P))
-        quant(V(xq, P, P + 128), V(xs, P, P + 128), V(x, X0 + 4 * 256))
-        mm(PS(BANK_Q, 0, 128), ut, ust, V(xq, P, P + 128), V(xs, P, P + 128))
+        if t in WHOLE_X:
+            quant(V(xq, E, C), V(xs, E, C), V(x, X0 + 4 * E))
+            mm(PS(BANK_S, 0, P), ut, ust, V(xq, E, C), V(xs, E, C))
+            last = PS(BANK_S, 192, P)
+        else:
+            quant(V(xq, E, P), V(xs, E, P), V(x, X0 + 4 * E, X0 + 4 * P))
+            mm(PS(BANK_S, 0, 192), ut, ust, V(xq, E, P), V(xs, E, P))
+            quant(V(xq, P, P + 128), V(xs, P, P + 128), V(x, X0 + 4 * 256))
+            mm(PS(BANK_Q, 0, 128), ut, ust, V(xq, P, P + 128), V(xs, P, P + 128))
+            last = PS(BANK_Q, 32, 128)
         if not home:
             quant(V(xq, 0, 128), V(xs, 0, 128), V(x, X0, X0 + 512))
             send([(T[lq][:].bitcast(dt.uint8), T[xq][:, 0:P].bitcast(dt.uint8)), (T[ls][:], T[xs][:, 0:P])], "aq%d" % t,
@@ -364,7 +393,7 @@ def build(g, core, T, topo):
         tt(V("t2", 0, 96), (fw(0, B0), V("lb", 0, 6)), fw(L0 + B), A.not_equal)
         tt(fw(B0), (fw(W0, 192), pa[1]), V("t2", 0, 96), A.mult)
         tt(fw(T1), (fw(W1 - B, 192), pa[1]), fw(L0 + B), A.mult)
-        tt(fw(L0 + 192), PS(BANK_Q, 32, 128), V("eqb", 192, 288), A.is_lt)
+        tt(fw(L0 + 192), last, V("eqb", 192, 288), A.is_lt)
         tt(V("t2", 96, 192), (fw(0, A0), V("lb", 6, 12)), fw(L0 + 192), A.not_equal)
         tt(V("t2", 192, 288), (fw(Z1, T2 - Z1), V("lb", 12, 18)), fw(L0 + 192), A.not_equal)
         tt(fw(A0), (fw(W0, P), pa[2]), V("t2", 96, 192), A.mult)
@@ -384,23 +413,39 @@ def build(g, core, T, topo):
         ts(V("un", 1, 30, 3), V("acci"), 8, 255, A.logical_shift_right, A.bitwise_and)
         ts(V("un", 2, 30, 3), V("acci"), 16, None, A.logical_shift_right)
         tt(V("un", 0, 12), V("un", 0, 12), V("un", 18, 30), A.add)
-        cp(V("n16"), V("un", 0, 18))
+        if t in COUNTS:
+            nn = "n%d" % t
+            cp(V(nn), V("un", 0, 18))
+            send([(T[lh][:], T[nn][:])], "ah%d" % t, [V(nn)], [V(lh)], 2200)
+            n16, came = V(lh), ("ah%d" % t, 1)
+        else:
+            cp(V("n16"), V("un", 0, 18))
+            n16, came = V("n16"), None
         quant(V("fq"), V("fs"), fw(B0, 576))
         mm(PS(BANK_S, 0, 144), V("cq"), V("cs"), V("fq"), V("fs"))
         tt(V("pr", 0, 144), PS(BANK_S, 0, 144), SQ(0, 144), A.mult)
-        tt(V("gd"), PS(BANK_S, 72, 144), V("dab"), A.mult)
+        tt(V("pr", 144, 216), V("bs"), PS(BANK_S, 72, 144), A.subtract)
         tt(V("pr", 24, 48), V("pr", 24, 48), V("pr", 48, 72), A.max)
-        tt(V("pr", 144, 216), V("gd"), V("b16", 0, 72), A.add)
+        ts(V("doff", 72, 144), V("pr", 144, 216), 128.0, R12, A.mult, A.add)
         tt(V("pr", 96, 144), V("pr", 96, 144), V("pr", 0, 48), A.max)
-        ts(V("doff"), V("pr", 72, 216), F4D, R12, A.mult, A.add)
-        act(V("junk", j, j + P), (V("tab"), V("n16")), AF.Sign, bias=TH, acc=col("ga", 0))
-        line(V("nr"), (V("tab"), V("n16")), 1.0, -1.0)
-        ts(V("g32"), V("m32"), col("ga", 0), 192.0, A.add, A.is_ge)
+        ts(V("doff", 0, 72), V("pr", 72, 144), F4D, R12, A.mult, A.add)
+        act(V("junk", j, j + P), (V("tab"), n16), AF.Sign, bias=TH, acc=col("ga", 0))
+        ops[-1]["arr"] = came
+        line(V("nr"), (V("tab"), n16), 2.0, -34.0)
+        ops[-1]["arr"] = came
+        act(V("g32"), V("m32"), AF.Sign, bias=col("ga", 0))
         turn(V("g32t"), V("g32"))
+        act(V("g32"), V("g32t"), AF.Identity, acc=col("ga", 1))
         red(col("ga", 1), V("g32t"))
-        ts(V("gt"), V("nr"), col("ga", 1), -2.0, A.is_gt, A.mult)
+        either()
         ts(V("ge"), V("nr"), col("ga", 1), 2.0, A.is_ge, A.mult)
-        scan(V("cap", 1, 289, -1), V("gt", 0, P, -1), V("gt", 0, P, -1), 0.0, A.add, A.min)
+        if t in GT_A:
+            act(V("junk", j + P, j + P + 32), V("g32t"), AF.Identity, bias=1.0 / 32, acc=col("ga", 2))
+            act(V("gt"), V("nr"), AF.Sign, scale=-1.0, bias=col("ga", 2))
+            scan(V("cap", 1, 289, -1), V("gt", 0, P, -1), V("one"), 0.0, A.add, A.subtract)
+        else:
+            ts(V("gt"), V("nr"), col("ga", 1), -2.0, A.is_gt, A.mult)
+            scan(V("cap", 1, 289, -1), V("gt", 0, P, -1), V("gt", 0, P, -1), 0.0, A.add, A.min)
         scan(V("cum"), V("ge"), V("cap", 2, 290), -192.0, A.add, A.min)
         na = 6 - LIST_V[t]
         for c in range(6):
@@ -440,19 +485,20 @@ def build(g, core, T, topo):
             quant(V(gq), V(gs), V("fb"))
             send([(T[lq][:, 0:128].bitcast(dt.uint8), T[gq][:].bitcast(dt.uint8)), (T[ls][:, 0:128], T[gs][:])], "aq%d" % t,
                  [V(gq), V(gs)], [V(lq), V(ls)], 2500)
-        else:
+        elif t not in COUNTS:
             send([(T[lh][:], T[hh][:])], "ah%d" % t, [V(hh)], [V(lh)], 2200)
-        for k in range(3):
-            lo, hi = 384 * k, 384 * k + 384
-            move(V("xa", lo, hi), (win, V("aoff", 24 * k, 24 * k + 24)))
-            tt(V("mx", lo, hi), (win, V("doff", 72 + 24 * k, 96 + 24 * k)), V("xa", lo, hi), A.max)
-            if (t, k) in M_DMA:
-                move(V("mt", lo, hi), (win, V("doff", 24 * k, 24 * k + 24)))
+        n = 12 if t in HALVES else 24
+        for c in range(0, 72, n):
+            lo, hi = 16 * c, 16 * (c + n)
+            move(V("xa", lo, hi), (win, V("aoff", c, c + n)))
+            tt(V("mx", lo, hi), (V(x), V("doff", 72 + c, 72 + c + n)), V("xa", lo, hi), A.max)
+            if (t, c // 24) in M_DMA:
+                move(V("mt", lo, hi), (win, V("doff", c, c + n)))
                 add("g", 700, [V("mx", lo, hi), V("mt", lo, hi), V("vb")], [V("mt", lo, hi)],
                     lambda o=V("mt", lo, hi), r=V("mx", lo, hi): g.dma_start(ap(o), ap(r), accum_op=A.add), kind="d", lat=2800)
             else:
-                tt(V("mt", lo, hi), (win, V("doff", 24 * k, 24 * k + 24)), V("mx", lo, hi), A.add)
-        for h, (c0, n, skip) in enumerate(((0, 192, 0), (160, 128, 32))):
+                tt(V("mt", lo, hi), (win, V("doff", c, c + n)), V("mx", lo, hi), A.add)
+        for h, (c0, n, skip) in enumerate(((0, P, 0),) if t in WHOLE_M else ((0, 192, 0), (160, 128, 32))):
             lo, hi = 4 * (c0 + skip), 4 * (c0 + n)
             mq, ms = V("mq8", 192 * h, 192 * h + n), V("ms8", 192 * h, 192 * h + n)
             quant(mq, ms, V("mt", 4 * c0, hi))
@@ -465,6 +511,9 @@ def build(g, core, T, topo):
                     dma("s", ap(new), ap(old), [old], [new], 2200)
                     add("g", 700, [V("rr", l2, l2 + 384), new, V("vb")], [new],
                         lambda new=new, r=V("rr", l2, l2 + 384): g.dma_start(ap(new), ap(r), accum_op=A.add), kind="d", lat=2800)
+                elif (t, l2 // 384) in BY_ROW:
+                    for b in range(4):
+                        tt(new[0:1] + (new[1] + b, new[2], 4), V("rr", l2 + b, l2 + 384, 4), old[0:1] + (old[1] + b, old[2], 4), A.add)
                 else:
                     tt(new, V("rr", l2, l2 + 384), old, A.add)
         if t == R - 1:
@@ -488,7 +537,9 @@ def build(g, core, T, topo):
                 tt(V(xn, X0 + b, X0 + 4 * E, 4), PS(bank, 0, E), V(x, X0 + b, X0 + 4 * E, 4), A.max)
             else:
                 move(V("dx", b, 4 * P, 4), PS(bank, 0, P))
-        if not home:
+        if t in COUNTS:
+            tt(V(xn, X0, X0 + 4 * E), (V("dx"), V(hh)), V(x, X0, X0 + 4 * E), A.max)
+        elif not home:
             tt(V(xn, X0, X0 + 4 * E), (V("dx"), V(lh)), V(x, X0, X0 + 4 * E), A.max, arr=("ah%d" % t, 1))
     xn = "x%d" % R
     quant(V("oq", 0, 128), V("op", 0, 128), V(xn, X0, X0 + 512))
@@ -515,9 +566,13 @@ def link(ops):
                     deps.add(j)
         deps.discard(k)
         o["deps"] = sorted(deps)
-        o["after"] = []
+        far = 0
         for j in deps:
-            ops[j]["after"].append(k)
+            far |= ops[j]["behind"]
+        o["near"], o["next"], o["all"] = [j for j in o["deps"] if not far >> j & 1], [], tuple(range(len(o["ways"])))
+        o["behind"] = far | sum([1 << j for j in deps if not far >> j & 1])
+        for j in o["near"]:
+            ops[j]["next"].append(k)
         for v in o["rd"]:
             seen.setdefault(v[0], []).append((k, v, False))
         for v in o["wr"]:
@@ -525,16 +580,21 @@ def link(ops):
 
 
 def deal(ops, key, way, back, lean):
-    pre = "after" if back else "deps"
+    pre = "next" if back else "near"
     n = len(ops)
     at, fin, w = [0.0] * n, [0.0] * n, list(way)
     st, en = {q: [] for q in "vatgs"}, {q: [] for q in "vatgs"}
-    for k in sorted(range(n), key=lambda k: (key[k], k)):
+    for k in sorted(range(n), key=lambda k: key[k]):
         o = ops[k]
-        can = max([fin[j] for j in o[pre]] + [0.0]) + (o["lat"] if back else 0.0)
+        can = 0.0
+        for j in o[pre]:
+            if fin[j] > can:
+                can = fin[j]
+        if back:
+            can += o["lat"]
         best = None
-        for i in ((w[k],) if back else range(len(o["ways"]))):
-            q, c = o["ways"][i][0:2]
+        for i in ((w[k],) if back else o["all"]):
+            q, c, f = o["ways"][i]
             s, e = st[q], en[q]
             m, t = len(s), can
             while m and e[m - 1] > can:
@@ -551,6 +611,65 @@ def deal(ops, key, way, back, lean):
         at[k] = t
         fin[k] = t + c + HOP + (0.0 if back else o["lat"])
     return max(fin), at, w
+
+
+def polish(ops, start, rng):
+    n = len(ops)
+    near, behind = [o["near"] for o in ops], [o["behind"] for o in ops]
+    tail = [HOP + o["lat"] for o in ops]
+    ways = [[("vatgs".index(w[0]), w[1]) for w in o["ways"]] for o in ops]
+    seq, way = sorted(range(n), key=lambda k: (start[1][k], k)), list(start[2])
+
+    def run(seq, way, lo, at, fin, by, was):
+        free, last = list(was[lo][0]), list(was[lo][1])
+        for i in range(lo, n):
+            k = seq[i]
+            was[i] = (tuple(free), tuple(last))
+            q, c = ways[k][way[k]]
+            t, b = free[q], last[q]
+            for j in near[k]:
+                if fin[j] > t:
+                    t, b = fin[j], j
+            at[k], by[k], free[q], last[q], fin[k] = t, b, t + c, ~k, t + c + tail[k]
+        return max(fin)
+
+    at, fin, by, was = [0.0] * n, [0.0] * n, [None] * n, [((0.0,) * 5, (None,) * 5)] * n
+    now = run(seq, way, 0, at, fin, by, was)
+    best, held = (now, list(at), list(way)), None
+    for it in range(SWAPS):
+        if held is None:
+            k, held, two = fin.index(now), [], []
+            while by[k] is not None:
+                if len(ways[k]) > 1:
+                    two.append(k)
+                if by[k] < 0:
+                    held.append((k, ~by[k]))
+                k = ~by[k] if by[k] < 0 else by[k]
+            pos = {k: i for i, k in enumerate(seq)}
+        r = rng.random(5).tolist()
+        s2, w2 = seq, way
+        if r[0] < 0.15 and two:
+            k = two[int(r[1] * len(two))]
+            w2 = list(way)
+            w2[k], lo = 1 - w2[k], pos[k]
+        else:
+            v, u = held[int(r[1] * len(held))]
+            if behind[v] >> u & 1:
+                continue
+            if r[2] < 0.5:
+                lo, hi = pos[u], min(n, pos[v] + 1 + int(12 * r[3] * r[3]))
+                late = [k == u or behind[k] >> u & 1 for k in seq[lo:hi]]
+            else:
+                lo, hi = max(0, pos[u] - int(12 * r[3] * r[3])), pos[v] + 1
+                late = [not (k == v or behind[v] >> k & 1) for k in seq[lo:hi]]
+            s2 = seq[:lo] + [k for k, e in zip(seq[lo:hi], late) if not e] + [k for k, e in zip(seq[lo:hi], late) if e] + seq[hi:]
+        a2, f2, b2, was2 = list(at), list(fin), list(by), list(was)
+        got = run(s2, w2, lo, a2, f2, b2, was2)
+        if got <= now - WARM * (1.0 - it / SWAPS) * math.log(1.0 - r[4]):
+            now, seq, way, at, fin, by, was, held = got, s2, w2, a2, f2, b2, was2, None
+            if got < best[0]:
+                best = (got, list(at), list(way))
+    return best
 
 
 KEPT = {}
@@ -577,17 +696,19 @@ def order(ops):
                     le[k] += d
             if r > 0.6:
                 shake[a:a + int(rng.integers(1, 25))] += float(rng.normal(0.0, 2000.0))
-            key = [float(shake[k]) - now[1][k] - ops[k]["ways"][now[2][k]][1] - ops[k]["lat"] for k in range(n)]
+            shake = shake.tolist()
+            key = [shake[k] - now[1][k] - ops[k]["ways"][now[2][k]][1] - ops[k]["lat"] for k in range(n)]
             for k in range(n - 1, -1, -1):
-                for j in ops[k]["deps"]:
-                    key[j] = max(key[j], key[k] + 0.01)
+                for j in ops[k]["near"]:
+                    if key[j] <= key[k]:
+                        key[j] = key[k] + 0.01
             b = deal(ops, key, now[2], True, le)
             got = deal(ops, [-b[1][k] - ops[k]["ways"][b[2][k]][1] for k in range(n)], b[2], False, le)
             if got[0] <= now[0] + TEMP * (1.0 - it / TRIES) * float(rng.exponential()):
                 now, lean = got, le
             if got[0] < best[0]:
                 best = got
-        KEPT["best"] = best
+        KEPT["best"] = polish(ops, best, rng)
     end, at, way = KEPT["best"]
     for k, o in enumerate(ops):
         o["at"] = at[k]

@@ -3,7 +3,10 @@ import numpy as np
 from concourse.mybir import dt, AluOpType as A, AxisListType as AX, ActivationFunctionType as AF
 
 C, E, B, P, R = 384, 96, 96, 288, 3
-X0 = 32
+XB, X0, XM = 4 * B, 4 * B + 32, 4 * B + 32 + 4 * C
+DROP = XM / 16
+PICK0 = True
+UNIT = 2048.0
 BIG = 1e29
 LIFT = 2.0 ** 51
 BY_DMA = ((0, 0), (0, 1), (1, 0), (2, 0), (2, 1))
@@ -11,15 +14,20 @@ BY_ROW = ((0, 2), (1, 2), (2, 2))
 HALVES = ()
 M_DMA = ()
 AT_HOME = ()
-COUNTS = ()
-LIST_V = (0, 0, 0)
-PLACE_V = (0, 0, 0)
+COUNTS = (2,)
+LIST_V = (0, 0, 2)
+PLACE_V = (1, 1, 3)
 EQ_RUNS = ((0, 1), (1, 3))
 GT_A = ()
+SIDES = ()
+AFTER = ()
+SEL4 = 96
+LEANING = (0, 1)
+SPLIT = (0,)
 WHOLE_X = (0,)
 WHOLE_M = ()
-TRIES, SEED, TEMP = 300, 3, 100.0
-SWAPS = 180000
+TRIES, SEED, TEMP = 300, 1, 100.0
+SWAPS = 300000
 WARM = 70.0
 F32, BF, I32, U16, QC, U8 = "float32", "bfloat16", "int32", "uint16", "float8_e4m3fn_x4", "uint8"
 W0, T0, B0, A0, A1, L0, Z1, W1, T1, T2, FW = 16, 112, 208, 304, 400, 496, 784, 896, 992, 1088, 1184
@@ -35,11 +43,11 @@ SCRATCH = {
     "wq": _sb(512, QC), "wp": _sb(512, U8), "oq": _sb(384, QC), "op": _sb(384, U8),
     "ab": _sb(36, I32), "ab16": _sb(36, U16), "lt2": _sb(6, U16), "lb": _sb(18, U16), "db": _sb(18, F32), "lbf": _sb(18, F32),
     "e16": _sb(18, F32), "el": _sb(18, U16), "zb": _sb(8, F32), "one": _sb(288, BF),
-    "tab": _sb(296, F32), "pix": _sb(5, I32), "pc": _sb(6, I32), "pf": _sb(20, F32),
+    "tab": _sb(296, F32), "pix": _sb(5, I32), "pc": _sb(6, I32), "pf": _sb(24, F32),
     "j16": _sb(16, F32), "p16": _sb(48, F32), "il": _sb(18, U16), "j2": _sb(32, F32), "p4": _sb(12, F32), "sel4": _sb(288, BF), "sel16": _sb(288, BF),
     "m16": _sb(16, F32), "m32": _sb(32, F32), "sb": _sb(6, F32), "jq": _sb(96, F32),
-    "wt": _sb(1056, F32), "wt1": _sb(288, F32), "eq": _sb(288, BF), "eqs": _sb(288, BF), "eqb": _sb(288, F32), "sq": _sb(864, F32),
-    "bs": _sb(72, F32), "aoff": _sb(72, U16), "bm": _sb(256, BF),
+    "wt": _sb(480, F32), "a4": _sb(144, I32), "sr": _sb(288, F32), "wt1": _sb(288, F32), "eq": _sb(288, BF), "eqs": _sb(288, BF), "eqb": _sb(288, F32), "sq": _sb(216, F32),
+    "bs": _sb(72, F32), "aoff": _sb(72, U16), "boff": _sb(24, U16), "bm": _sb(256, BF),
     "cqb": _sb(512, BF), "cq": _sb(128, QC), "cs": _sb(128, U8), "eb": _sb(2048, BF), "eqq": _sb(512, QC), "es": _sb(512, U8),
     "fw": _sb(FW, BF), "t2": _sb(288, BF), "fq": _sb(144, QC), "fs": _sb(144, U8),
     "pr": _sb(216, F32), "doff": _sb(144, U16),
@@ -54,7 +62,7 @@ SCRATCH = {
     "ps": ("psum", [128, 4096], F32),
 }
 for _t in range(R + 1):
-    SCRATCH["x%d" % _t] = _sb(X0 + 4 * C, BF)
+    SCRATCH["x%d" % _t] = _sb(XM + 4 * B, BF)
 for _t in range(R):
     SCRATCH["xq%d" % _t] = _sb(P + 128, QC)
     SCRATCH["xs%d" % _t] = _sb(P + 128, U8)
@@ -68,7 +76,7 @@ for _t in range(R):
         SCRATCH["lh%d" % _t] = _sb(18 if _t in COUNTS else 24, U16)
     if _t in COUNTS:
         SCRATCH["n%d" % _t] = _sb(18, U16)
-SEMAPHORES = ["sv", "sa", "st", "sg", "left", "od"] + ["d%d" % k for k in range(48)] + ["aq%d" % t for t in range(R)] + [
+SEMAPHORES = ["sv", "sa", "st", "sg", "left", "od", "r1", "r2"] + ["d%d" % k for k in range(48)] + ["aq%d" % t for t in range(R)] + [
     "ah%d" % t for t in range(R) if t not in AT_HOME]
 
 PER = ("t2 fq fs pr doff junk jw jx jr js acc acci un n16 nr ga g32 g32t gt ge cap cum wl wl16 wr kk ks rk rk16 hr hs "
@@ -78,7 +86,10 @@ for _k in PER:
     SCRATCH[_k] = _sb(R * (-(-WIDE[_k] // 32) * 32), SCRATCH[_k][2])
 NOW = [0]
 
-CYC, HOP, LEAN = 0.92, 150.0, 300.0
+ROUGH = ((1.0, 1.56, 3.8, 110.0, 0.65, 0.8, 0.9), (1.13, 1.9, 5.0, 130.0, 0.75, 0.9, 1.0))
+HOP = ROUGH[0][3]
+LONG = 500.0
+CYC, LEAN = 0.92, 300.0
 BANK_Z, BANK_S, BANK_Q, BANK_D = 0, 4, 5, 6
 
 
@@ -109,8 +120,8 @@ def meet(a, b):
     return not (a[3] == b[3] and a[3] > 1 and (a[1] - b[1]) % a[3] != 0)
 
 
-def build(g, core, T, topo):
-    ops = []
+def build(g, core, T, topo, rough=ROUGH[0]):
+    ops, sent = [], []
     NOW[0] = 0
     rank = T.rank_of(core)
     nxt = T.cores[(rank + 1) % len(T.cores)]
@@ -133,7 +144,8 @@ def build(g, core, T, topo):
         return out
 
     def add(q, cost, rd, wr, fn, kind="c", lat=0.0, arr=None):
-        ops.append({"ways": [(q, cost, fn)], "rd": views(rd), "wr": views(wr), "kind": kind, "lat": lat, "arr": arr})
+        lat *= rough[4 if kind == "r" else 5 if q == "g" else 6]
+        ops.append({"ways": [(q, cost * rough[0], fn)], "rd": views(rd), "wr": views(wr), "kind": kind, "lat": lat, "arr": arr})
 
     def either():
         o = ops.pop()
@@ -141,10 +153,10 @@ def build(g, core, T, topo):
 
     def vcost(out, first, per):
         n = size(out)
-        return 50 + 1.56 * CYC * n if len(first) == 2 else 20 + CYC * max(64, n * per)
+        return 50 + rough[1] * CYC * n if len(first) == 2 else 20 + CYC * max(64, n * per)
 
     def ts(out, in0, s1, s2, op0, op1=None):
-        per = 1 if len(in0) == 2 or not narrow(out, in0) else 0.5
+        per = 0.5 if len(in0) != 2 and narrow(out, in0) else 1
         if op1 is None:
             fn = lambda: g.vector.tensor_scalar(ap(out), ap(in0), ap(s1), None, op0)
         else:
@@ -166,7 +178,7 @@ def build(g, core, T, topo):
         either()
 
     def scatter(win, off, in_):
-        add("v", 50 + 3.8 * CYC * size(in_), [in_, off], [win], lambda: g.vector.tensor_copy(ap((win, off)), ap(in_)))
+        add("v", 50 + rough[2] * CYC * size(in_), [in_, off], [win], lambda: g.vector.tensor_copy(ap((win, off)), ap(in_)))
 
     def scan(out, d0, d1, init=0.0, op0=A.mult, op1=A.add):
         add("v", vcost(out, d0, 0.5 if narrow(out, d0, d1) else 1), [d0, d1, init], [out],
@@ -195,7 +207,7 @@ def build(g, core, T, topo):
                 kw["accum_out"] = ap(acc)
             return g.scalar.activation(ap(out), ap(in_), f, **kw)
         n = size(out)
-        add("a", 65 + (25 if acc else 0) + CYC * n * (1.56 if len(in_) == 2 else 1), [in_, scale, bias], [out, acc], fn)
+        add("a", 65 + (25 if acc else 0) + CYC * n * (rough[1] if len(in_) == 2 else 1), [in_, scale, bias], [out, acc], fn)
 
     def move(out, in_, scale=None):
         act(out, in_, AF.Copy, scale=scale)
@@ -209,6 +221,9 @@ def build(g, core, T, topo):
         act(out, V("one", 0, size(out)), AF.Copy, scale=c)
         fill(out, c)
         either()
+        if c == 0.0 and out[3] == 1:
+            iota(out, [[0, size(out)]], 0, 0)
+            either()
 
     def line(out, in_, scale, bias):
         act(out, in_, AF.Identity, scale=scale, bias=bias)
@@ -243,8 +258,15 @@ def build(g, core, T, topo):
             rid, pid = topo.addr(nxt)[0:2]
             for dst, src in pairs:
                 g.remote_dma(dst, src, T.sem[sem], T.sem.left, pid, rid, topo.mask(core, nxt))
-        add("g", 300 * len(pairs) + (2500 if sem == "aq0" else 0), rd, wr, fn, kind="r", lat=lat, arr=None)
-        ops[-1]["calls"] = len(pairs)
+        first = ("first", 0, 1, 1)
+        if sent:
+            add("g", 300 * len(pairs), rd + [first], wr, fn, kind="r", lat=lat)
+            ops[-1]["calls"] = len(pairs)
+        else:
+            add("g", 300 * len(pairs) + 2500, rd, [first], fn, kind="r")
+            ops[-1]["calls"] = len(pairs)
+            add("s", 0, [first], wr, None, kind="r", lat=lat)
+        sent.append(sem)
 
     def col(name, k):
         return V(name, k, k + 1)
@@ -256,8 +278,15 @@ def build(g, core, T, topo):
     dma("a", T.ab[:, 18:36], T.pb[:], [], [V("ab", 18, 36)], 1900)
     dma("a", T.ub[:], T.u[:], [], [V("ub")], 2400)
     dma("s", T.x0[:, X0 + 4 * E:X0 + 4 * P], T.x[:, 4 * E:4 * P], [], [V("x0", X0 + 4 * E, X0 + 4 * P)], 2900)
-    dma("s", T.x0[:, X0 + 4 * P:], T.x[:, 4 * P:], [], [V("x0", X0 + 4 * P)], 3200)
+    dma("s", T.x0[:, X0 + 4 * P:XM], T.x[:, 4 * P:], [], [V("x0", X0 + 4 * P, XM)], 3200)
     dma("s", T.x0[:, X0:X0 + 4 * E], T.x[:, 0:4 * E], [], [V("x0", X0, X0 + 4 * E)], 3600)
+    for k, src in enumerate((T.pa, T.pb)):
+        for s in range(4):
+            dma("s", T.a4[4 * s:128:16, 72 * k:72 * k + 72], src[s:128:4, :], [], [("rows", 4 * k + s, 4 * k + s + 1, 1)], 2200)
+            ops[-1]["sem"] = "r1"
+    for s in range(1, 4):
+        dma("s", T.a4[s:128:4, :], T.a4[0:128:4, :], [("rows", 0, 8, 1)], [("rows", 8 + s, 9 + s, 1)], 2000)
+        ops[-1]["sem"] = "r2"
     dma("s", T.wq[:].bitcast(dt.uint8), T.wc[:], [V("ab")], [V("wq")], 2500)
     dma("s", T.wp[:], T.ws[:], [V("ab")], [V("wp")], 2700)
 
@@ -272,10 +301,10 @@ def build(g, core, T, topo):
     blank(V("wt1", 0, 96))
     blank(V("zb", 0, 1))
     blank(V("zb", 1, 8), BIG)
-    blank(V("x0", 0, 16), -BIG)
-    blank(V("x0", 16, X0))
+    blank(V("x0", XB, XB + 16), -BIG)
+    blank(V("x0", XB + 16, X0))
     for t in range(1, R):
-        move(V("x%d" % t, 0, X0), V("x0", 0, X0))
+        dma("s", T["x%d" % t][:, XB:X0], T.x0[:, XB:X0], [V("x0", XB, X0)], [V("x%d" % t, XB, X0)], 2000)
     blank(V("cap", 289, SCRATCH["cap"][1][1], SCRATCH["cap"][1][1] // R))
     if AT_HOME:
         blank(V("fb", 4 * E))
@@ -293,15 +322,16 @@ def build(g, core, T, topo):
     ts(col("pc", 4), col("pix", 0), 3, None, A.bitwise_and)
     ts(col("pc", 5), col("pix", 0), 4, 1, A.logical_shift_right, A.bitwise_and)
     cp(V("pf", 0, 6), V("pc"))
-    S_, S1, I0, I1, R_, H_, R12, RM4, TH, I2, F4, F4H, F4D, F4E, F16, K0, K16, NK16 = [col("pf", k) for k in range(18)]
+    S_, S1, I0, I1, R_, H_, R12, RM4, TH, I2, F4, F4H, SB0, F16, K0, K16, NK16, TH2 = [col("pf", k) for k in range(18)]
     line(R12, R_, 1.0, 12.0)
     line(RM4, R_, 1.0, -4.0)
-    line(TH, I0, -1.0, -1.5)
+    if len(AFTER) < R:
+        line(TH, I0, -1.0, -1.5)
+    if AFTER:
+        line(TH2, I0, -1.0, 15.5)
     line(I2, I0, 2.0, -223.0)
     ts(F4, S_, 3.0, 1.0 / LIFT, A.is_equal, A.max)
     move(F4H, F4, 4.0)
-    move(F4D, F4, 1.0 / 16)
-    move(F4E, F4, 1.0 / 64)
     ts(F16, I0, 15.0, 1.0 / LIFT, A.is_equal, A.max)
     ts(K0, I0, 15.0, LIFT, A.not_equal, A.mult)
     ts(K16, K0, 1.0, None, A.max)
@@ -311,7 +341,7 @@ def build(g, core, T, topo):
     ts(V("p4", 4, 8), V("j16", 0, 4), S1, LIFT, A.is_equal, A.mult)
     tt(V("p4", 8, 12), V("p4", 0, 4), V("p4", 4, 8), A.max)
     for s in range(4):
-        move(V("sel4", s, 288, 4), V("one", 0, 72), col("p4", 8 + s))
+        move(V("sel4", s, SEL4, 4), V("one", 0, SEL4 // 4), col("p4", 8 + s))
     ts(V("p16", 16, 32), V("j16"), I0, None, A.not_equal)
     ts(V("p16", 32, 48), V("j16"), I1, LIFT, A.is_equal, A.mult)
     tt(V("p16", 0, 16), V("p16", 16, 32), V("p16", 32, 48), A.max)
@@ -326,8 +356,11 @@ def build(g, core, T, topo):
     for k in range(6):
         w = (0.5 if k < 3 else -0.5) * 256.0 ** (k % 3)
         move(fw(W0 + 16 * k, 16), V("m16"), w)
-        move(V("wt", 16 * k, 16 * k + 16), V("tab", 16 * k, 16 * k + 16), 64.0 / w)
-        move(V("wt1", B + 16 * k, B + 16 * k + 16), V("tab", B + 16 * k, B + 16 * k + 16), 64.0 / w)
+        for name, lo in (("wt", 16 * k), ("wt1", B + 16 * k)):
+            move(V(name, lo, lo + 16), V("tab", lo, lo + 16), 16 * UNIT / w)
+            if k % 3:
+                iota(V(name, lo, lo + 16), [[int(16 * UNIT / w), 16]], int(16 * UNIT / w) * (lo + 1), 0)
+                either()
     move(fw(W1), fw(W0))
     cp(V("ul"), V("ui"))
     quant(V("uq"), V("us"), V("ub"))
@@ -351,43 +384,54 @@ def build(g, core, T, topo):
     move(V("wt", 288, 384), (V("wt", 0, 288), pa[2]))
     move(V("wt1", 192, 288), (V("wt1", 0, 192), pa[1]))
     move(V("wt", 384, 480), (V("wt1"), pa[2]))
-    move(V("wt", 480, 768), (V("tab"), V("ab16", 0, 18)), 4.0)
-    move(V("wt", 768, 1056), (V("tab"), V("ab16", 18, 36)), 4.0 / 128)
     for k, (win, lst) in enumerate(((V("wt", 0, 192), pb[1]), (V("wt", 0, 288), pb[2]), (V("wt1"), pb[2]))):
         tt(V("eq", B * k, B * k + B), (win, lst), V("wt", 192 + B * k, 288 + B * k), A.is_equal)
     for lo, hi in EQ_RUNS:
         scan(V("eqs", B * lo, B * hi), V("sel16", 0, B * (hi - lo)), V("eq", B * lo, B * hi), op1=A.max)
         tt(V("lbf", 6 * lo, 6 * hi), V("eqs", B * lo + 15, B * hi, 16), V("db", 6 * lo, 6 * hi), A.mult)
         cp(V("lb", 6 * lo, 6 * hi), V("lbf", 6 * lo, 6 * hi))
-    for k in range(3):
-        scan(V("sq", P * k, P * k + P), V("sel4"), V("wt", 192 + P * k, 480 + P * k))
+    for lo in range(0, P, SEL4):
+        scan(V("sr", lo, lo + SEL4), V("sel4", 0, SEL4), V("wt", 192 + lo, 192 + lo + SEL4))
+    move(V("sq", 0, 72), V("sr", 3, P, 4), F4)
+    for k in range(2):
+        for m in range(4):
+            ts(V("sq", 72 * k + 72 + m, 72 * k + 144, 4), V("a4", 72 * k + 18 * m, 72 * k + 18 * m + 18), 1.0, UNIT, A.add, A.mult)
+            ops[-1]["rd"].append(("rows", 0, 12, 1))
 
     def SQ(lo, hi):
-        return V("sq", 4 * lo + 3, 4 * hi, 4)
-    ts(V("aoff"), SQ(72, 144), F4, R12, A.mult, A.add)
-    line(V("bs"), SQ(144, 216), F4, 0.125)
+        return V("sq", lo, hi)
+    ts(V("aoff"), SQ(72, 144), 4.0 / UNIT, R12, A.mult, A.add)
+    if PICK0:
+        ts(V("boff"), SQ(144, 168), 4.0 / UNIT, R12, A.mult, A.add)
+        line(SB0, S_, 4.0 / DROP, (XM - 28.0) / DROP)
+        line(V("bs", 0, 24), V("tab", 0, 24), 16.0 / DROP, SB0)
+        line(V("bs", 24, 72), SQ(168, 216), 4.0 / UNIT / DROP, 16.0 / DROP)
+    else:
+        line(V("bs"), SQ(144, 216), 4.0 / UNIT / DROP, 16.0 / DROP)
 
     for t in range(R):
         NOW[0] = t
         x, xn = "x%d" % t, "x%d" % (t + 1)
         xq, xs, lq, ls, hh, lh = ["%s%d" % (s, t) for s in ("xq", "xs", "lq", "ls", "h", "lh")]
-        win = V(x, 16)
+        win = V(x, XB + 16, XM)
         home = t in AT_HOME
         ut, ust = V("ut", 128 * t, 128 * t + 128), V("ust", 128 * t, 128 * t + 128)
         if t in WHOLE_X:
-            quant(V(xq, E, C), V(xs, E, C), V(x, X0 + 4 * E))
+            quant(V(xq, E, C), V(xs, E, C), V(x, X0 + 4 * E, XM))
             mm(PS(BANK_S, 0, P), ut, ust, V(xq, E, C), V(xs, E, C))
             last = PS(BANK_S, 192, P)
         else:
             quant(V(xq, E, P), V(xs, E, P), V(x, X0 + 4 * E, X0 + 4 * P))
             mm(PS(BANK_S, 0, 192), ut, ust, V(xq, E, P), V(xs, E, P))
-            quant(V(xq, P, P + 128), V(xs, P, P + 128), V(x, X0 + 4 * 256))
+            quant(V(xq, P, P + 128), V(xs, P, P + 128), V(x, X0 + 4 * 256, XM))
             mm(PS(BANK_Q, 0, 128), ut, ust, V(xq, P, P + 128), V(xs, P, P + 128))
             last = PS(BANK_Q, 32, 128)
         if not home:
-            quant(V(xq, 0, 128), V(xs, 0, 128), V(x, X0, X0 + 512))
-            send([(T[lq][:].bitcast(dt.uint8), T[xq][:, 0:P].bitcast(dt.uint8)), (T[ls][:], T[xs][:, 0:P])], "aq%d" % t,
-                 [V(xq, 0, P), V(xs, 0, P)], [V(lq), V(ls)], 3500)
+            for lo, hi in (((128, P), (0, 128)) if t in SPLIT else ((0, P),)):
+                if lo == 0:
+                    quant(V(xq, 0, 128), V(xs, 0, 128), V(x, X0, X0 + 512))
+                send([(T[lq][:, lo:hi].bitcast(dt.uint8), T[xq][:, lo:hi].bitcast(dt.uint8)), (T[ls][:, lo:hi], T[xs][:, lo:hi])], "aq%d" % t,
+                     [V(xq, lo, hi), V(xs, lo, hi)], [V(lq, lo, hi), V(ls, lo, hi)], 3500)
         tt(fw(L0, 192), PS(BANK_S, 0, 192), V("eqb", 0, 192), A.is_lt)
         tt(fw(T0), (fw(W0), pa[0]), fw(L0), A.mult)
         tt(V("t2", 0, 96), (fw(0, B0), V("lb", 0, 6)), fw(L0 + B), A.not_equal)
@@ -403,12 +447,18 @@ def build(g, core, T, topo):
         for k, run in enumerate((fw(A0), fw(A1), fw(T2), fw(T0, 192), fw(T1))):
             for w in range(2):
                 n = size(run)
-                act(V("junk", j, j + n), run, AF.Abs if w else AF.Identity, acc=col("acc", 5 * w + k))
-                red(col("acc", 5 * w + k), run, sizes=bool(w))
-                either()
+                if t in SIDES:
+                    act(V("junk", j, j + n), run, AF.Relu, scale=-2.0 if w else 2.0, acc=col("acc", 2 * k + w))
+                else:
+                    act(V("junk", j, j + n), run, AF.Abs if w else AF.Identity, acc=col("acc", 5 * w + k))
+                    red(col("acc", 5 * w + k), run, sizes=bool(w))
+                    either()
                 j += n
-        tt(V("acci", 0, 10, 2), V("acc", 5, 10), V("acc", 0, 5), A.add)
-        tt(V("acci", 1, 10, 2), V("acc", 5, 10), V("acc", 0, 5), A.subtract)
+        if t in SIDES:
+            cp(V("acci"), V("acc"))
+        else:
+            tt(V("acci", 0, 10, 2), V("acc", 5, 10), V("acc", 0, 5), A.add)
+            tt(V("acci", 1, 10, 2), V("acc", 5, 10), V("acc", 0, 5), A.subtract)
         ts(V("un", 0, 30, 3), V("acci"), 255, None, A.bitwise_and)
         ts(V("un", 1, 30, 3), V("acci"), 8, 255, A.logical_shift_right, A.bitwise_and)
         ts(V("un", 2, 30, 3), V("acci"), 16, None, A.logical_shift_right)
@@ -426,13 +476,16 @@ def build(g, core, T, topo):
         tt(V("pr", 0, 144), PS(BANK_S, 0, 144), SQ(0, 144), A.mult)
         tt(V("pr", 144, 216), V("bs"), PS(BANK_S, 72, 144), A.subtract)
         tt(V("pr", 24, 48), V("pr", 24, 48), V("pr", 48, 72), A.max)
-        ts(V("doff", 72, 144), V("pr", 144, 216), 128.0, R12, A.mult, A.add)
+        ts(V("doff", 72, 144), V("pr", 144, 216), DROP, R12, A.mult, A.add)
         tt(V("pr", 96, 144), V("pr", 96, 144), V("pr", 0, 48), A.max)
-        ts(V("doff", 0, 72), V("pr", 72, 144), F4D, R12, A.mult, A.add)
-        act(V("junk", j, j + P), (V("tab"), n16), AF.Sign, bias=TH, acc=col("ga", 0))
-        ops[-1]["arr"] = came
+        ts(V("doff", 0, 72), V("pr", 72, 144), 0.25 / UNIT, R12, A.mult, A.add)
         line(V("nr"), (V("tab"), n16), 2.0, -34.0)
         ops[-1]["arr"] = came
+        if t in AFTER:
+            act(V("junk", j, j + P), V("nr"), AF.Sign, scale=0.5, bias=TH2, acc=col("ga", 0))
+        else:
+            act(V("junk", j, j + P), (V("tab"), n16), AF.Sign, bias=TH, acc=col("ga", 0))
+            ops[-1]["arr"] = came
         act(V("g32"), V("m32"), AF.Sign, bias=col("ga", 0))
         turn(V("g32t"), V("g32"))
         act(V("g32"), V("g32t"), AF.Identity, acc=col("ga", 1))
@@ -448,18 +501,24 @@ def build(g, core, T, topo):
             scan(V("cap", 1, 289, -1), V("gt", 0, P, -1), V("gt", 0, P, -1), 0.0, A.add, A.min)
         scan(V("cum"), V("ge"), V("cap", 2, 290), -192.0, A.add, A.min)
         na = 6 - LIST_V[t]
-        for c in range(6):
-            jk = V("jw", P * c, P * c + P)
-            if c < na:
-                act(jk, V("cum"), AF.Sign, scale=-1.0, bias=col("sb", c), acc=col("wl", c))
+        runs = ((0, 3), (3, 6)) if na == 6 and t in LEANING else ((0, na), (na, 6)) if na < 6 else ((0, 6),)
+        for c0, c1 in runs:
+            more = max(range(-80, 81, 16), key=lambda m: min([min(16 * c - m, 80 - 16 * c) >= 0 and min(16 * c, 80 - 16 * c + m) >= 0 for c in range(c0, c1)])
+                       * (1 + sum([2 * min(16 * c, 80 - 16 * c + m) - m for c in range(c0, c1)])))
+            cut = {c: min(16 * c, 80 - 16 * c + more) for c in range(c0, c1)}
+            for c in range(c0, c1):
+                jk, cum = V("jw", P * c + 2 * cut[c] - more, P * c + P), V("cum", cut[c], P - cut[c] + more)
+                if c < na:
+                    act(jk, cum, AF.Sign, scale=-1.0, bias=col("sb", c), acc=col("wl", c))
+                else:
+                    ts(jk, cum, col("sb", c), -0.5, A.is_lt, A.add)
+            if c0 < na:
+                ts(V("wl16", c0, c1), V("wl", c0, c1), 0.5, 144.0 + more / 2, A.mult, A.add)
             else:
-                ts(jk, V("cum"), col("sb", c), -0.5, A.is_lt, A.add)
-        for c in range(na, 6):
-            scan(V("jx", P * c, P * c + P), V("one"), V("jw", P * c, P * c + P))
-        if na < 6:
-            ts(V("wl16", na, 6), V("jx", P * na + P - 1, 6 * P, P), 144.0, None, A.add)
-        if na:
-            ts(V("wl16", 0, na), V("wl", 0, na), 0.5, 144.0, A.mult, A.add)
+                for c in range(c0, c1):
+                    lo = 2 * cut[c] - more
+                    scan(V("jx", P * c + lo, P * c + P), V("one", lo), V("jw", P * c + lo, P * c + P))
+                ts(V("wl16", c0, c1), V("jx", P * c0 + P - 1, P * c1, P), 144.0 + more / 2, None, A.add)
         tt(V("kk"), (V("nr"), V("wl16")), V("jq"), A.subtract)
         move(V("wr"), (V("tab"), V("wl16")))
         scan(V("ks"), SEL16, V("kk"), op1=A.max)
@@ -491,7 +550,13 @@ def build(g, core, T, topo):
         for c in range(0, 72, n):
             lo, hi = 16 * c, 16 * (c + n)
             move(V("xa", lo, hi), (win, V("aoff", c, c + n)))
-            tt(V("mx", lo, hi), (V(x), V("doff", 72 + c, 72 + c + n)), V("xa", lo, hi), A.max)
+            if PICK0 and c < 24:
+                tt(V(x, XM + lo, XM + hi), (win, V("boff", c, c + n)), V("xa", lo, hi), A.max)
+                move(V(x, lo, hi), V("xa", lo, hi), 2.0)
+                if c + n == 24:
+                    move(V("mt", 0, hi), (V(x), V("doff", 72, 96)))
+                continue
+            tt(V("mx", lo, hi), (V(x, XB, XM), V("doff", 72 + c, 72 + c + n)), V("xa", lo, hi), A.max)
             if (t, c // 24) in M_DMA:
                 move(V("mt", lo, hi), (win, V("doff", c, c + n)))
                 add("g", 700, [V("mx", lo, hi), V("mt", lo, hi), V("vb")], [V("mt", lo, hi)],
@@ -517,7 +582,7 @@ def build(g, core, T, topo):
                 else:
                     tt(new, V("rr", l2, l2 + 384), old, A.add)
         if t == R - 1:
-            line(V("dv"), V("pr", 72, 168), F4E, -1.0)
+            line(V("dv"), V("pr", 72, 168), 0.0625 / UNIT, -1.0)
             turn(V("dw"), V("dv"))
             move(V("dr"), V("dw", 0, 96, 4))
             for gr in range(8):
@@ -525,14 +590,14 @@ def build(g, core, T, topo):
                     c0 = 8 * k + 4 * (gr % 2)
                     dma("s", T.od[gr, 128 * k:128 * k + 4 * n], T.dr[32 * (gr // 2):32 * (gr // 2) + n, c0:c0 + 4], [V("dr")], [], 2000)
                     ops[-1]["sem"] = "od"
-            quant(V("oq", 128, 384), V("op", 128, 384), V(xn, X0 + 512))
+            quant(V("oq", 128, 384), V("op", 128, 384), V(xn, X0 + 512, XM))
             dma("s", T.oc[:, 512:], T.oq[:, 128:384].bitcast(dt.uint8), [V("oq", 128, 384)], [], 2400)
             mm(PS(BANK_S, 0, 256), V("vq"), V("vs"), V("oq", 128, 384), V("op", 128, 384))
             move(V("yo", 128, 384), PS(BANK_S, 0, 256))
             dma("s", T.y[:, 128:], T.yo[:, 128:], [V("yo", 128, 384)], [], 2400)
         for b in range(4):
             bank, n = BANK_D + b % 2, 128 if home else P
-            mm(PS(bank, 0, n), V("eqq", 128 * b, 128 * b + 128), V("es", 128 * b, 128 * b + 128), V(lq, 0, n), V(ls, 0, n), arr=("aq%d" % t, 2))
+            mm(PS(bank, 0, n), V("eqq", 128 * b, 128 * b + 128), V("es", 128 * b, 128 * b + 128), V(lq, 0, n), V(ls, 0, n), arr=("aq%d" % t, sent.count("aq%d" % t) * 2))
             if home:
                 tt(V(xn, X0 + b, X0 + 4 * E, 4), PS(bank, 0, E), V(x, X0 + b, X0 + 4 * E, 4), A.max)
             else:
@@ -613,69 +678,142 @@ def deal(ops, key, way, back, lean):
     return max(fin), at, w
 
 
-def polish(ops, start, rng):
+def polish(ops, sets, start, rng):
     n = len(ops)
-    near, behind = [o["near"] for o in ops], [o["behind"] for o in ops]
-    tail = [HOP + o["lat"] for o in ops]
-    ways = [[("vatgs".index(w[0]), w[1]) for w in o["ways"]] for o in ops]
+    near, nex, behind = [o["near"] for o in ops], [o["next"] for o in ops], [o["behind"] for o in ops]
+    tails = [[rough[3] + o["lat"] for o in each] for rough, each in zip(ROUGH, sets)]
+    costs = [[[("vatgs".index(w[0]), w[1]) for w in o["ways"]] for o in each] for each in sets]
+    ways = costs[0]
     seq, way = sorted(range(n), key=lambda k: (start[1][k], k)), list(start[2])
 
-    def run(seq, way, lo, at, fin, by, was):
-        free, last = list(was[lo][0]), list(was[lo][1])
-        for i in range(lo, n):
-            k = seq[i]
-            was[i] = (tuple(free), tuple(last))
-            q, c = ways[k][way[k]]
-            t, b = free[q], last[q]
-            for j in near[k]:
-                if fin[j] > t:
-                    t, b = fin[j], j
-            at[k], by[k], free[q], last[q], fin[k] = t, b, t + c, ~k, t + c + tail[k]
-        return max(fin)
+    def run(seq, way, lo, hi, old):
+        new, before, after = [], [None] * 5, [None] * 5
+        for k in seq[:lo]:
+            before[ways[k][way[k]][0]] = ~k
+        for k in seq[:hi - 1:-1]:
+            after[ways[k][way[k]][0]] = k
+        for cost, tail, (fin, by, left) in zip(costs, tails, old):
+            fin, by, left, last = fin[:], by[:], left[:], before[:]
+            free = [0.0 if b is None else fin[~b] - tail[~b] for b in before]
+            for k in seq[lo:]:
+                q, c = cost[k][way[k]]
+                t, b = free[q], last[q]
+                for j in near[k]:
+                    if fin[j] > t:
+                        t, b = fin[j], j
+                t += c
+                by[k] = b
+                free[q] = t
+                last[q] = ~k
+                fin[k] = t + tail[k]
+            free = [0.0 if a is None else left[a] for a in after]
+            for k in seq[hi - 1::-1]:
+                q, c = cost[k][way[k]]
+                t = 0.0
+                for j in nex[k]:
+                    if left[j] > t:
+                        t = left[j]
+                t += tail[k]
+                if free[q] > t:
+                    t = free[q]
+                left[k] = free[q] = t + c
+            new.append((fin, by, left))
+        return new, [max(e[0]) for e in new]
 
-    at, fin, by, was = [0.0] * n, [0.0] * n, [None] * n, [((0.0,) * 5, (None,) * 5)] * n
-    now = run(seq, way, 0, at, fin, by, was)
-    best, held = (now, list(at), list(way)), None
+    def least(seg, way, lo, hi, used):
+        before, after, out = {}, {}, 0.0
+        for q in used:
+            i = lo - 1
+            while i >= 0 and qs[i] != q:
+                i -= 1
+            before[q] = seq[i] if i >= 0 else None
+            i = hi
+            while i < n and qs[i] != q:
+                i += 1
+            after[q] = seq[i] if i < n else None
+        for cost, tail, (fin, by, left), s in zip(costs, tails, state, share):
+            free = {q: 0.0 if b is None else fin[b] - tail[b] for q, b in before.items()}
+            mine, end = {}, 0.0
+            for k in seg:
+                q, c = cost[k][way[k]]
+                t = free[q]
+                for j in near[k]:
+                    f = mine.get(j) or fin[j]
+                    if f > t:
+                        t = f
+                free[q] = t = t + c
+                mine[k] = t = t + tail[k]
+                if t > end:
+                    end = t
+                for j in nex[k]:
+                    if pos[j] >= hi and t + left[j] > end:
+                        end = t + left[j]
+            for q, a in after.items():
+                if a is not None and free[q] + left[a] > end:
+                    end = free[q] + left[a]
+            out += end * s
+        return out
+
+    state, ends = run(seq, way, 0, n, [([0.0] * n, [None] * n, [0.0] * n) for each in sets])
+    pos, qs = [0] * n, [0] * n
+    share = [ends[0] / e / len(ends) for e in ends]
+    now = sum([e * s for e, s in zip(ends, share)])
+    best, held = (now, seq, way, state, ends), None
     for it in range(SWAPS):
         if held is None:
-            k, held, two = fin.index(now), [], []
-            while by[k] is not None:
-                if len(ways[k]) > 1:
-                    two.append(k)
-                if by[k] < 0:
-                    held.append((k, ~by[k]))
-                k = ~by[k] if by[k] < 0 else by[k]
-            pos = {k: i for i, k in enumerate(seq)}
-        r = rng.random(5).tolist()
-        s2, w2 = seq, way
-        if r[0] < 0.15 and two:
+            held, two = [], []
+            for (fin, by, left), end in zip(state, ends):
+                k = fin.index(end)
+                while by[k] is not None:
+                    if len(ways[k]) > 1:
+                        two.append(k)
+                    if by[k] < 0:
+                        held.append((k, ~by[k]))
+                    k = ~by[k] if by[k] < 0 else by[k]
+            for i, k in enumerate(seq):
+                pos[k], qs[i] = i, ways[k][way[k]][0]
+        if it % 1000 == 0:
+            draws = rng.random((1000, 5)).tolist()
+        r = draws[it % 1000]
+        w2 = way
+        if r[0] < 0.2 and two:
             k = two[int(r[1] * len(two))]
-            w2 = list(way)
-            w2[k], lo = 1 - w2[k], pos[k]
+            w2 = way[:]
+            w2[k] = (w2[k] + 1 + int(r[2] * (len(ways[k]) - 1))) % len(ways[k])
+            lo, hi, seg = pos[k], pos[k] + 1, [k]
+            used = (qs[lo], ways[k][w2[k]][0])
         else:
             v, u = held[int(r[1] * len(held))]
             if behind[v] >> u & 1:
                 continue
             if r[2] < 0.5:
-                lo, hi = pos[u], min(n, pos[v] + 1 + int(12 * r[3] * r[3]))
-                late = [k == u or behind[k] >> u & 1 for k in seq[lo:hi]]
+                lo, hi = pos[u], min(n, pos[v] + 1 + int(25 * r[3] * r[3]))
+                seg = seq[lo:hi]
+                seg = [k for k in seg if k != u and not behind[k] >> u & 1] + [k for k in seg if k == u or behind[k] >> u & 1]
             else:
-                lo, hi = max(0, pos[u] - int(12 * r[3] * r[3])), pos[v] + 1
-                late = [not (k == v or behind[v] >> k & 1) for k in seq[lo:hi]]
-            s2 = seq[:lo] + [k for k, e in zip(seq[lo:hi], late) if not e] + [k for k, e in zip(seq[lo:hi], late) if e] + seq[hi:]
-        a2, f2, b2, was2 = list(at), list(fin), list(by), list(was)
-        got = run(s2, w2, lo, a2, f2, b2, was2)
-        if got <= now - WARM * (1.0 - it / SWAPS) * math.log(1.0 - r[4]):
-            now, seq, way, at, fin, by, was, held = got, s2, w2, a2, f2, b2, was2, None
+                lo, hi = max(0, pos[u] - int(25 * r[3] * r[3])), pos[v] + 1
+                seg, bv = seq[lo:hi], behind[v] | 1 << v
+                seg = [k for k in seg if bv >> k & 1] + [k for k in seg if not bv >> k & 1]
+            used = sorted(set(qs[lo:hi]))
+        most = now - WARM * (1.0 - it / SWAPS) * math.log(1.0 - r[4])
+        if least(seg, w2, lo, hi, used) > most:
+            continue
+        s2 = seq[:lo] + seg + seq[hi:]
+        st2, e2 = run(s2, w2, lo, hi, state)
+        got = sum([e * s for e, s in zip(e2, share)])
+        if got <= most:
+            now, seq, way, state, ends, held = got, s2, w2, st2, e2, None
             if got < best[0]:
-                best = (got, list(at), list(way))
-    return best
+                best = (got, seq, way, state, ends)
+    now, seq, way, state, ends = best
+    return ends, [state[0][0][k] - tails[0][k] - ways[k][way[k]][1] for k in range(n)], way, seq
 
 
 KEPT = {}
 
 
-def order(ops):
+def order(sets):
+    ops = sets[0]
     link(ops)
     n = len(ops)
     if "best" not in KEPT:
@@ -708,26 +846,28 @@ def order(ops):
                 now, lean = got, le
             if got[0] < best[0]:
                 best = got
-        KEPT["best"] = polish(ops, best, rng)
-    end, at, way = KEPT["best"]
+        KEPT["best"] = polish(ops, sets, best, rng)
+    end, at, way, seq = KEPT["best"]
     for k, o in enumerate(ops):
         o["at"] = at[k]
         o["q"], o["cost"], o["fn"] = o["ways"][way[k]]
-    return sorted(range(n), key=lambda k: (at[k], k))
+    return seq
 
 
 def rank_program(g, core, T, topo):
     if T.rank_of(core) is None:
         return
-    ops = build(g, core, T, topo)
-    seq = order(ops)
+    sets = [build(g, core, T, topo, rough) for rough in ROUGH]
+    ops, seq = sets[0], order(sets)
     prev = T.cores[(T.rank_of(core) - 1) % len(T.cores)]
     nxt = T.cores[(T.rank_of(core) + 1) % len(T.cores)]
     eng = {"v": g.vector, "a": g.scalar, "t": g.tensor, "g": g, "s": g.sync}
-    total = {"left": 0}
+    total, done = {"left": 0}, {}
     know = {q: {} for q in eng}
     for k in seq:
         o = ops[k]
+        if o["fn"] is None:
+            continue
         q, mine = o["q"], know[o["q"]]
         need = {}
         for j in o["deps"]:
@@ -738,6 +878,9 @@ def rank_program(g, core, T, topo):
                 need[s] = (val, j)
         for s, (val, j) in sorted(need.items(), key=lambda e: -ops[e[1][1]]["at"]):
             if mine.get(s, 0) < val:
+                for i in done.get(s, [])[val:]:
+                    if ops[i]["at"] + ops[i]["cost"] + HOP + (0.0 if s == "s" + q else LONG) <= o["at"]:
+                        val, j = ops[i]["tok"][1], i
                 eng[q].wait_ge(T.sem[s], val)
                 for s2, v2 in ops[j]["clock"].items():
                     mine[s2] = max(mine.get(s2, 0), v2)
@@ -755,6 +898,7 @@ def rank_program(g, core, T, topo):
             s, inc = o.get("sem", "d%d" % len([1 for e in total if e[0] == "d"])), 16
         else:
             s, inc = "s" + q, 1
+            done.setdefault(s, []).append(k)
         total[s] = total.get(s, 0) + inc
         ins.then_inc(T.sem[s], inc)
         o["tok"] = (s, total[s])

import math
import numpy as np
from concourse.mybir import dt, AluOpType as A, AxisListType as AX, ActivationFunctionType as AF

C, E, B, P, R = 384, 96, 96, 288, 3
XB, X0, XM = 4 * B, 4 * B + 32, 4 * B + 32 + 4 * C
DROP = XM / 16
PICK0 = True
UNIT = 2048.0
BIG = 1e29
LIFT = 2.0 ** 51
BY_DMA = ((0, 0), (0, 1), (1, 0), (2, 0), (2, 1))
BY_ROW = ((0, 2), (1, 2), (2, 2))
HALVES = ()
M_DMA = ()
AT_HOME = ()
COUNTS = (2,)
LIST_V = (0, 0, 2)
PLACE_V = (1, 1, 3)
EQ_RUNS = ((0, 1), (1, 3))
GT_A = ()
SIDES = ()
AFTER = ()
SEL4 = 96
LEANING = (0, 1)
SPLIT = (0,)
WHOLE_X = (0,)
WHOLE_M = ()
TRIES, SEED, TEMP = 300, 1, 100.0
SWAPS = 300000
WARM = 70.0
F32, BF, I32, U16, QC, U8 = "float32", "bfloat16", "int32", "uint16", "float8_e4m3fn_x4", "uint8"
W0, T0, B0, A0, A1, L0, Z1, W1, T1, T2, FW = 16, 112, 208, 304, 400, 496, 784, 896, 992, 1088, 1184


def _sb(n, d):
    return ("sbuf", [128, n], d)


SCRATCH = {
    "ub": _sb(512, BF), "vb": _sb(512, BF), "uq": _sb(128, QC), "us": _sb(128, U8), "vq": _sb(128, QC), "vs": _sb(128, U8),
    "ut": _sb(384, QC), "ust": _sb(384, U8), "ui": _sb(24, I32), "ul": _sb(24, U16),
    "wq": _sb(512, QC), "wp": _sb(512, U8), "oq": _sb(384, QC), "op": _sb(384, U8),
    "ab": _sb(36, I32), "ab16": _sb(36, U16), "lt2": _sb(6, U16), "lb": _sb(18, U16), "db": _sb(18, F32), "lbf": _sb(18, F32),
    "e16": _sb(18, F32), "el": _sb(18, U16), "zb": _sb(8, F32), "one": _sb(288, BF),
    "tab": _sb(296, F32), "pix": _sb(5, I32), "pc": _sb(6, I32), "pf": _sb(24, F32),
    "j16": _sb(16, F32), "p16": _sb(48, F32), "il": _sb(18, U16), "j2": _sb(32, F32), "p4": _sb(12, F32), "sel4": _sb(288, BF), "sel16": _sb(288, BF),
    "m16": _sb(16, F32), "m32": _sb(32, F32), "sb": _sb(6, F32), "jq": _sb(96, F32),
    "wt": _sb(480, F32), "a4": _sb(144, I32), "sr": _sb(288, F32), "wt1": _sb(288, F32), "eq": _sb(288, BF), "eqs": _sb(288, BF), "eqb": _sb(288, F32), "sq": _sb(216, F32),
    "bs": _sb(72, F32), "aoff": _sb(72, U16), "boff": _sb(24, U16), "bm": _sb(256, BF),
    "cqb": _sb(512, BF), "cq": _sb(128, QC), "cs": _sb(128, U8), "eb": _sb(2048, BF), "eqq": _sb(512, QC), "es": _sb(512, U8),
    "fw": _sb(FW, BF), "t2": _sb(288, BF), "fq": _sb(144, QC), "fs": _sb(144, U8),
    "pr": _sb(216, F32), "doff": _sb(144, U16),
    "junk": _sb(1152 + 320, BF), "jw": _sb(6 * 288, BF), "jx": _sb(6 * 288, BF), "jr": _sb(6 * 96, BF), "js": _sb(6 * 96, BF),
    "acc": _sb(10, F32), "acci": _sb(10, I32),
    "un": _sb(30, I32), "n16": _sb(18, U16), "nr": _sb(288, BF), "ga": _sb(4, F32), "g32": _sb(32, F32), "g32t": _sb(32, F32),
    "gt": _sb(288, BF), "ge": _sb(288, BF), "cap": _sb(290, BF), "cum": _sb(288, BF), "wl": _sb(6, F32), "wl16": _sb(6, U16),
    "wr": _sb(96, F32), "kk": _sb(96, F32), "ks": _sb(96, F32), "rk": _sb(6, F32), "rk16": _sb(6, U16),
    "hr": _sb(96, F32), "hs": _sb(96, F32), "dx": _sb(4 * P, BF), "fb": _sb(512, BF),
    "xa": _sb(1152, BF), "mx": _sb(1152, BF), "mt": _sb(1152, BF), "mq8": _sb(320, QC), "ms8": _sb(320, U8), "rr": _sb(1152, F32),
    "dv": _sb(96, F32), "dw": _sb(96, F32), "dr": _sb(24, F32), "yo": _sb(384, F32),
    "ps": ("psum", [128, 4096], F32),
}
for _t in range(R + 1):
    SCRATCH["x%d" % _t] = _sb(XM + 4 * B, BF)
for _t in range(R):
    SCRATCH["xq%d" % _t] = _sb(P + 128, QC)
    SCRATCH["xs%d" % _t] = _sb(P + 128, U8)
    SCRATCH["lq%d" % _t] = _sb(P, QC)
    SCRATCH["ls%d" % _t] = _sb(P, U8)
    SCRATCH["h%d" % _t] = _sb(24, U16)
    if _t in AT_HOME:
        SCRATCH["gq%d" % _t] = _sb(128, QC)
        SCRATCH["gs%d" % _t] = _sb(128, U8)
    else:
        SCRATCH["lh%d" % _t] = _sb(18 if _t in COUNTS else 24, U16)
    if _t in COUNTS:
        SCRATCH["n%d" % _t] = _sb(18, U16)
SEMAPHORES = ["sv", "sa", "st", "sg", "left", "od", "r1", "r2"] + ["d%d" % k for k in range(48)] + ["aq%d" % t for t in range(R)] + [
    "ah%d" % t for t in range(R) if t not in AT_HOME]

PER = ("t2 fq fs pr doff junk jw jx jr js acc acci un n16 nr ga g32 g32t gt ge cap cum wl wl16 wr kk ks rk rk16 hr hs "
       "dx xa mx mt mq8 ms8 rr").split()
WIDE = {k: v[1][1] for k, v in SCRATCH.items()}
for _k in PER:
    SCRATCH[_k] = _sb(R * (-(-WIDE[_k] // 32) * 32), SCRATCH[_k][2])
NOW = [0]

ROUGH = ((1.0, 1.56, 3.8, 110.0, 0.65, 0.8, 0.9), (1.13, 1.9, 5.0, 130.0, 0.75, 0.9, 1.0))
HOP = ROUGH[0][3]
LONG = 500.0
CYC, LEAN = 0.92, 300.0
BANK_Z, BANK_S, BANK_Q, BANK_D = 0, 4, 5, 6


def V(name, lo=0, hi=None, st=1):
    o = NOW[0] * (SCRATCH[name][1][1] // R) if name in PER else 0
    return (name, o + lo, o + (WIDE[name] if hi is None else hi), st)


def PS(bank, lo, hi):
    return ("ps", 512 * bank + lo, 512 * bank + hi, 1)


def size(v):
    return len(range(v[1], v[2], abs(v[3])))


def narrow(*vs):
    return all(SCRATCH[v[0]][2] in (BF, U16) for v in vs)


def meet(a, b):
    if a[0] != b[0]:
        return False
    if a[0] == "ps":
        return a[1] // 512 == b[1] // 512
    if a[1] >= b[2] or b[1] >= a[2]:
        return False
    return not (a[3] == b[3] and a[3] > 1 and (a[1] - b[1]) % a[3] != 0)


def build(g, core, T, topo, rough=ROUGH[0]):
    ops, sent = [], []
    NOW[0] = 0
    rank = T.rank_of(core)
    nxt = T.cores[(rank + 1) % len(T.cores)]

    def ap(v):
        if isinstance(v, (int, float)):
            return v
        if len(v) == 2:
            return ap(v[0]).indirect(ap(v[1]))
        if v[3] == -1:
            return T[v[0]][:, v[2] - 1:(v[1] - 1 if v[1] else None):-1]
        return T[v[0]][:, v[1]:v[2]] if v[3] == 1 else T[v[0]][:, v[1]:v[2]:v[3]]

    def views(xs):
        out = []
        for v in xs:
            if v is None or isinstance(v, (int, float)):
                continue
            out.extend(v if len(v) == 2 else [v])
        return out

    def add(q, cost, rd, wr, fn, kind="c", lat=0.0, arr=None):
        lat *= rough[4 if kind == "r" else 5 if q == "g" else 6]
        ops.append({"ways": [(q, cost * rough[0], fn)], "rd": views(rd), "wr": views(wr), "kind": kind, "lat": lat, "arr": arr})

    def either():
        o = ops.pop()
        ops[-1]["ways"].extend(o["ways"])

    def vcost(out, first, per):
        n = size(out)
        return 50 + rough[1] * CYC * n if len(first) == 2 else 20 + CYC * max(64, n * per)

    def ts(out, in0, s1, s2, op0, op1=None):
        per = 0.5 if len(in0) != 2 and narrow(out, in0) else 1
        if op1 is None:
            fn = lambda: g.vector.tensor_scalar(ap(out), ap(in0), ap(s1), None, op0)
        else:
            fn = lambda: g.vector.tensor_scalar(ap(out), ap(in0), ap(s1), ap(s2), op0, op1)
        add("v", vcost(out, in0, per), [in0, s1, s2], [out], fn)

    def tt(out, in0, in1, op, arr=None):
        per = 1 if "ps" in (in0[0], in1[0]) else 2
        add("v", vcost(out, in0, per), [in0, in1], [out], lambda: g.vector.tensor_tensor(ap(out), ap(in0), ap(in1), op), arr=arr)

    def cp(out, in_):
        add("v", vcost(out, in_, 1), [in_], [out], lambda: g.vector.tensor_copy(ap(out), ap(in_)))

    def pick(q, s, wq, ws, off):
        add("v", vcost(q, (wq, off), 1), [wq, off], [q],
            lambda: g.vector.tensor_copy(ap(q).bitcast(dt.uint32), ap(wq).bitcast(dt.uint32).indirect(ap(off))))
        act(s, (ws, off), AF.Copy)
        cp(s, (ws, off))
        either()

    def scatter(win, off, in_):
        add("v", 50 + rough[2] * CYC * size(in_), [in_, off], [win], lambda: g.vector.tensor_copy(ap((win, off)), ap(in_)))

    def scan(out, d0, d1, init=0.0, op0=A.mult, op1=A.add):
        add("v", vcost(out, d0, 0.5 if narrow(out, d0, d1) else 1), [d0, d1, init], [out],
            lambda: g.vector.tensor_tensor_scan(ap(out), ap(d0), ap(d1), ap(init), op0, op1))

    def red(out, in_, op=A.add, sizes=False):
        add("v", vcost(in_, in_, 1), [in_], [out], lambda: g.vector.tensor_reduce(ap(out), ap(in_), AX.X, op, apply_absolute_value=sizes))

    def turn(out, in_):
        add("v", vcost(in_, in_, 1), [in_], [out], lambda: g.vector.transpose(ap(out), ap(in_)))

    def fill(out, c):
        add("v", vcost(out, out, 0.5 if narrow(out) else 1), [], [out], lambda: g.vector.memset(ap(out), c))

    def quant(q, s, in_):
        add("v", 30 + 0.27 * size(in_), [in_], [q, s], lambda: g.vector.quantize_mx(ap(q), ap(s), ap(in_)))

    def act(out, in_, f, scale=None, bias=None, acc=None):
        def fn():
            kw = {}
            if scale is not None:
                kw["scale"] = ap(scale)
            if bias is not None:
                kw["bias"] = ap(bias)
            if acc is not None:
                kw["accum_out"] = ap(acc)
            return g.scalar.activation(ap(out), ap(in_), f, **kw)
        n = size(out)
        add("a", 65 + (25 if acc else 0) + CYC * n * (rough[1] if len(in_) == 2 else 1), [in_, scale, bias], [out, acc], fn)

    def move(out, in_, scale=None):
        act(out, in_, AF.Copy, scale=scale)
        if scale is None:
            cp(out, in_)
        else:
            ts(out, in_, scale, None, A.mult)
        either()

    def blank(out, c=0.0):
        act(out, V("one", 0, size(out)), AF.Copy, scale=c)
        fill(out, c)
        either()
        if c == 0.0 and out[3] == 1:
            iota(out, [[0, size(out)]], 0, 0)
            either()

    def line(out, in_, scale, bias):
        act(out, in_, AF.Identity, scale=scale, bias=bias)
        ts(out, in_, scale, bias, A.mult, A.add)
        either()

    def relu(out, in_, scale):
        act(out, in_, AF.Relu, scale=scale)
        ts(out, in_, 0.0, scale, A.max, A.mult)
        either()

    def mm(out, lq, ls, rq, rs, arr=None):
        add("t", 60 + 0.9 * (size(out) + 16), [lq, ls, rq, rs], [out],
            lambda: g.tensor.matmul_mx(ap(out), ap(lq), ap(ls), ap(rq), ap(rs), True, True), arr=arr)

    def iota(out, pat, base, cm):
        if SCRATCH[out[0]][2] == I32:
            fn = lambda: g.iota(ap(out), pat, base, cm)
        else:
            fn = lambda: g.iota(ap(out), pat, base, cm, allow_small_or_imprecise_dtypes=True)
        add("g", 140 + 2 * CYC * size(out), [], [out], fn)

    def sel(out, in_, pat, op, base, cm):
        add("g", 180 + 2 * CYC * size(out), [in_], [out], lambda: g.affine_select(ap(out), ap(in_), pat, op, 0.0, base, cm))

    def dma(q, out, in_, rd, wr, lat):
        eng = g.sync if q == "s" else g.scalar
        add(q, 60, rd, wr, lambda: eng.dma_start(out, in_), kind="d", lat=lat)

    def send(pairs, sem, rd, wr, lat):
        def fn():
            rid, pid = topo.addr(nxt)[0:2]
            for dst, src in pairs:
                g.remote_dma(dst, src, T.sem[sem], T.sem.left, pid, rid, topo.mask(core, nxt))
        first = ("first", 0, 1, 1)
        if sent:
            add("g", 300 * len(pairs), rd + [first], wr, fn, kind="r", lat=lat)
            ops[-1]["calls"] = len(pairs)
        else:
            add("g", 300 * len(pairs) + 2500, rd, [first], fn, kind="r")
            ops[-1]["calls"] = len(pairs)
            add("s", 0, [first], wr, None, kind="r", lat=lat)
        sent.append(sem)

    def col(name, k):
        return V(name, k, k + 1)

    def fw(lo, n=B):
        return V("fw", lo, lo + n)

    dma("s", T.ab[:, 0:18], T.pa[:], [], [V("ab", 0, 18)], 1900)
    dma("a", T.ab[:, 18:36], T.pb[:], [], [V("ab", 18, 36)], 1900)
    dma("a", T.ub[:], T.u[:], [], [V("ub")], 2400)
    dma("s", T.x0[:, X0 + 4 * E:X0 + 4 * P], T.x[:, 4 * E:4 * P], [], [V("x0", X0 + 4 * E, X0 + 4 * P)], 2900)
    dma("s", T.x0[:, X0 + 4 * P:XM], T.x[:, 4 * P:], [], [V("x0", X0 + 4 * P, XM)], 3200)
    dma("s", T.x0[:, X0:X0 + 4 * E], T.x[:, 0:4 * E], [], [V("x0", X0, X0 + 4 * E)], 3600)
    for k, src in enumerate((T.pa, T.pb)):
        for s in range(4):
            dma("s", T.a4[4 * s:128:16, 72 * k:72 * k + 72], src[s:128:4, :], [], [("rows", 4 * k + s, 4 * k + s + 1, 1)], 2200)
            ops[-1]["sem"] = "r1"
    for s in range(1, 4):
        dma("s", T.a4[s:128:4, :], T.a4[0:128:4, :], [("rows", 0, 8, 1)], [("rows", 8 + s, 9 + s, 1)], 2000)
        ops[-1]["sem"] = "r2"
    dma("s", T.wq[:].bitcast(dt.uint8), T.wc[:], [V("ab")], [V("wq")], 2500)
    dma("s", T.wp[:], T.ws[:], [V("ab")], [V("wp")], 2700)

    iota(V("pix"), [[1, 5]], 0, 1)
    iota(V("j16"), [[1, 16]], 0, 0)
    iota(V("tab"), [[1, 296]], 1, 0)
    iota(V("ui"), [[1, R], [16, 8]], 0, 0)
    iota(V("j2"), [[1, 2], [0, 16]], 0, 0)
    fill(V("one"), 1.0)
    blank(fw(0, W0))
    blank(fw(Z1, W1 - Z1))
    blank(V("wt1", 0, 96))
    blank(V("zb", 0, 1))
    blank(V("zb", 1, 8), BIG)
    blank(V("x0", XB, XB + 16), -BIG)
    blank(V("x0", XB + 16, X0))
    for t in range(1, R):
        dma("s", T["x%d" % t][:, XB:X0], T.x0[:, XB:X0], [V("x0", XB, X0)], [V("x%d" % t, XB, X0)], 2000)
    blank(V("cap", 289, SCRATCH["cap"][1][1], SCRATCH["cap"][1][1] // R))
    if AT_HOME:
        blank(V("fb", 4 * E))
    sel(V("bm", 0, 128), V("one", 0, 128), [[-16, 8], [0, 16]], A.is_ge, 0, 1)
    sel(V("bm", 128, 256), V("bm", 0, 128), [[16, 8], [0, 16]], A.is_ge, 15, -1)
    for e in range(4):
        sel(V("cqb", e, 512, 4), V("bm", 128, 256), [[0, 8], [1, 4], [0, 4]], A.is_equal, -e, 0)
    quant(V("cq"), V("cs"), V("cqb"))
    for b in range(4):
        for lo in (0, 256):
            sel(V("eb", 512 * b + lo, 512 * b + lo + 256), V("one", 0, 256), [[1, 256]], A.is_equal, lo - b, -4)
    quant(V("eqq"), V("es"), V("eb"))
    ts(V("pc", 0, 2), V("pix", 0, 5, 4), 2, 3, A.logical_shift_right, A.bitwise_and)
    ts(V("pc", 2, 4), V("pix", 0, 2), 15, None, A.bitwise_and)
    ts(col("pc", 4), col("pix", 0), 3, None, A.bitwise_and)
    ts(col("pc", 5), col("pix", 0), 4, 1, A.logical_shift_right, A.bitwise_and)
    cp(V("pf", 0, 6), V("pc"))
    S_, S1, I0, I1, R_, H_, R12, RM4, TH, I2, F4, F4H, SB0, F16, K0, K16, NK16, TH2 = [col("pf", k) for k in range(18)]
    line(R12, R_, 1.0, 12.0)
    line(RM4, R_, 1.0, -4.0)
    if len(AFTER) < R:
        line(TH, I0, -1.0, -1.5)
    if AFTER:
        line(TH2, I0, -1.0, 15.5)
    line(I2, I0, 2.0, -223.0)
    ts(F4, S_, 3.0, 1.0 / LIFT, A.is_equal, A.max)
    move(F4H, F4, 4.0)
    ts(F16, I0, 15.0, 1.0 / LIFT, A.is_equal, A.max)
    ts(K0, I0, 15.0, LIFT, A.not_equal, A.mult)
    ts(K16, K0, 1.0, None, A.max)
    move(NK16, K16, -1.0)
    ts(V("m16"), V("j16", 0, 16), I0, None, A.is_equal)
    ts(V("p4", 0, 4), V("j16", 0, 4), S_, None, A.not_equal)
    ts(V("p4", 4, 8), V("j16", 0, 4), S1, LIFT, A.is_equal, A.mult)
    tt(V("p4", 8, 12), V("p4", 0, 4), V("p4", 4, 8), A.max)
    for s in range(4):
        move(V("sel4", s, SEL4, 4), V("one", 0, SEL4 // 4), col("p4", 8 + s))
    ts(V("p16", 16, 32), V("j16"), I0, None, A.not_equal)
    ts(V("p16", 32, 48), V("j16"), I1, LIFT, A.is_equal, A.mult)
    tt(V("p16", 0, 16), V("p16", 16, 32), V("p16", 32, 48), A.max)
    ts(V("il"), V("one", 0, 18), I0, None, A.mult)
    n = max([hi - lo for lo, hi in EQ_RUNS])
    move(V("sel16", 0, B * n), (V("p16", 0, 16), V("il", 0, 6 * n)))
    SEL16 = V("sel16", 0, 96)
    ts(V("j2"), V("j2"), H_, None, A.is_equal)
    line(V("m32"), V("j2"), 1440.0, -1343.0)
    line(V("sb"), V("tab", 0, 6), 32.0, I2)
    line(V("jq"), V("tab", 0, 96), 1.0 / 128, -34.0)
    for k in range(6):
        w = (0.5 if k < 3 else -0.5) * 256.0 ** (k % 3)
        move(fw(W0 + 16 * k, 16), V("m16"), w)
        for name, lo in (("wt", 16 * k), ("wt1", B + 16 * k)):
            move(V(name, lo, lo + 16), V("tab", lo, lo + 16), 16 * UNIT / w)
            if k % 3:
                iota(V(name, lo, lo + 16), [[int(16 * UNIT / w), 16]], int(16 * UNIT / w) * (lo + 1), 0)
                either()
    move(fw(W1), fw(W0))
    cp(V("ul"), V("ui"))
    quant(V("uq"), V("us"), V("ub"))
    pick(V("ut", 0, 128), V("ust", 0, 128), V("uq"), V("us"), V("ul", 0, 8))
    pick(V("ut", 128, 384), V("ust", 128, 384), V("uq"), V("us"), V("ul", 8, 24))
    add("g", 2000, [V("cqb", 0, 512)], [V("vb")], lambda: g.dma_start(T.vb[:], T.v[:]), kind="d", lat=2500)
    quant(V("vq"), V("vs"), V("vb"))

    cp(V("ab16"), V("ab"))
    pa = [V("ab16", 6 * k, 6 * k + 6) for k in range(3)]
    pb = [V("ab16", 18 + 6 * k, 24 + 6 * k) for k in range(3)]
    tt(V("e16"), V("ab", 0, 18), V("ab", 18, 36), A.is_equal)
    cp(V("el"), V("e16"))
    move(V("eqb", 0, 192), (V("zb"), V("el", 0, 12)))
    move(V("eqb", 192, 288), (V("zb"), V("el", 12, 18)))
    ts(V("lt2"), V("ab", 12, 18), -96.0, None, A.add)
    ts(V("db", 0, 12), V("ab", 24, 36), float(W0), F16, A.add, A.mult)
    ts(V("db", 12, 18), V("ab", 30, 36), float(W0), F16, A.add, A.mult)
    move(V("wt", 96, 192), (V("wt", 0, 96), pa[0]))
    move(V("wt", 192, 288), (V("wt", 0, 192), pa[1]))
    move(V("wt", 288, 384), (V("wt", 0, 288), pa[2]))
    move(V("wt1", 192, 288), (V("wt1", 0, 192), pa[1]))
    move(V("wt", 384, 480), (V("wt1"), pa[2]))
    for k, (win, lst) in enumerate(((V("wt", 0, 192), pb[1]), (V("wt", 0, 288), pb[2]), (V("wt1"), pb[2]))):
        tt(V("eq", B * k, B * k + B), (win, lst), V("wt", 192 + B * k, 288 + B * k), A.is_equal)
    for lo, hi in EQ_RUNS:
        scan(V("eqs", B * lo, B * hi), V("sel16", 0, B * (hi - lo)), V("eq", B * lo, B * hi), op1=A.max)
        tt(V("lbf", 6 * lo, 6 * hi), V("eqs", B * lo + 15, B * hi, 16), V("db", 6 * lo, 6 * hi), A.mult)
        cp(V("lb", 6 * lo, 6 * hi), V("lbf", 6 * lo, 6 * hi))
    for lo in range(0, P, SEL4):
        scan(V("sr", lo, lo + SEL4), V("sel4", 0, SEL4), V("wt", 192 + lo, 192 + lo + SEL4))
    move(V("sq", 0, 72), V("sr", 3, P, 4), F4)
    for k in range(2):
        for m in range(4):
            ts(V("sq", 72 * k + 72 + m, 72 * k + 144, 4), V("a4", 72 * k + 18 * m, 72 * k + 18 * m + 18), 1.0, UNIT, A.add, A.mult)
            ops[-1]["rd"].append(("rows", 0, 12, 1))

    def SQ(lo, hi):
        return V("sq", lo, hi)
    ts(V("aoff"), SQ(72, 144), 4.0 / UNIT, R12, A.mult, A.add)
    if PICK0:
        ts(V("boff"), SQ(144, 168), 4.0 / UNIT, R12, A.mult, A.add)
        line(SB0, S_, 4.0 / DROP, (XM - 28.0) / DROP)
        line(V("bs", 0, 24), V("tab", 0, 24), 16.0 / DROP, SB0)
        line(V("bs", 24, 72), SQ(168, 216), 4.0 / UNIT / DROP, 16.0 / DROP)
    else:
        line(V("bs"), SQ(144, 216), 4.0 / UNIT / DROP, 16.0 / DROP)

    for t in range(R):
        NOW[0] = t
        x, xn = "x%d" % t, "x%d" % (t + 1)
        xq, xs, lq, ls, hh, lh = ["%s%d" % (s, t) for s in ("xq", "xs", "lq", "ls", "h", "lh")]
        win = V(x, XB + 16, XM)
        home = t in AT_HOME
        ut, ust = V("ut", 128 * t, 128 * t + 128), V("ust", 128 * t, 128 * t + 128)
        if t in WHOLE_X:
            quant(V(xq, E, C), V(xs, E, C), V(x, X0 + 4 * E, XM))
            mm(PS(BANK_S, 0, P), ut, ust, V(xq, E, C), V(xs, E, C))
            last = PS(BANK_S, 192, P)
        else:
            quant(V(xq, E, P), V(xs, E, P), V(x, X0 + 4 * E, X0 + 4 * P))
            mm(PS(BANK_S, 0, 192), ut, ust, V(xq, E, P), V(xs, E, P))
            quant(V(xq, P, P + 128), V(xs, P, P + 128), V(x, X0 + 4 * 256, XM))
            mm(PS(BANK_Q, 0, 128), ut, ust, V(xq, P, P + 128), V(xs, P, P + 128))
            last = PS(BANK_Q, 32, 128)
        if not home:
            for lo, hi in (((128, P), (0, 128)) if t in SPLIT else ((0, P),)):
                if lo == 0:
                    quant(V(xq, 0, 128), V(xs, 0, 128), V(x, X0, X0 + 512))
                send([(T[lq][:, lo:hi].bitcast(dt.uint8), T[xq][:, lo:hi].bitcast(dt.uint8)), (T[ls][:, lo:hi], T[xs][:, lo:hi])], "aq%d" % t,
                     [V(xq, lo, hi), V(xs, lo, hi)], [V(lq, lo, hi), V(ls, lo, hi)], 3500)
        tt(fw(L0, 192), PS(BANK_S, 0, 192), V("eqb", 0, 192), A.is_lt)
        tt(fw(T0), (fw(W0), pa[0]), fw(L0), A.mult)
        tt(V("t2", 0, 96), (fw(0, B0), V("lb", 0, 6)), fw(L0 + B), A.not_equal)
        tt(fw(B0), (fw(W0, 192), pa[1]), V("t2", 0, 96), A.mult)
        tt(fw(T1), (fw(W1 - B, 192), pa[1]), fw(L0 + B), A.mult)
        tt(fw(L0 + 192), last, V("eqb", 192, 288), A.is_lt)
        tt(V("t2", 96, 192), (fw(0, A0), V("lb", 6, 12)), fw(L0 + 192), A.not_equal)
        tt(V("t2", 192, 288), (fw(Z1, T2 - Z1), V("lb", 12, 18)), fw(L0 + 192), A.not_equal)
        tt(fw(A0), (fw(W0, P), pa[2]), V("t2", 96, 192), A.mult)
        tt(fw(A1), (fw(W1 - B, P), pa[2]), V("t2", 192, 288), A.mult)
        tt(fw(T2), (fw(W1 - B, 192), V("lt2")), fw(L0 + 192), A.mult)
        j = 0
        for k, run in enumerate((fw(A0), fw(A1), fw(T2), fw(T0, 192), fw(T1))):
            for w in range(2):
                n = size(run)
                if t in SIDES:
                    act(V("junk", j, j + n), run, AF.Relu, scale=-2.0 if w else 2.0, acc=col("acc", 2 * k + w))
                else:
                    act(V("junk", j, j + n), run, AF.Abs if w else AF.Identity, acc=col("acc", 5 * w + k))
                    red(col("acc", 5 * w + k), run, sizes=bool(w))
                    either()
                j += n
        if t in SIDES:
            cp(V("acci"), V("acc"))
        else:
            tt(V("acci", 0, 10, 2), V("acc", 5, 10), V("acc", 0, 5), A.add)
            tt(V("acci", 1, 10, 2), V("acc", 5, 10), V("acc", 0, 5), A.subtract)
        ts(V("un", 0, 30, 3), V("acci"), 255, None, A.bitwise_and)
        ts(V("un", 1, 30, 3), V("acci"), 8, 255, A.logical_shift_right, A.bitwise_and)
        ts(V("un", 2, 30, 3), V("acci"), 16, None, A.logical_shift_right)
        tt(V("un", 0, 12), V("un", 0, 12), V("un", 18, 30), A.add)
        if t in COUNTS:
            nn = "n%d" % t
            cp(V(nn), V("un", 0, 18))
            send([(T[lh][:], T[nn][:])], "ah%d" % t, [V(nn)], [V(lh)], 2200)
            n16, came = V(lh), ("ah%d" % t, 1)
        else:
            cp(V("n16"), V("un", 0, 18))
            n16, came = V("n16"), None
        quant(V("fq"), V("fs"), fw(B0, 576))
        mm(PS(BANK_S, 0, 144), V("cq"), V("cs"), V("fq"), V("fs"))
        tt(V("pr", 0, 144), PS(BANK_S, 0, 144), SQ(0, 144), A.mult)
        tt(V("pr", 144, 216), V("bs"), PS(BANK_S, 72, 144), A.subtract)
        tt(V("pr", 24, 48), V("pr", 24, 48), V("pr", 48, 72), A.max)
        ts(V("doff", 72, 144), V("pr", 144, 216), DROP, R12, A.mult, A.add)
        tt(V("pr", 96, 144), V("pr", 96, 144), V("pr", 0, 48), A.max)
        ts(V("doff", 0, 72), V("pr", 72, 144), 0.25 / UNIT, R12, A.mult, A.add)
        line(V("nr"), (V("tab"), n16), 2.0, -34.0)
        ops[-1]["arr"] = came
        if t in AFTER:
            act(V("junk", j, j + P), V("nr"), AF.Sign, scale=0.5, bias=TH2, acc=col("ga", 0))
        else:
            act(V("junk", j, j + P), (V("tab"), n16), AF.Sign, bias=TH, acc=col("ga", 0))
            ops[-1]["arr"] = came
        act(V("g32"), V("m32"), AF.Sign, bias=col("ga", 0))
        turn(V("g32t"), V("g32"))
        act(V("g32"), V("g32t"), AF.Identity, acc=col("ga", 1))
        red(col("ga", 1), V("g32t"))
        either()
        ts(V("ge"), V("nr"), col("ga", 1), 2.0, A.is_ge, A.mult)
        if t in GT_A:
            act(V("junk", j + P, j + P + 32), V("g32t"), AF.Identity, bias=1.0 / 32, acc=col("ga", 2))
            act(V("gt"), V("nr"), AF.Sign, scale=-1.0, bias=col("ga", 2))
            scan(V("cap", 1, 289, -1), V("gt", 0, P, -1), V("one"), 0.0, A.add, A.subtract)
        else:
            ts(V("gt"), V("nr"), col("ga", 1), -2.0, A.is_gt, A.mult)
            scan(V("cap", 1, 289, -1), V("gt", 0, P, -1), V("gt", 0, P, -1), 0.0, A.add, A.min)
        scan(V("cum"), V("ge"), V("cap", 2, 290), -192.0, A.add, A.min)
        na = 6 - LIST_V[t]
        runs = ((0, 3), (3, 6)) if na == 6 and t in LEANING else ((0, na), (na, 6)) if na < 6 else ((0, 6),)
        for c0, c1 in runs:
            more = max(range(-80, 81, 16), key=lambda m: min([min(16 * c - m, 80 - 16 * c) >= 0 and min(16 * c, 80 - 16 * c + m) >= 0 for c in range(c0, c1)])
                       * (1 + sum([2 * min(16 * c, 80 - 16 * c + m) - m for c in range(c0, c1)])))
            cut = {c: min(16 * c, 80 - 16 * c + more) for c in range(c0, c1)}
            for c in range(c0, c1):
                jk, cum = V("jw", P * c + 2 * cut[c] - more, P * c + P), V("cum", cut[c], P - cut[c] + more)
                if c < na:
                    act(jk, cum, AF.Sign, scale=-1.0, bias=col("sb", c), acc=col("wl", c))
                else:
                    ts(jk, cum, col("sb", c), -0.5, A.is_lt, A.add)
            if c0 < na:
                ts(V("wl16", c0, c1), V("wl", c0, c1), 0.5, 144.0 + more / 2, A.mult, A.add)
            else:
                for c in range(c0, c1):
                    lo = 2 * cut[c] - more
                    scan(V("jx", P * c + lo, P * c + P), V("one", lo), V("jw", P * c + lo, P * c + P))
                ts(V("wl16", c0, c1), V("jx", P * c0 + P - 1, P * c1, P), 144.0 + more / 2, None, A.add)
        tt(V("kk"), (V("nr"), V("wl16")), V("jq"), A.subtract)
        move(V("wr"), (V("tab"), V("wl16")))
        scan(V("ks"), SEL16, V("kk"), op1=A.max)
        na = 6 - PLACE_V[t]
        for c in range(6):
            jk = V("jr", B * c, B * c + B)
            if c < na:
                act(jk, V("kk"), AF.Sign, scale=NK16, bias=col("ks", 16 * c + 15), acc=col("rk", c))
            else:
                ts(jk, V("kk"), K16, col("ks", 16 * c + 15), A.mult, A.is_gt)
        for c in range(na, 6):
            scan(V("js", B * c, B * c + B), V("one", 0, B), V("jr", B * c, B * c + B))
        if na < 6:
            cp(V("rk16", na, 6), V("js", B * na + B - 1, 6 * B, B))
        if na:
            ts(V("rk16", 0, na), V("rk", 0, na), -0.5, 47.5, A.mult, A.add)
        scatter(V("hr"), V("rk16"), V("wr"))
        scan(V("hs"), V("sel4", 0, 96), V("hr"), op1=A.max)
        ts(V(hh), V("hs", 3, 96, 4), F4H, R12 if home else RM4, A.mult, A.add)
        if home:
            gq, gs = "gq%d" % t, "gs%d" % t
            move(V("fb", 0, 4 * E), (win, V(hh)))
            quant(V(gq), V(gs), V("fb"))
            send([(T[lq][:, 0:128].bitcast(dt.uint8), T[gq][:].bitcast(dt.uint8)), (T[ls][:, 0:128], T[gs][:])], "aq%d" % t,
                 [V(gq), V(gs)], [V(lq), V(ls)], 2500)
        elif t not in COUNTS:
            send([(T[lh][:], T[hh][:])], "ah%d" % t, [V(hh)], [V(lh)], 2200)
        n = 12 if t in HALVES else 24
        for c in range(0, 72, n):
            lo, hi = 16 * c, 16 * (c + n)
            move(V("xa", lo, hi), (win, V("aoff", c, c + n)))
            if PICK0 and c < 24:
                tt(V(x, XM + lo, XM + hi), (win, V("boff", c, c + n)), V("xa", lo, hi), A.max)
                move(V(x, lo, hi), V("xa", lo, hi), 2.0)
                if c + n == 24:
                    move(V("mt", 0, hi), (V(x), V("doff", 72, 96)))
                continue
            tt(V("mx", lo, hi), (V(x, XB, XM), V("doff", 72 + c, 72 + c + n)), V("xa", lo, hi), A.max)
            if (t, c // 24) in M_DMA:
                move(V("mt", lo, hi), (win, V("doff", c, c + n)))
                add("g", 700, [V("mx", lo, hi), V("mt", lo, hi), V("vb")], [V("mt", lo, hi)],
                    lambda o=V("mt", lo, hi), r=V("mx", lo, hi): g.dma_start(ap(o), ap(r), accum_op=A.add), kind="d", lat=2800)
            else:
                tt(V("mt", lo, hi), (win, V("doff", c, c + n)), V("mx", lo, hi), A.add)
        for h, (c0, n, skip) in enumerate(((0, P, 0),) if t in WHOLE_M else ((0, 192, 0), (160, 128, 32))):
            lo, hi = 4 * (c0 + skip), 4 * (c0 + n)
            mq, ms = V("mq8", 192 * h, 192 * h + n), V("ms8", 192 * h, 192 * h + n)
            quant(mq, ms, V("mt", 4 * c0, hi))
            for b in range(4):
                mm(PS(BANK_Z + b, 0, n), V("wq", 128 * b, 128 * b + 128), V("wp", 128 * b, 128 * b + 128), mq, ms)
                relu(V("rr", lo + b, hi, 4), PS(BANK_Z + b, skip, n), 0.015625)
            for l2 in range(lo, hi, 384):
                old, new = V(x, X0 + 4 * E + l2, X0 + 4 * E + l2 + 384), V(xn, X0 + 4 * E + l2, X0 + 4 * E + l2 + 384)
                if (t, l2 // 384) in BY_DMA:
                    dma("s", ap(new), ap(old), [old], [new], 2200)
                    add("g", 700, [V("rr", l2, l2 + 384), new, V("vb")], [new],
                        lambda new=new, r=V("rr", l2, l2 + 384): g.dma_start(ap(new), ap(r), accum_op=A.add), kind="d", lat=2800)
                elif (t, l2 // 384) in BY_ROW:
                    for b in range(4):
                        tt(new[0:1] + (new[1] + b, new[2], 4), V("rr", l2 + b, l2 + 384, 4), old[0:1] + (old[1] + b, old[2], 4), A.add)
                else:
                    tt(new, V("rr", l2, l2 + 384), old, A.add)
        if t == R - 1:
            line(V("dv"), V("pr", 72, 168), 0.0625 / UNIT, -1.0)
            turn(V("dw"), V("dv"))
            move(V("dr"), V("dw", 0, 96, 4))
            for gr in range(8):
                for k, n in enumerate((32, 32, 8)):
                    c0 = 8 * k + 4 * (gr % 2)
                    dma("s", T.od[gr, 128 * k:128 * k + 4 * n], T.dr[32 * (gr // 2):32 * (gr // 2) + n, c0:c0 + 4], [V("dr")], [], 2000)
                    ops[-1]["sem"] = "od"
            quant(V("oq", 128, 384), V("op", 128, 384), V(xn, X0 + 512, XM))
            dma("s", T.oc[:, 512:], T.oq[:, 128:384].bitcast(dt.uint8), [V("oq", 128, 384)], [], 2400)
            mm(PS(BANK_S, 0, 256), V("vq"), V("vs"), V("oq", 128, 384), V("op", 128, 384))
            move(V("yo", 128, 384), PS(BANK_S, 0, 256))
            dma("s", T.y[:, 128:], T.yo[:, 128:], [V("yo", 128, 384)], [], 2400)
        for b in range(4):
            bank, n = BANK_D + b % 2, 128 if home else P
            mm(PS(bank, 0, n), V("eqq", 128 * b, 128 * b + 128), V("es", 128 * b, 128 * b + 128), V(lq, 0, n), V(ls, 0, n), arr=("aq%d" % t, sent.count("aq%d" % t) * 2))
            if home:
                tt(V(xn, X0 + b, X0 + 4 * E, 4), PS(bank, 0, E), V(x, X0 + b, X0 + 4 * E, 4), A.max)
            else:
                move(V("dx", b, 4 * P, 4), PS(bank, 0, P))
        if t in COUNTS:
            tt(V(xn, X0, X0 + 4 * E), (V("dx"), V(hh)), V(x, X0, X0 + 4 * E), A.max)
        elif not home:
            tt(V(xn, X0, X0 + 4 * E), (V("dx"), V(lh)), V(x, X0, X0 + 4 * E), A.max, arr=("ah%d" % t, 1))
    xn = "x%d" % R
    quant(V("oq", 0, 128), V("op", 0, 128), V(xn, X0, X0 + 512))
    mm(PS(BANK_Q, 0, 128), V("vq"), V("vs"), V("oq", 0, 128), V("op", 0, 128))
    dma("s", T.oc[:, 0:512], T.oq[:, 0:128].bitcast(dt.uint8), [V("oq", 0, 128)], [], 2000)
    for k in range(4):
        dma("sa"[k % 2], T.osc[4 * k:4 * k + 4, :], T.op[32 * k:32 * k + 4, :], [V("op")], [], 1900)
    move(V("yo", 0, 128), PS(BANK_Q, 0, 128))
    dma("s", T.y[:, 0:128], T.yo[:, 0:128], [V("yo", 0, 128)], [], 2000)
    return ops


def link(ops):
    seen = {}
    for k, o in enumerate(ops):
        deps = set()
        for v in o["rd"]:
            for j, w, wr in seen.get(v[0], []):
                if meet(v, w) and (wr or (v[0] == "ps" and len(o["ways"]) + len(ops[j]["ways"]) > 2)):
                    deps.add(j)
        for v in o["wr"]:
            for j, w, wr in seen.get(v[0], []):
                if meet(v, w):
                    deps.add(j)
        deps.discard(k)
        o["deps"] = sorted(deps)
        far = 0
        for j in deps:
            far |= ops[j]["behind"]
        o["near"], o["next"], o["all"] = [j for j in o["deps"] if not far >> j & 1], [], tuple(range(len(o["ways"])))
        o["behind"] = far | sum([1 << j for j in deps if not far >> j & 1])
        for j in o["near"]:
            ops[j]["next"].append(k)
        for v in o["rd"]:
            seen.setdefault(v[0], []).append((k, v, False))
        for v in o["wr"]:
            seen.setdefault(v[0], []).append((k, v, True))


def deal(ops, key, way, back, lean):
    pre = "next" if back else "near"
    n = len(ops)
    at, fin, w = [0.0] * n, [0.0] * n, list(way)
    st, en = {q: [] for q in "vatgs"}, {q: [] for q in "vatgs"}
    for k in sorted(range(n), key=lambda k: key[k]):
        o = ops[k]
        can = 0.0
        for j in o[pre]:
            if fin[j] > can:
                can = fin[j]
        if back:
            can += o["lat"]
        best = None
        for i in ((w[k],) if back else o["all"]):
            q, c, f = o["ways"][i]
            s, e = st[q], en[q]
            m, t = len(s), can
            while m and e[m - 1] > can:
                m -= 1
            while m < len(s) and s[m] < t + c:
                t = e[m]
                m += 1
            end = t + c + (lean[k] if q == "v" else 0.0)
            if best is None or end < best[0]:
                best = (end, i, q, t, c, m)
        end, w[k], q, t, c, m = best
        st[q].insert(m, t)
        en[q].insert(m, t + c)
        at[k] = t
        fin[k] = t + c + HOP + (0.0 if back else o["lat"])
    return max(fin), at, w


def polish(ops, sets, start, rng):
    n = len(ops)
    near, nex, behind = [o["near"] for o in ops], [o["next"] for o in ops], [o["behind"] for o in ops]
    tails = [[rough[3] + o["lat"] for o in each] for rough, each in zip(ROUGH, sets)]
    costs = [[[("vatgs".index(w[0]), w[1]) for w in o["ways"]] for o in each] for each in sets]
    ways = costs[0]
    seq, way = sorted(range(n), key=lambda k: (start[1][k], k)), list(start[2])

    def run(seq, way, lo, hi, old):
        new, before, after = [], [None] * 5, [None] * 5
        for k in seq[:lo]:
            before[ways[k][way[k]][0]] = ~k
        for k in seq[:hi - 1:-1]:
            after[ways[k][way[k]][0]] = k
        for cost, tail, (fin, by, left) in zip(costs, tails, old):
            fin, by, left, last = fin[:], by[:], left[:], before[:]
            free = [0.0 if b is None else fin[~b] - tail[~b] for b in before]
            for k in seq[lo:]:
                q, c = cost[k][way[k]]
                t, b = free[q], last[q]
                for j in near[k]:
                    if fin[j] > t:
                        t, b = fin[j], j
                t += c
                by[k] = b
                free[q] = t
                last[q] = ~k
                fin[k] = t + tail[k]
            free = [0.0 if a is None else left[a] for a in after]
            for k in seq[hi - 1::-1]:
                q, c = cost[k][way[k]]
                t = 0.0
                for j in nex[k]:
                    if left[j] > t:
                        t = left[j]
                t += tail[k]
                if free[q] > t:
                    t = free[q]
                left[k] = free[q] = t + c
            new.append((fin, by, left))
        return new, [max(e[0]) for e in new]

    def least(seg, way, lo, hi, used):
        before, after, out = {}, {}, 0.0
        for q in used:
            i = lo - 1
            while i >= 0 and qs[i] != q:
                i -= 1
            before[q] = seq[i] if i >= 0 else None
            i = hi
            while i < n and qs[i] != q:
                i += 1
            after[q] = seq[i] if i < n else None
        for cost, tail, (fin, by, left), s in zip(costs, tails, state, share):
            free = {q: 0.0 if b is None else fin[b] - tail[b] for q, b in before.items()}
            mine, end = {}, 0.0
            for k in seg:
                q, c = cost[k][way[k]]
                t = free[q]
                for j in near[k]:
                    f = mine.get(j) or fin[j]
                    if f > t:
                        t = f
                free[q] = t = t + c
                mine[k] = t = t + tail[k]
                if t > end:
                    end = t
                for j in nex[k]:
                    if pos[j] >= hi and t + left[j] > end:
                        end = t + left[j]
            for q, a in after.items():
                if a is not None and free[q] + left[a] > end:
                    end = free[q] + left[a]
            out += end * s
        return out

    state, ends = run(seq, way, 0, n, [([0.0] * n, [None] * n, [0.0] * n) for each in sets])
    pos, qs = [0] * n, [0] * n
    share = [ends[0] / e / len(ends) for e in ends]
    now = sum([e * s for e, s in zip(ends, share)])
    best, held = (now, seq, way, state, ends), None
    for it in range(SWAPS):
        if held is None:
            held, two = [], []
            for (fin, by, left), end in zip(state, ends):
                k = fin.index(end)
                while by[k] is not None:
                    if len(ways[k]) > 1:
                        two.append(k)
                    if by[k] < 0:
                        held.append((k, ~by[k]))
                    k = ~by[k] if by[k] < 0 else by[k]
            for i, k in enumerate(seq):
                pos[k], qs[i] = i, ways[k][way[k]][0]
        if it % 1000 == 0:
            draws = rng.random((1000, 5)).tolist()
        r = draws[it % 1000]
        w2 = way
        if r[0] < 0.2 and two:
            k = two[int(r[1] * len(two))]
            w2 = way[:]
            w2[k] = (w2[k] + 1 + int(r[2] * (len(ways[k]) - 1))) % len(ways[k])
            lo, hi, seg = pos[k], pos[k] + 1, [k]
            used = (qs[lo], ways[k][w2[k]][0])
        else:
            v, u = held[int(r[1] * len(held))]
            if behind[v] >> u & 1:
                continue
            if r[2] < 0.5:
                lo, hi = pos[u], min(n, pos[v] + 1 + int(25 * r[3] * r[3]))
                seg = seq[lo:hi]
                seg = [k for k in seg if k != u and not behind[k] >> u & 1] + [k for k in seg if k == u or behind[k] >> u & 1]
            else:
                lo, hi = max(0, pos[u] - int(25 * r[3] * r[3])), pos[v] + 1
                seg, bv = seq[lo:hi], behind[v] | 1 << v
                seg = [k for k in seg if bv >> k & 1] + [k for k in seg if not bv >> k & 1]
            used = sorted(set(qs[lo:hi]))
        most = now - WARM * (1.0 - it / SWAPS) * math.log(1.0 - r[4])
        if least(seg, w2, lo, hi, used) > most:
            continue
        s2 = seq[:lo] + seg + seq[hi:]
        st2, e2 = run(s2, w2, lo, hi, state)
        got = sum([e * s for e, s in zip(e2, share)])
        if got <= most:
            now, seq, way, state, ends, held = got, s2, w2, st2, e2, None
            if got < best[0]:
                best = (got, seq, way, state, ends)
    now, seq, way, state, ends = best
    return ends, [state[0][0][k] - tails[0][k] - ways[k][way[k]][1] for k in range(n)], way, seq


KEPT = {}


def order(sets):
    ops = sets[0]
    link(ops)
    n = len(ops)
    if "best" not in KEPT:
        rng = np.random.default_rng(SEED)
        key = [0.0] * n
        for k in range(n - 1, -1, -1):
            key[k] -= min([w[1] for w in ops[k]["ways"]]) + HOP + ops[k]["lat"]
            for j in ops[k]["deps"]:
                key[j] = min(key[j], key[k])
        lean = [LEAN] * n
        best = now = deal(ops, key, [0] * n, False, lean)
        for it in range(TRIES):
            r, a, le = rng.random(), int(rng.integers(n)), list(lean)
            shake = rng.normal(0.0, (30.0, 150.0, 500.0)[it % 3], n)
            if r < 0.3:
                d = float(rng.normal(0.0, 600.0))
                for k in range(a, min(n, a + int(rng.integers(1, 30)))):
                    le[k] += d
            if r > 0.6:
                shake[a:a + int(rng.integers(1, 25))] += float(rng.normal(0.0, 2000.0))
            shake = shake.tolist()
            key = [shake[k] - now[1][k] - ops[k]["ways"][now[2][k]][1] - ops[k]["lat"] for k in range(n)]
            for k in range(n - 1, -1, -1):
                for j in ops[k]["near"]:
                    if key[j] <= key[k]:
                        key[j] = key[k] + 0.01
            b = deal(ops, key, now[2], True, le)
            got = deal(ops, [-b[1][k] - ops[k]["ways"][b[2][k]][1] for k in range(n)], b[2], False, le)
            if got[0] <= now[0] + TEMP * (1.0 - it / TRIES) * float(rng.exponential()):
                now, lean = got, le
            if got[0] < best[0]:
                best = got
        KEPT["best"] = polish(ops, sets, best, rng)
    end, at, way, seq = KEPT["best"]
    for k, o in enumerate(ops):
        o["at"] = at[k]
        o["q"], o["cost"], o["fn"] = o["ways"][way[k]]
    return seq


def rank_program(g, core, T, topo):
    if T.rank_of(core) is None:
        return
    sets = [build(g, core, T, topo, rough) for rough in ROUGH]
    ops, seq = sets[0], order(sets)
    prev = T.cores[(T.rank_of(core) - 1) % len(T.cores)]
    nxt = T.cores[(T.rank_of(core) + 1) % len(T.cores)]
    eng = {"v": g.vector, "a": g.scalar, "t": g.tensor, "g": g, "s": g.sync}
    total, done = {"left": 0}, {}
    know = {q: {} for q in eng}
    for k in seq:
        o = ops[k]
        if o["fn"] is None:
            continue
        q, mine = o["q"], know[o["q"]]
        need = {}
        for j in o["deps"]:
            if ops[j]["kind"] == "r":
                continue
            s, val = ops[j]["tok"]
            if val > need.get(s, (0, 0))[0]:
                need[s] = (val, j)
        for s, (val, j) in sorted(need.items(), key=lambda e: -ops[e[1][1]]["at"]):
            if mine.get(s, 0) < val:
                for i in done.get(s, [])[val:]:
                    if ops[i]["at"] + ops[i]["cost"] + HOP + (0.0 if s == "s" + q else LONG) <= o["at"]:
                        val, j = ops[i]["tok"][1], i
                eng[q].wait_ge(T.sem[s], val)
                for s2, v2 in ops[j]["clock"].items():
                    mine[s2] = max(mine.get(s2, 0), v2)
        if o["arr"] is not None:
            s, val = o["arr"][0], o["arr"][1] * len(topo.engines(prev, core))
            total[s] = val
            if mine.get(s, 0) < val:
                eng[q].wait_ge(T.sem[s], val)
                mine[s] = val
        ins = o["fn"]()
        if o["kind"] == "r":
            total["left"] += o["calls"] * len(topo.engines(core, nxt))
            continue
        if o["kind"] == "d":
            s, inc = o.get("sem", "d%d" % len([1 for e in total if e[0] == "d"])), 16
        else:
            s, inc = "s" + q, 1
            done.setdefault(s, []).append(k)
        total[s] = total.get(s, 0) + inc
        ins.then_inc(T.sem[s], inc)
        o["tok"] = (s, total[s])
        o["clock"] = dict(mine)
        o["clock"][s] = total[s]
    for s, val in total.items():
        if know["g"].get(s, 0) < val:
            g.wait_ge(T.sem[s], val)
